import numpy as np
import ml_dtypes


def mxq(x, axis, fmt="e4m3"):
    dtype, down = {"e4m3": (ml_dtypes.float8_e4m3fn, 7), "e5m2": (ml_dtypes.float8_e5m2, 14)}[fmt]
    v = np.moveaxis(np.asarray(x, np.float32).astype(ml_dtypes.bfloat16).astype(np.float64), axis, -1)
    blocks = v.reshape(v.shape[:-1] + (-1, 32))
    amax = np.abs(blocks).max(-1, keepdims=True)
    byte = np.maximum(np.where(amax > 0, np.frexp(amax)[1] - 1 + 127, 0) - down, 1)
    scale = np.exp2(byte - 127.0)
    codes = (blocks / scale).astype(np.float32).astype(dtype).astype(np.float64)
    return np.moveaxis((codes * scale).reshape(v.shape), -1, axis)


WIDE = False


def mx_kscale(k):
    if not WIDE:
        return np.ones(k)
    levels = np.array([10, -10, 5, -5, 0])
    if k % 512:
        return np.exp2(np.random.permutation(np.resize(levels, k // 32))).repeat(32)
    a = np.empty((k // 512, 16))
    for p in range(k // 512):
        a[p, :8] = np.random.permutation(np.resize(levels, 8))
        for g in range(8):
            far = levels[np.abs(levels - a[p, g]) >= 10]
            a[p, g + 8] = far[np.random.randint(len(far))]
    return np.exp2(a.ravel()).repeat(32)


BF16 = ml_dtypes.bfloat16


def bf(x):
    return np.asarray(x, np.float32).astype(BF16)


def f64(x):
    return np.asarray(x).astype(np.float64)


E2M1 = np.array([0.0, 0.5, 1.0, 1.5, 2.0, 3.0, 4.0, 6.0, -0.0, -0.5, -1.0, -1.5, -2.0, -3.0, -4.0, -6.0])


def pack_weight(w, fmt):
    k, n = w.shape
    w = f64(bf(w)).reshape(k // 32, 32, n)
    amax = np.abs(w).max(1)
    if fmt == "e4m3":
        byte = np.frexp(amax)[1] - 1 + 127 - 7
    else:
        mant, ex = np.frexp(amax / 6.0)
        byte = np.where(mant > 0.5, ex, ex - 1) + 127
    byte = np.clip(np.where(amax > 0, byte, 1), 1, 254)
    scaled = (w * np.exp2(127.0 - byte)[:, None, :]).reshape(k, n).astype(np.float32)
    by_word = np.ascontiguousarray(scaled.reshape(k // 512, 128, 4, n).transpose(0, 1, 3, 2))
    if fmt == "e4m3":
        words = by_word.astype(ml_dtypes.float8_e4m3fn).view(np.uint8)
    else:
        c = by_word.astype(ml_dtypes.float4_e2m1fn).view(np.uint8) & 0xF
        words = c[..., 0::2] | (c[..., 1::2] << 4)
    return np.ascontiguousarray(words), np.ascontiguousarray(byte.astype(np.uint8).reshape(k // 512, 16, n))


def unpack_weight(words, scales, fmt):
    g, p, n, _ = words.shape
    if fmt == "e4m3":
        vals = np.ascontiguousarray(words).view(ml_dtypes.float8_e4m3fn).astype(np.float64)
    else:
        nib = np.empty((g, p, n, 4), np.uint8)
        nib[..., 0::2] = words & 0xF
        nib[..., 1::2] = words >> 4
        vals = E2M1[nib]
    vals = vals * np.repeat(np.exp2(scales.astype(np.float64) - 127.0), 8, axis=1)[..., None]
    return vals.transpose(0, 1, 3, 2).reshape(g * 512, n)
def pack4(w):
    words, scales = pack_weight(w, "e2m1")
    return words.reshape(words.shape[0], 128, -1), scales


def unpack4(words, scales):
    return unpack_weight(words.reshape(words.shape[0], 128, -1, 2), scales, "e2m1")


M, K, F, R = 1024, 2048, 1024, 2048


def setup_inputs():
    s, t = mx_kscale(K), mx_kscale(F)
    cells = np.random.standard_normal((K, M)) * s[:, None]
    inter = np.random.standard_normal((K, F)) / np.sqrt(K) / s[:, None] * t
    c_words, c_scales = pack4(cells)
    b_words, b_scales = pack4(inter)
    return {"c_words": c_words,
            "c_scales": c_scales,
            "b_words": b_words,
            "b_scales": b_scales,
            "activity": bf(1.0 + 0.5 * np.random.standard_normal((M, F))),
            "pairs": bf(1.5 * np.random.standard_normal((R, F)) / np.sqrt(F) / t),
            "pair_bias": bf(0.5 * np.random.standard_normal(R))}


def reference(c_words, c_scales, b_words, b_scales, activity, pairs, pair_bias):
    c = unpack4(c_words, c_scales)
    b = unpack4(b_words, b_scales)
    h = c.T @ b
    h = h * f64(activity)
    d = mxq(f64(pairs), 1, "e4m3")
    z = mxq(h, 1, "e4m3") @ d.T
    z = z + f64(pair_bias)
    return 1.0 / (1.0 + np.exp(-z))

@@ -1,0 +1,352 @@
+from contextlib import ExitStack
+
+import concourse.mybir as mybir
+from concourse.masks import make_identity
+
+M, K, F, R = 1024, 2048, 1024, 2048
+FLOPS = 2 * M * K * F + 2 * M * F * R
+
+F32 = mybir.dt.float32
+BF16 = mybir.dt.bfloat16
+I32 = mybir.dt.int32
+U32 = mybir.dt.uint32
+U8 = mybir.dt.uint8
+FP4X4 = mybir.dt.float4_e2m1fn_x4
+FP8X4 = mybir.dt.float8_e4m3fn_x4
+ACT = mybir.ActivationFunctionType
+ALU = mybir.AluOpType
+
+P = 128
+KG = K // 512
+FG = F // 512
+MT = M // P
+RT = R // P
+RC = R // 512
+WARM_UP = 2
+
+
+def tile_drug_synergy_bilinear_s4_kernel(
+    tc, c_words, c_scales, b_words, b_scales, activity, pairs, pair_bias, out
+):
+    nc = tc.nc
+    with ExitStack() as ctx:
+        keep = ctx.enter_context(tc.tile_pool(name="keep", bufs=1))
+        work = ctx.enter_context(tc.tile_pool(name="work", bufs=4))
+        psum = ctx.enter_context(tc.psum_pool(name="psum", bufs=8))
+        ctx.enter_context(tc.manual_schedule())
+
+        def fixed(name, shape, dtype):
+            return keep.tile(shape, dtype, name=name, tag=name, align_bytes=64)
+
+        def new_bank():
+            return psum.tile([P, 512], F32, name="bank", tag="bank")
+
+        c_plane = [fixed("c_plane%d" % i, [P, KG, 512], U8) for i in range(2)]
+        b_plane = [fixed("b_plane%d" % i, [P, KG, 512], U8) for i in range(2)]
+        c_code = [[fixed("c_code%d%d" % (i, h), [P, 2, 1024], U8) for h in range(2)] for i in range(2)]
+        b_code = [[fixed("b_code%d%d" % (i, h), [P, 2, 1024], U8) for h in range(2)] for i in range(2)]
+        act = [fixed("act%d" % j, [P, 2, F], BF16) for j in range(MT // 2)]
+        raw = [fixed("raw%d" % j, [P, 2, F], BF16) for j in range(RT // 2)]
+        d_code = fixed("d_code", [P, RC, FG, 512], U32)
+        d_plane = fixed("d_plane", [P, RC, FG, 512], U8)
+        ident = fixed("ident", [P, P], F32)
+        bias_rows = fixed("bias_rows", [P, 256], BF16)
+        bias_cols = fixed("bias_cols", [P, 8], F32)
+        bias = fixed("bias", [P, R], BF16)
+        warm = fixed("warm", [P, 1], F32)
+
+        def clear(engine, plane):
+            engine.memset(plane[:].rearrange("p g n -> p (g n)").bitcast(I32), 0)
+
+        nc.vector.memset(bias_rows[:].bitcast(I32), 0)
+        clear(nc.vector, c_plane[0])
+        clear(nc.vector, b_plane[0])
+        nc.vector.memset(warm[:], 0.0)
+        pairs_v = pairs.rearrange("(n i p) k -> n p i k", i=2, p=P)
+        act_v = activity.rearrange("(n i p) f -> n p i f", i=2, p=P)
+        c_scales_v = c_scales.bitcast(I32).rearrange("g r n -> r g n")
+        b_scales_v = b_scales.bitcast(I32).rearrange("g r n -> r g n")
+        c_words_v = c_words.bitcast(I32).rearrange("(h g) p n -> h p g n", g=2)
+        b_words_v = b_words.bitcast(I32).rearrange("(h g) p n -> h p g n", g=2)
+
+        def load_pairs(j, queue=nc.sync):
+            queue.dma_start(out=raw[j][:], in_=pairs_v[j])
+
+        def load_act(j):
+            nc.sync.dma_start(out=act[j][:], in_=act_v[j])
+
+        def load_codes(queue, codes, source, i, h):
+            queue.dma_start(out=codes[i][h][:].bitcast(I32), in_=source[h, :, :, 256 * i : 256 * (i + 1)])
+
+        def load_scales(queue, plane, source, i):
+            for q in range(4):
+                queue.dma_start(
+                    out=plane[i][32 * q : 32 * q + 4].bitcast(I32),
+                    in_=source[4 * q : 4 * q + 4, :, 128 * i : 128 * (i + 1)],
+                )
+
+        make_identity(nc, ident[:])
+        clear(nc.gpsimd, c_plane[1])
+        clear(nc.gpsimd, b_plane[1])
+        load_codes(nc.sync, c_code, c_words_v, 0, 0)
+        nc.scalar.dma_start(out=bias_rows[0:8, :], in_=pair_bias.rearrange("(c n) -> c n", n=256))
+        load_scales(nc.sync, c_plane, c_scales_v, 0)
+        load_codes(nc.sync, b_code, b_words_v, 0, 0)
+        load_scales(nc.sync, b_plane, b_scales_v, 0)
+        load_pairs(0)
+        load_codes(nc.sync, c_code, c_words_v, 0, 1)
+        load_codes(nc.sync, b_code, b_words_v, 0, 1)
+        load_scales(nc.sync, b_plane, b_scales_v, 1)
+        load_codes(nc.sync, b_code, b_words_v, 1, 0)
+        load_codes(nc.sync, b_code, b_words_v, 1, 1)
+        load_act(0)
+        load_act(1)
+        load_pairs(1)
+        load_pairs(2)
+        nc.scalar.activation(out=warm[:], in_=warm[:], func=ACT.Sigmoid)
+
+        def bias_step():
+            bank = new_bank()
+            nc.tensor.transpose(bank[:, 0:P], bias_rows[:].bitcast(F32), ident[:])
+            nc.scalar.copy(out=bias_cols[:], in_=bank[:, 0:8])
+            for half in range(2):
+                bank = new_bank()
+                for i in range(4):
+                    c = 4 * half + i
+                    nc.tensor.transpose(
+                        bank[:, i * P : (i + 1) * P], bias_cols[:, c : c + 1].to_broadcast([P, P]), ident[:]
+                    )
+                nc.scalar.copy(out=bias[:, 1024 * half : 1024 * (half + 1)].bitcast(F32), in_=bank[:])
+
+        def warm_up():
+            bank = new_bank()
+            for i in range(WARM_UP):
+                nc.tensor.matmul_mx(
+                    out=bank[:],
+                    lhsT=c_code[0][0][:, 0, 0:256].bitcast(FP4X4),
+                    lhsT_scale=c_plane[1][:, 1, 0:P],
+                    rhs=b_code[0][0][:, 0, :].bitcast(FP4X4),
+                    rhs_scale=c_plane[1][:, 0, :],
+                    start=(i == 0),
+                    stop=(i == WARM_UP - 1),
+                )
+
+        perm = {}
+        grouped = {}
+
+        def pairs_permute(j, copy=nc.vector.tensor_copy):
+            t = work.tile([P, 2 * F // 2], F32, name="perm", tag="perm", bufs=4, align_bytes=64)
+            perm[j] = t
+            copy(
+                out=t[:].rearrange("p (u n x) -> p u n x", u=2, x=8),
+                in_=raw[j][:].rearrange("p i k -> p (i k)").bitcast(F32).rearrange("p (n u x) -> p u n x", u=2, x=8),
+            )
+
+        def pairs_turn(i):
+            j, rc = i // 2, i // 4
+            if i % 4 == 0:
+                grouped[rc] = work.tile([P, FG, 512, 4], BF16, name="grouped", tag="grouped", bufs=2, align_bytes=64)
+            bank = new_bank()
+            words = perm[j][:]
+            for g in range(FG):
+                for u in range(2):
+                    start = 512 * u + 256 * (i % 2) + 128 * g
+                    nc.tensor.transpose(
+                        bank[:, (2 * g + u) * P : (2 * g + u + 1) * P], words[:, start : start + P], ident[:]
+                    )
+            r0 = 128 * (i % 4)
+            nc.scalar.copy(
+                out=grouped[rc][:].rearrange("p g r t -> p g (r t)").bitcast(F32)[:, :, 2 * r0 : 2 * r0 + 256].rearrange("p g (r u) -> p g r u", u=2),
+                in_=bank[:].rearrange("p (g u r) -> p g r u", g=FG, u=2),
+            )
+
+        def pairs_quantize(rc):
+            nc.vector.quantize_mx(
+                out=d_code[:, rc].rearrange("p g r -> p (g r)").bitcast(FP8X4),
+                scales=d_plane[:, rc].rearrange("p g r -> p (g r)"),
+                in_=grouped[rc][:].rearrange("p g r t -> p (g r t)"),
+            )
+
+        def first_pass(bank, m, f, g):
+            h, s = g // 2, g % 2
+            c_cols = slice(P * (m % 4), P * (m % 4 + 1))
+            nc.tensor.matmul_mx(
+                out=bank[:],
+                lhsT=c_code[m // 4][h][:, s, 256 * (m % 4) : 256 * (m % 4 + 1)].bitcast(FP4X4),
+                lhsT_scale=c_plane[m // 4][:, g, c_cols],
+                rhs=b_code[f][h][:, s, :].bitcast(FP4X4),
+                rhs_scale=b_plane[f][:, g, :],
+                start=(g == 0),
+                stop=(g == KG - 1),
+            )
+
+        gated = {}
+        h_code = {}
+        h_plane = {}
+        h_turned = {}
+
+        def gate(bank, m, f):
+            if f == 0:
+                gated[m] = work.tile([P, F], BF16, name="gated", tag="gated", bufs=6, align_bytes=64)
+            nc.vector.tensor_tensor(
+                out=gated[m][:].rearrange("p (u g n) -> p u g n", u=2, g=FG)[:, :, f, :].rearrange("p u (b x) -> p u b x", x=16),
+                in0=bank[:].rearrange("p (b u x) -> p u b x", u=2, x=16),
+                in1=act[m // 2][:, m % 2, 512 * f : 512 * (f + 1)].rearrange("p (b u x) -> p u b x", u=2, x=16),
+                op=ALU.mult,
+            )
+
+        def first_half(m, f):
+            bank = new_bank()
+            for g in range(KG):
+                first_pass(bank, m, f, g)
+            gate(bank, m, f)
+
+        four = []
+
+        def first_four(h):
+            if h == 0:
+                four.extend([new_bank() for m in range(4)])
+            for m in range(4):
+                for g in range(2 * h, 2 * h + 2):
+                    first_pass(four[m], m, 0, g)
+            if h == 1:
+                for m in range(4):
+                    gate(four[m], m, 0)
+
+        def h_turn(m):
+            bank = new_bank()
+            words = gated[m][:].bitcast(F32)
+            for g in range(FG):
+                for u in range(2):
+                    start = 256 * u + 128 * g
+                    nc.tensor.transpose(
+                        bank[:, (2 * g + u) * P : (2 * g + u + 1) * P], words[:, start : start + P], ident[:]
+                    )
+            h_turned[m] = work.tile([P, 4 * FG * P], BF16, name="h_turned", tag="h_turned", bufs=4, align_bytes=64)
+            nc.scalar.copy(
+                out=h_turned[m][:].bitcast(F32).rearrange("p (g r u) -> p g r u", g=FG, u=2),
+                in_=bank[:].rearrange("p (g u r) -> p g r u", g=FG, u=2),
+            )
+
+        def h_quantize(m):
+            h_code[m] = work.tile([P, FG * P], U32, name="h_code", tag="h_code", bufs=6, align_bytes=64)
+            h_plane[m] = work.tile([P, FG * P], U8, name="h_plane", tag="h_plane", bufs=6, align_bytes=64)
+            nc.vector.quantize_mx(out=h_code[m][:].bitcast(FP8X4), scales=h_plane[m][:], in_=h_turned[m][:])
+
+        def second(m, half, pieces=((0, 1024),)):
+            z = work.tile([P, 1024], F32, name="z", tag="z", bufs=8, align_bytes=64)
+            for i in range(2):
+                bank = new_bank()
+                rc = 2 * half + i
+                for g in range(FG):
+                    nc.tensor.matmul_mx(
+                        out=bank[:],
+                        lhsT=h_code[m][:, P * g : P * (g + 1)].bitcast(FP8X4),
+                        lhsT_scale=h_plane[m][:, P * g : P * (g + 1)],
+                        rhs=d_code[:, rc, g].bitcast(FP8X4),
+                        rhs_scale=d_plane[:, rc, g],
+                        start=(g == 0),
+                        stop=(g == FG - 1),
+                    )
+                for first_col, end_col in pieces:
+                    lo, hi = max(first_col, 512 * i), min(end_col, 512 * (i + 1))
+                    if lo < hi:
+                        nc.vector.tensor_tensor(
+                            out=z[:, lo:hi],
+                            in0=bank[:, lo - 512 * i : hi - 512 * i],
+                            in1=bias[:, 1024 * half + lo : 1024 * half + hi],
+                            op=ALU.add,
+                        )
+                    if lo < hi and hi == end_col:
+                        piece = z[:, first_col:end_col]
+                        nc.scalar.activation(out=piece, in_=piece, func=ACT.Sigmoid)
+                        nc.sync.dma_start(
+                            out=out[P * m : P * (m + 1), 1024 * half + first_col : 1024 * half + end_col], in_=piece
+                        )
+
+        bias_step()
+        warm_up()
+        load_scales(nc.sync, c_plane, c_scales_v, 1)
+        load_codes(nc.sync, c_code, c_words_v, 1, 0)
+        load_codes(nc.sync, c_code, c_words_v, 1, 1)
+        load_pairs(3)
+        load_pairs(4)
+        load_act(2)
+        load_pairs(5)
+        load_pairs(6)
+        load_pairs(7)
+        load_act(3)
+        pairs_permute(0, nc.scalar.copy)
+        first_four(0)
+        first_four(1)
+        first_half(0, 1)
+        pairs_turn(0)
+        pairs_turn(1)
+        first_half(1, 1)
+        first_half(2, 1)
+        pairs_permute(1, nc.scalar.copy)
+        pairs_permute(2)
+        h_turn(0)
+        pairs_turn(2)
+        pairs_turn(3)
+        h_quantize(0)
+        pairs_permute(3)
+        h_turn(1)
+        first_half(3, 1)
+        pairs_turn(4)
+        pairs_turn(5)
+        h_quantize(1)
+        h_turn(2)
+        pairs_permute(4)
+        pairs_quantize(0)
+        h_quantize(2)
+        h_turn(3)
+        pairs_permute(5)
+        h_quantize(3)
+        first_half(4, 0)
+        first_half(4, 1)
+        pairs_turn(6)
+        pairs_turn(7)
+        pairs_permute(6, nc.scalar.copy)
+        pairs_permute(7, nc.scalar.copy)
+        pairs_quantize(1)
+        first_half(5, 0)
+        first_half(5, 1)
+        h_turn(4)
+        h_quantize(4)
+        pairs_turn(8)
+        pairs_turn(9)
+        pairs_turn(10)
+        pairs_turn(11)
+        second(0, 0)
+        second(1, 0)
+        pairs_turn(12)
+        pairs_turn(13)
+        pairs_quantize(2)
+        pairs_turn(14)
+        pairs_turn(15)
+        second(2, 0)
+        first_half(6, 0)
+        first_half(6, 1)
+        second(3, 0)
+        pairs_quantize(3)
+        h_turn(5)
+        h_turn(6)
+        second(4, 0)
+        second(0, 1)
+        second(1, 1)
+        first_half(7, 0)
+        first_half(7, 1)
+        second(2, 1)
+        h_quantize(5)
+        h_turn(7)
+        second(3, 1)
+        second(5, 0)
+        second(4, 1, ((0, 512), (512, 1024)))
+        h_quantize(6)
+        second(5, 1, ((0, 512), (512, 1024)))
+        second(6, 0, ((0, 512), (512, 1024)))
+        h_quantize(7)
+        second(6, 1, ((0, 512), (512, 1024)))
+        second(7, 0, ((0, 512), (512, 1024)))
+        second(7, 1, ((0, 512), (512, 768), (768, 1024)))

@@ -22,7 +22,9 @@ FG = F // 512
 MT = M // P
 RT = R // P
 RC = R // 512
-WARM_UP = 2
+PERM_BUFS = 8
+Z_BUFS = 8
+PIECES = (((0, 1), (1, 4)), ((0, 4),))
 
 
 def tile_drug_synergy_bilinear_s4_kernel(
@@ -43,138 +45,101 @@ def tile_drug_synergy_bilinear_s4_kernel(
 
         c_plane = [fixed("c_plane%d" % i, [P, KG, 512], U8) for i in range(2)]
         b_plane = [fixed("b_plane%d" % i, [P, KG, 512], U8) for i in range(2)]
-        c_code = [[fixed("c_code%d%d" % (i, h), [P, 2, 1024], U8) for h in range(2)] for i in range(2)]
-        b_code = [[fixed("b_code%d%d" % (i, h), [P, 2, 1024], U8) for h in range(2)] for i in range(2)]
+        c_code = {(i, lo): fixed("c_code%d%d" % (i, lo), [P, hi - lo, 1024], U8) for i in range(2) for lo, hi in PIECES[i]}
+        b_code = {(i, lo): fixed("b_code%d%d" % (i, lo), [P, hi - lo, 1024], U8) for i in range(2) for lo, hi in PIECES[i]}
         act = [fixed("act%d" % j, [P, 2, F], BF16) for j in range(MT // 2)]
         raw = [fixed("raw%d" % j, [P, 2, F], BF16) for j in range(RT // 2)]
-        d_code = fixed("d_code", [P, RC, FG, 512], U32)
-        d_plane = fixed("d_plane", [P, RC, FG, 512], U8)
+        d_code = [fixed("d_code%d" % rc, [P, FG, 512], U32) for rc in range(RC)]
+        d_plane = [fixed("d_plane%d" % rc, [P, FG, 512], U8) for rc in range(RC)]
         ident = fixed("ident", [P, P], F32)
-        bias_rows = fixed("bias_rows", [P, 256], BF16)
-        bias_cols = fixed("bias_cols", [P, 8], F32)
+        bias_words = fixed("bias_words", [P, 8], F32)
         bias = fixed("bias", [P, R], BF16)
         warm = fixed("warm", [P, 1], F32)
 
         def clear(engine, plane):
             engine.memset(plane[:].rearrange("p g n -> p (g n)").bitcast(I32), 0)
 
-        nc.vector.memset(bias_rows[:].bitcast(I32), 0)
-        clear(nc.vector, c_plane[0])
-        clear(nc.vector, b_plane[0])
-        nc.vector.memset(warm[:], 0.0)
         pairs_v = pairs.rearrange("(n i p) k -> n p i k", i=2, p=P)
         act_v = activity.rearrange("(n i p) f -> n p i f", i=2, p=P)
-        c_scales_v = c_scales.bitcast(I32).rearrange("g r n -> r g n")
-        b_scales_v = b_scales.bitcast(I32).rearrange("g r n -> r g n")
-        c_words_v = c_words.bitcast(I32).rearrange("(h g) p n -> h p g n", g=2)
-        b_words_v = b_words.bitcast(I32).rearrange("(h g) p n -> h p g n", g=2)
+        c_scales_v = c_scales.bitcast(I32).rearrange("g (q r) n -> r q g n", r=4)
+        b_scales_v = b_scales.bitcast(I32).rearrange("g (q r) n -> r q g n", r=4)
+        c_words_v = c_words.bitcast(I32).rearrange("g p n -> p g n")
+        b_words_v = b_words.bitcast(I32).rearrange("g p n -> p g n")
 
-        def load_pairs(j, queue=nc.sync):
-            queue.dma_start(out=raw[j][:], in_=pairs_v[j])
+        def load_pairs(j):
+            nc.sync.dma_start(out=raw[j][:], in_=pairs_v[j])
 
         def load_act(j):
             nc.sync.dma_start(out=act[j][:], in_=act_v[j])
 
-        def load_codes(queue, codes, source, i, h):
-            queue.dma_start(out=codes[i][h][:].bitcast(I32), in_=source[h, :, :, 256 * i : 256 * (i + 1)])
+        def load_codes(codes, source, i, piece):
+            lo, hi = PIECES[i][piece]
+            nc.sync.dma_start(out=codes[i, lo][:].bitcast(I32), in_=source[:, lo:hi, 256 * i : 256 * (i + 1)])
 
-        def load_scales(queue, plane, source, i):
-            for q in range(4):
-                queue.dma_start(
-                    out=plane[i][32 * q : 32 * q + 4].bitcast(I32),
-                    in_=source[4 * q : 4 * q + 4, :, 128 * i : 128 * (i + 1)],
+        def codes_of(codes, i, g):
+            lo = max(first_g for first_g, end_g in PIECES[i] if first_g <= g)
+            return codes[i, lo][:, g - lo]
+
+        def load_scales(plane, source, i):
+            for r in range(4):
+                nc.sync.dma_start(
+                    out=plane[i][r:P:32].bitcast(I32),
+                    in_=source[r, :, :, 128 * i : 128 * (i + 1)],
                 )
 
-        make_identity(nc, ident[:])
-        clear(nc.gpsimd, c_plane[1])
-        clear(nc.gpsimd, b_plane[1])
-        load_codes(nc.sync, c_code, c_words_v, 0, 0)
-        nc.scalar.dma_start(out=bias_rows[0:8, :], in_=pair_bias.rearrange("(c n) -> c n", n=256))
-        load_scales(nc.sync, c_plane, c_scales_v, 0)
-        load_codes(nc.sync, b_code, b_words_v, 0, 0)
-        load_scales(nc.sync, b_plane, b_scales_v, 0)
-        load_pairs(0)
-        load_codes(nc.sync, c_code, c_words_v, 0, 1)
-        load_codes(nc.sync, b_code, b_words_v, 0, 1)
-        load_scales(nc.sync, b_plane, b_scales_v, 1)
-        load_codes(nc.sync, b_code, b_words_v, 1, 0)
-        load_codes(nc.sync, b_code, b_words_v, 1, 1)
-        load_act(0)
-        load_act(1)
-        load_pairs(1)
-        load_pairs(2)
-        nc.scalar.activation(out=warm[:], in_=warm[:], func=ACT.Sigmoid)
+        def load_bias():
+            nc.sync.dma_start(out=bias_words[:].bitcast(BF16), in_=pair_bias.rearrange("(p n) -> p n", p=P))
 
-        def bias_step():
-            bank = new_bank()
-            nc.tensor.transpose(bank[:, 0:P], bias_rows[:].bitcast(F32), ident[:])
-            nc.scalar.copy(out=bias_cols[:], in_=bank[:, 0:8])
+        def spread_bias():
+            spread = bias[:].bitcast(F32).rearrange("q (p h c) -> q h p c", h=2, c=4)
             for half in range(2):
                 bank = new_bank()
-                for i in range(4):
-                    c = 4 * half + i
-                    nc.tensor.transpose(
-                        bank[:, i * P : (i + 1) * P], bias_cols[:, c : c + 1].to_broadcast([P, P]), ident[:]
-                    )
-                nc.scalar.copy(out=bias[:, 1024 * half : 1024 * (half + 1)].bitcast(F32), in_=bank[:])
-
-        def warm_up():
-            bank = new_bank()
-            for i in range(WARM_UP):
-                nc.tensor.matmul_mx(
-                    out=bank[:],
-                    lhsT=c_code[0][0][:, 0, 0:256].bitcast(FP4X4),
-                    lhsT_scale=c_plane[1][:, 1, 0:P],
-                    rhs=b_code[0][0][:, 0, :].bitcast(FP4X4),
-                    rhs_scale=c_plane[1][:, 0, :],
-                    start=(i == 0),
-                    stop=(i == WARM_UP - 1),
-                )
+                for c in range(4):
+                    column = bias_words[:, 4 * half + c : 4 * half + c + 1]
+                    nc.tensor.transpose(bank[:, c * P : (c + 1) * P], column.to_broadcast([P, P]), ident[:])
+                nc.scalar.copy(out=spread[:, half], in_=bank[:].rearrange("q (c p) -> q p c", c=4))
 
         perm = {}
         grouped = {}
 
-        def pairs_permute(j, copy=nc.vector.tensor_copy):
-            t = work.tile([P, 2 * F // 2], F32, name="perm", tag="perm", bufs=4, align_bytes=64)
-            perm[j] = t
+        def pairs_permute(j, copy):
+            perm[j] = work.tile([P, F], F32, name="perm", tag="perm", bufs=PERM_BUFS, align_bytes=64)
             copy(
-                out=t[:].rearrange("p (u n x) -> p u n x", u=2, x=8),
+                out=perm[j][:].rearrange("p (u n x) -> p u n x", u=2, x=8),
                 in_=raw[j][:].rearrange("p i k -> p (i k)").bitcast(F32).rearrange("p (n u x) -> p u n x", u=2, x=8),
             )
 
-        def pairs_turn(i):
+        def pairs_turn(i, copy=nc.scalar.copy):
             j, rc = i // 2, i // 4
             if i % 4 == 0:
                 grouped[rc] = work.tile([P, FG, 512, 4], BF16, name="grouped", tag="grouped", bufs=2, align_bytes=64)
             bank = new_bank()
-            words = perm[j][:]
             for g in range(FG):
                 for u in range(2):
                     start = 512 * u + 256 * (i % 2) + 128 * g
                     nc.tensor.transpose(
-                        bank[:, (2 * g + u) * P : (2 * g + u + 1) * P], words[:, start : start + P], ident[:]
+                        bank[:, (2 * g + u) * P : (2 * g + u + 1) * P], perm[j][:, start : start + P], ident[:]
                     )
             r0 = 128 * (i % 4)
-            nc.scalar.copy(
-                out=grouped[rc][:].rearrange("p g r t -> p g (r t)").bitcast(F32)[:, :, 2 * r0 : 2 * r0 + 256].rearrange("p g (r u) -> p g r u", u=2),
+            words = grouped[rc][:].rearrange("p g r t -> p g (r t)").bitcast(F32)
+            copy(
+                out=words[:, :, 2 * r0 : 2 * r0 + 256].rearrange("p g (r u) -> p g r u", u=2),
                 in_=bank[:].rearrange("p (g u r) -> p g r u", g=FG, u=2),
             )
 
         def pairs_quantize(rc):
             nc.vector.quantize_mx(
-                out=d_code[:, rc].rearrange("p g r -> p (g r)").bitcast(FP8X4),
-                scales=d_plane[:, rc].rearrange("p g r -> p (g r)"),
+                out=d_code[rc][:].rearrange("p g r -> p (g r)").bitcast(FP8X4),
+                scales=d_plane[rc][:].rearrange("p g r -> p (g r)"),
                 in_=grouped[rc][:].rearrange("p g r t -> p (g r t)"),
             )
 
         def first_pass(bank, m, f, g):
-            h, s = g // 2, g % 2
-            c_cols = slice(P * (m % 4), P * (m % 4 + 1))
             nc.tensor.matmul_mx(
                 out=bank[:],
-                lhsT=c_code[m // 4][h][:, s, 256 * (m % 4) : 256 * (m % 4 + 1)].bitcast(FP4X4),
-                lhsT_scale=c_plane[m // 4][:, g, c_cols],
-                rhs=b_code[f][h][:, s, :].bitcast(FP4X4),
+                lhsT=codes_of(c_code, m // 4, g)[:, 256 * (m % 4) : 256 * (m % 4 + 1)].bitcast(FP4X4),
+                lhsT_scale=c_plane[m // 4][:, g, P * (m % 4) : P * (m % 4 + 1)],
+                rhs=codes_of(b_code, f, g).bitcast(FP4X4),
                 rhs_scale=b_plane[f][:, g, :],
                 start=(g == 0),
                 stop=(g == KG - 1),
@@ -186,34 +151,32 @@ def tile_drug_synergy_bilinear_s4_kernel(
         h_turned = {}
 
         def gate(bank, m, f):
-            if f == 0:
+            if m not in gated:
                 gated[m] = work.tile([P, F], BF16, name="gated", tag="gated", bufs=6, align_bytes=64)
+            half = gated[m][:].rearrange("p (u g n) -> p u g n", u=2, g=FG)[:, :, f, :]
             nc.vector.tensor_tensor(
-                out=gated[m][:].rearrange("p (u g n) -> p u g n", u=2, g=FG)[:, :, f, :].rearrange("p u (b x) -> p u b x", x=16),
+                out=half.rearrange("p u (b x) -> p u b x", x=16),
                 in0=bank[:].rearrange("p (b u x) -> p u b x", u=2, x=16),
                 in1=act[m // 2][:, m % 2, 512 * f : 512 * (f + 1)].rearrange("p (b u x) -> p u b x", u=2, x=16),
                 op=ALU.mult,
             )
 
-        def first_half(m, f):
+        def first(m, f):
             bank = new_bank()
             for g in range(KG):
                 first_pass(bank, m, f, g)
             gate(bank, m, f)
 
-        four = []
-
-        def first_four(h):
-            if h == 0:
-                four.extend([new_bank() for m in range(4)])
+        def first_four():
+            banks = [new_bank() for m in range(4)]
             for m in range(4):
-                for g in range(2 * h, 2 * h + 2):
-                    first_pass(four[m], m, 0, g)
-            if h == 1:
-                for m in range(4):
-                    gate(four[m], m, 0)
+                first_pass(banks[m], m, 0, 0)
+            for m in range(4):
+                for g in range(1, KG):
+                    first_pass(banks[m], m, 0, g)
+                gate(banks[m], m, 0)
 
-        def h_turn(m):
+        def h_turn(m, copy=nc.scalar.copy):
             bank = new_bank()
             words = gated[m][:].bitcast(F32)
             for g in range(FG):
@@ -223,130 +186,166 @@ def tile_drug_synergy_bilinear_s4_kernel(
                         bank[:, (2 * g + u) * P : (2 * g + u + 1) * P], words[:, start : start + P], ident[:]
                     )
             h_turned[m] = work.tile([P, 4 * FG * P], BF16, name="h_turned", tag="h_turned", bufs=4, align_bytes=64)
-            nc.scalar.copy(
+            copy(
                 out=h_turned[m][:].bitcast(F32).rearrange("p (g r u) -> p g r u", g=FG, u=2),
                 in_=bank[:].rearrange("p (g u r) -> p g r u", g=FG, u=2),
             )
 
         def h_quantize(m):
-            h_code[m] = work.tile([P, FG * P], U32, name="h_code", tag="h_code", bufs=6, align_bytes=64)
-            h_plane[m] = work.tile([P, FG * P], U8, name="h_plane", tag="h_plane", bufs=6, align_bytes=64)
+            h_code[m] = work.tile([P, FG * P], U32, name="h_code", tag="h_code", bufs=MT, align_bytes=64)
+            h_plane[m] = work.tile([P, FG * P], U8, name="h_plane", tag="h_plane", bufs=MT, align_bytes=64)
             nc.vector.quantize_mx(out=h_code[m][:].bitcast(FP8X4), scales=h_plane[m][:], in_=h_turned[m][:])
 
-        def second(m, half, pieces=((0, 1024),)):
-            z = work.tile([P, 1024], F32, name="z", tag="z", bufs=8, align_bytes=64)
-            for i in range(2):
-                bank = new_bank()
-                rc = 2 * half + i
-                for g in range(FG):
-                    nc.tensor.matmul_mx(
-                        out=bank[:],
-                        lhsT=h_code[m][:, P * g : P * (g + 1)].bitcast(FP8X4),
-                        lhsT_scale=h_plane[m][:, P * g : P * (g + 1)],
-                        rhs=d_code[:, rc, g].bitcast(FP8X4),
-                        rhs_scale=d_plane[:, rc, g],
-                        start=(g == 0),
-                        stop=(g == FG - 1),
-                    )
-                for first_col, end_col in pieces:
-                    lo, hi = max(first_col, 512 * i), min(end_col, 512 * (i + 1))
-                    if lo < hi:
-                        nc.vector.tensor_tensor(
-                            out=z[:, lo:hi],
-                            in0=bank[:, lo - 512 * i : hi - 512 * i],
-                            in1=bias[:, 1024 * half + lo : 1024 * half + hi],
-                            op=ALU.add,
-                        )
-                    if lo < hi and hi == end_col:
-                        piece = z[:, first_col:end_col]
-                        nc.scalar.activation(out=piece, in_=piece, func=ACT.Sigmoid)
-                        nc.sync.dma_start(
-                            out=out[P * m : P * (m + 1), 1024 * half + first_col : 1024 * half + end_col], in_=piece
-                        )
+        z = {}
+        waiting = []
 
-        bias_step()
-        warm_up()
-        load_scales(nc.sync, c_plane, c_scales_v, 1)
-        load_codes(nc.sync, c_code, c_words_v, 1, 0)
-        load_codes(nc.sync, c_code, c_words_v, 1, 1)
+        def second(m, rc, lo=0, hi=512):
+            if (m, rc // 2) not in z:
+                z[m, rc // 2] = work.tile([P, 1024], F32, name="z", tag="z", bufs=Z_BUFS, align_bytes=64)
+            bank = new_bank()
+            for g in range(FG):
+                nc.tensor.matmul_mx(
+                    out=bank[:, lo:hi],
+                    lhsT=h_code[m][:, P * g : P * (g + 1)].bitcast(FP8X4),
+                    lhsT_scale=h_plane[m][:, P * g : P * (g + 1)],
+                    rhs=d_code[rc][:, g, lo:hi].bitcast(FP8X4),
+                    rhs_scale=d_plane[rc][:, g, lo:hi],
+                    start=(g == 0),
+                    stop=(g == FG - 1),
+                )
+            col = 512 * rc
+            nc.vector.tensor_tensor(
+                out=z[m, rc // 2][:, col % 1024 + lo : col % 1024 + hi],
+                in0=bank[:, lo:hi],
+                in1=bias[:, col + lo : col + hi],
+                op=ALU.add,
+            )
+            waiting.append((m, col + lo, col + hi))
+
+        def finish(join=True):
+            open_from = None
+            for n, (m, lo, hi) in enumerate(waiting):
+                piece = z[m, lo // 1024][:, lo % 1024 : lo % 1024 + hi - lo]
+                nc.scalar.activation(out=piece, in_=piece, func=ACT.Sigmoid)
+                if open_from is None:
+                    open_from = lo
+                follows = n + 1 < len(waiting) and waiting[n + 1][:2] == (m, hi) and hi % 1024 != 0
+                if not (join and follows):
+                    nc.sync.dma_start(
+                        out=out[P * m : P * (m + 1), open_from:hi],
+                        in_=z[m, lo // 1024][:, open_from % 1024 : open_from % 1024 + hi - open_from],
+                    )
+                    open_from = None
+            waiting.clear()
+
+        on_vector, on_scalar = nc.vector.tensor_copy, nc.scalar.copy
+
+        clear(nc.vector, c_plane[0])
+        clear(nc.vector, b_plane[0])
+        nc.vector.memset(warm[:], 0.0)
+        clear(nc.vector, b_plane[1])
+        clear(nc.vector, c_plane[1])
+        make_identity(nc, ident[:])
+        load_bias()
+        load_codes(c_code, c_words_v, 0, 0)
+        load_codes(b_code, b_words_v, 0, 0)
+        load_scales(c_plane, c_scales_v, 0)
+        load_scales(b_plane, b_scales_v, 0)
+        load_codes(c_code, c_words_v, 0, 1)
+        load_codes(b_code, b_words_v, 0, 1)
+        load_scales(b_plane, b_scales_v, 1)
+        load_codes(b_code, b_words_v, 1, 0)
+        load_act(0)
+        load_act(1)
+        load_pairs(0)
+        load_pairs(1)
+        load_scales(c_plane, c_scales_v, 1)
+        load_codes(c_code, c_words_v, 1, 0)
+        load_pairs(2)
         load_pairs(3)
-        load_pairs(4)
         load_act(2)
+        load_pairs(4)
         load_pairs(5)
         load_pairs(6)
         load_pairs(7)
         load_act(3)
-        pairs_permute(0, nc.scalar.copy)
-        first_four(0)
-        first_four(1)
-        first_half(0, 1)
-        pairs_turn(0)
-        pairs_turn(1)
-        first_half(1, 1)
-        first_half(2, 1)
-        pairs_permute(1, nc.scalar.copy)
-        pairs_permute(2)
-        h_turn(0)
-        pairs_turn(2)
-        pairs_turn(3)
-        h_quantize(0)
-        pairs_permute(3)
-        h_turn(1)
-        first_half(3, 1)
-        pairs_turn(4)
-        pairs_turn(5)
-        h_quantize(1)
-        h_turn(2)
-        pairs_permute(4)
+        nc.scalar.activation(out=warm[:], in_=warm[:], func=ACT.Sigmoid)
+        spread_bias()
+
+        first_four()
+        pairs_permute(0, on_scalar)
+        pairs_permute(1, on_scalar)
+        for m in range(4):
+            first(m, 1)
+        for i in range(0, 4):
+            pairs_turn(i)
+        first(4, 0)
+        pairs_permute(2, on_vector)
         pairs_quantize(0)
+        for m in range(4):
+            h_turn(m)
+        pairs_permute(3, on_vector)
+        first(4, 1)
+        h_quantize(0)
+        h_quantize(1)
+        first(5, 0)
+        for i in range(4, 8):
+            pairs_turn(i)
         h_quantize(2)
-        h_turn(3)
-        pairs_permute(5)
         h_quantize(3)
-        first_half(4, 0)
-        first_half(4, 1)
-        pairs_turn(6)
-        pairs_turn(7)
-        pairs_permute(6, nc.scalar.copy)
-        pairs_permute(7, nc.scalar.copy)
-        pairs_quantize(1)
-        first_half(5, 0)
-        first_half(5, 1)
-        h_turn(4)
-        h_quantize(4)
-        pairs_turn(8)
-        pairs_turn(9)
-        pairs_turn(10)
-        pairs_turn(11)
+        pairs_permute(4, on_vector)
         second(0, 0)
         second(1, 0)
-        pairs_turn(12)
-        pairs_turn(13)
-        pairs_quantize(2)
-        pairs_turn(14)
-        pairs_turn(15)
+        pairs_permute(5, on_vector)
         second(2, 0)
-        first_half(6, 0)
-        first_half(6, 1)
+        finish()
+        pairs_quantize(1)
         second(3, 0)
-        pairs_quantize(3)
-        h_turn(5)
-        h_turn(6)
-        second(4, 0)
+        for i in range(8, 12):
+            pairs_turn(i)
+        pairs_permute(6, on_vector)
+        first(5, 1)
+        pairs_permute(7, on_vector)
         second(0, 1)
+        finish()
         second(1, 1)
-        first_half(7, 0)
-        first_half(7, 1)
+        pairs_quantize(2)
+        for i in range(12, 16):
+            pairs_turn(i)
         second(2, 1)
-        h_quantize(5)
-        h_turn(7)
         second(3, 1)
-        second(5, 0)
-        second(4, 1, ((0, 512), (512, 1024)))
+        finish()
+        first(6, 0)
+        h_turn(4)
+        h_turn(5)
+        pairs_quantize(3)
+        first(6, 1)
+        h_quantize(4)
+        h_quantize(5)
+        for m in range(4):
+            second(m, 2)
+            second(m, 3)
+            finish()
+            if m % 2 == 0:
+                first(7, m // 2)
+        h_turn(6)
+        h_turn(7)
+        second(4, 0)
+        second(4, 1)
         h_quantize(6)
-        second(5, 1, ((0, 512), (512, 1024)))
-        second(6, 0, ((0, 512), (512, 1024)))
+        finish()
+        second(4, 2)
+        second(4, 3)
         h_quantize(7)
-        second(6, 1, ((0, 512), (512, 1024)))
-        second(7, 0, ((0, 512), (512, 1024)))
-        second(7, 1, ((0, 512), (512, 768), (768, 1024)))
+        finish()
+        for m in range(5, 8):
+            second(m, 0)
+            second(m, 1)
+            finish()
+            second(m, 2)
+            if m < 7:
+                second(m, 3)
+            finish()
+        second(7, 3, 0, 256)
+        second(7, 3, 256, 512)
+        finish(False)

@@ -23,8 +23,12 @@ MT = M // P
 RT = R // P
 RC = R // 512
 PERM_BUFS = 8
-Z_BUFS = 8
-PIECES = (((0, 1), (1, 4)), ((0, 4),))
+Z_BUFS = 10
+PIECES = (((0, 1), (1, 2), (2, 4)), ((0, 4),))
+PERMS = {0: ((1, "V"),), 1: ((2, "V"), (3, "S")), 2: ((4, "V"), (5, "S")), 3: ((6, "V"), (7, "S"))}
+UNITS = [3,3,3,3,4,4,4,4,3,3]
+AHEAD = 0
+HQ_AFTER = 1
 
 
 def tile_drug_synergy_bilinear_s4_kernel(
@@ -169,12 +173,11 @@ def tile_drug_synergy_bilinear_s4_kernel(
 
         def first_four():
             banks = [new_bank() for m in range(4)]
-            for m in range(4):
-                first_pass(banks[m], m, 0, 0)
-            for m in range(4):
-                for g in range(1, KG):
-                    first_pass(banks[m], m, 0, g)
-                gate(banks[m], m, 0)
+            for lo, hi in PIECES[0]:
+                for m in range(4):
+                    for g in range(lo, hi):
+                        first_pass(banks[m], m, 0, g)
+            return banks
 
         def h_turn(m, copy=nc.scalar.copy):
             bank = new_bank()
@@ -225,26 +228,37 @@ def tile_drug_synergy_bilinear_s4_kernel(
         def finish(join=True):
             open_from = None
             for n, (m, lo, hi) in enumerate(waiting):
-                piece = z[m, lo // 1024][:, lo % 1024 : lo % 1024 + hi - lo]
-                nc.scalar.activation(out=piece, in_=piece, func=ACT.Sigmoid)
                 if open_from is None:
                     open_from = lo
                 follows = n + 1 < len(waiting) and waiting[n + 1][:2] == (m, hi) and hi % 1024 != 0
                 if not (join and follows):
-                    nc.sync.dma_start(
-                        out=out[P * m : P * (m + 1), open_from:hi],
-                        in_=z[m, lo // 1024][:, open_from % 1024 : open_from % 1024 + hi - open_from],
-                    )
+                    piece = z[m, lo // 1024][:, open_from % 1024 : open_from % 1024 + hi - open_from]
+                    nc.scalar.activation(out=piece, in_=piece, func=ACT.Sigmoid)
+                    nc.sync.dma_start(out=out[P * m : P * (m + 1), open_from:hi], in_=piece)
                     open_from = None
             waiting.clear()
+
+        def warm_up(passes):
+            zeros = c_plane[1][:].rearrange("p g n -> p (g n)")
+            bank = new_bank()
+            for i in range(passes):
+                nc.tensor.matmul_mx(
+                    out=bank[:],
+                    lhsT=zeros[:, 0:256].bitcast(FP4X4),
+                    lhsT_scale=zeros[:, 0:P],
+                    rhs=zeros[:, 0:1024].bitcast(FP4X4),
+                    rhs_scale=zeros[:, 0:512],
+                    start=(i == 0),
+                    stop=(i == passes - 1),
+                )
 
         on_vector, on_scalar = nc.vector.tensor_copy, nc.scalar.copy
 
         clear(nc.vector, c_plane[0])
         clear(nc.vector, b_plane[0])
+        clear(nc.vector, c_plane[1])
         nc.vector.memset(warm[:], 0.0)
         clear(nc.vector, b_plane[1])
-        clear(nc.vector, c_plane[1])
         make_identity(nc, ident[:])
         load_bias()
         load_codes(c_code, c_words_v, 0, 0)
@@ -253,99 +267,77 @@ def tile_drug_synergy_bilinear_s4_kernel(
         load_scales(b_plane, b_scales_v, 0)
         load_codes(c_code, c_words_v, 0, 1)
         load_codes(b_code, b_words_v, 0, 1)
+        load_codes(c_code, c_words_v, 0, 2)
+        load_codes(b_code, b_words_v, 0, 2)
+        load_act(0)
         load_scales(b_plane, b_scales_v, 1)
         load_codes(b_code, b_words_v, 1, 0)
-        load_act(0)
-        load_act(1)
         load_pairs(0)
+        load_act(1)
         load_pairs(1)
-        load_scales(c_plane, c_scales_v, 1)
-        load_codes(c_code, c_words_v, 1, 0)
         load_pairs(2)
         load_pairs(3)
-        load_act(2)
-        load_pairs(4)
-        load_pairs(5)
-        load_pairs(6)
-        load_pairs(7)
-        load_act(3)
         nc.scalar.activation(out=warm[:], in_=warm[:], func=ACT.Sigmoid)
+        warm_up(2)
         spread_bias()
+        warm_up(2)
+        load_scales(c_plane, c_scales_v, 1)
+        load_codes(c_code, c_words_v, 1, 0)
+        load_act(2)
+        for j in range(4, 8):
+            load_pairs(j)
+        load_act(3)
 
-        first_four()
+        four = first_four()
+        gate(four[0], 0, 0)
+        gate(four[1], 1, 0)
         pairs_permute(0, on_scalar)
-        pairs_permute(1, on_scalar)
-        for m in range(4):
-            first(m, 1)
-        for i in range(0, 4):
-            pairs_turn(i)
-        first(4, 0)
-        pairs_permute(2, on_vector)
-        pairs_quantize(0)
-        for m in range(4):
-            h_turn(m)
-        pairs_permute(3, on_vector)
-        first(4, 1)
-        h_quantize(0)
-        h_quantize(1)
-        first(5, 0)
-        for i in range(4, 8):
-            pairs_turn(i)
-        h_quantize(2)
-        h_quantize(3)
-        pairs_permute(4, on_vector)
-        second(0, 0)
-        second(1, 0)
-        pairs_permute(5, on_vector)
-        second(2, 0)
-        finish()
-        pairs_quantize(1)
-        second(3, 0)
-        for i in range(8, 12):
-            pairs_turn(i)
-        pairs_permute(6, on_vector)
-        first(5, 1)
-        pairs_permute(7, on_vector)
-        second(0, 1)
-        finish()
-        second(1, 1)
-        pairs_quantize(2)
-        for i in range(12, 16):
-            pairs_turn(i)
-        second(2, 1)
-        second(3, 1)
-        finish()
-        first(6, 0)
-        h_turn(4)
-        h_turn(5)
-        pairs_quantize(3)
-        first(6, 1)
-        h_quantize(4)
-        h_quantize(5)
-        for m in range(4):
-            second(m, 2)
-            second(m, 3)
-            finish()
-            if m % 2 == 0:
-                first(7, m // 2)
-        h_turn(6)
-        h_turn(7)
-        second(4, 0)
-        second(4, 1)
-        h_quantize(6)
-        finish()
-        second(4, 2)
-        second(4, 3)
-        h_quantize(7)
-        finish()
-        for m in range(5, 8):
-            second(m, 0)
-            second(m, 1)
-            finish()
-            second(m, 2)
-            if m < 7:
-                second(m, 3)
-            finish()
-        second(7, 3, 0, 256)
-        second(7, 3, 256, 512)
+        first(0, 1)
+        gate(four[2], 2, 0)
+        first(1, 1)
+        gate(four[3], 3, 0)
+        halves = [(2, 1), (3, 1)] + [(m, f) for m in range(4, MT) for f in range(FG)]
+        to_turn = [0, 1]
+        ready_cells, ready_pairs, ready_units = [], [], []
+        step = 0
+        while halves:
+            units, ready_units = ready_units[:UNITS[step]], ready_units[UNITS[step]:]
+            turned = to_turn.pop(0) if to_turn else None
+            if step < RT // 2:
+                pairs_turn(2 * step)
+                pairs_turn(2 * step + 1)
+            if turned is not None:
+                h_turn(turned)
+            for j, copy in PERMS.get(step, ()):
+                pairs_permute(j, on_vector if copy == "V" else on_scalar)
+            finish(False)
+            for m, rc in units[:AHEAD]:
+                second(m, rc)
+            m, f = halves.pop(0)
+            first(m, f)
+            if f == FG - 1:
+                to_turn.append(m)
+            if step < RT // 2 and step % 2 == 1:
+                pairs_quantize(step // 2)
+                ready_pairs.append(step // 2)
+                ready_units.extend((m, step // 2) for m in ready_cells)
+            for m, rc in units[AHEAD:AHEAD + HQ_AFTER]:
+                second(m, rc)
+            if turned is not None:
+                h_quantize(turned)
+                ready_cells.append(turned)
+                ready_units.extend((turned, rc) for rc in ready_pairs)
+            for m, rc in units[AHEAD + HQ_AFTER:]:
+                second(m, rc)
+            step += 1
+        h_turn(MT - 1)
+        finish(False)
+        for n, (m, rc) in enumerate(ready_units + [(MT - 1, rc) for rc in range(RC - 1)]):
+            second(m, rc)
+            if n == 0:
+                h_quantize(MT - 1)
+            else:
+                finish(False)
+        second(MT - 1, RC - 1, 0, 256)
+        second(MT - 1, RC - 1, 256, 512)
         finish(False)

@@ -22,13 +22,14 @@ FG = F // 512
 MT = M // P
 RT = R // P
 RC = R // 512
-PERM_BUFS = 8
-Z_BUFS = 10
+PERM_BUFS = 4
+Z_BUFS = 16
 PIECES = (((0, 1), (1, 2), (2, 4)), ((0, 4),))
-PERMS = {0: ((1, "V"),), 1: ((2, "V"), (3, "S")), 2: ((4, "V"), (5, "S")), 3: ((6, "V"), (7, "S"))}
-UNITS = [3,3,3,3,4,4,4,4,3,3]
-AHEAD = 0
-HQ_AFTER = 1
+PERMS = {1: ((2, "V"), (3, "S")), 2: ((4, "V"),), 3: ((5, "S"),), 4: ((6, "V"),), 5: ((7, "S"),)}
+UNITS = [3,3,3,3,3,4,3,4,3,3]
+SOLO = [0,0,1,1,1,1,1,1,1,1]
+GROUP = 2
+LEFT = 1
 
 
 def tile_drug_synergy_bilinear_s4_kernel(
@@ -113,7 +114,20 @@ def tile_drug_synergy_bilinear_s4_kernel(
                 in_=raw[j][:].rearrange("p i k -> p (i k)").bitcast(F32).rearrange("p (n u x) -> p u n x", u=2, x=8),
             )
 
-        def pairs_turn(i, copy=nc.scalar.copy):
+        copies = []
+
+        def last_first(items):
+            ordered = items[-1:] + items[:-1]
+            items.clear()
+            return ordered
+
+        def empty_turned(grouped_copies=True):
+            ordered = last_first(copies) if grouped_copies else copies[:]
+            copies.clear()
+            for target, source in ordered:
+                nc.scalar.copy(out=target, in_=source)
+
+        def pairs_turn(i):
             j, rc = i // 2, i // 4
             if i % 4 == 0:
                 grouped[rc] = work.tile([P, FG, 512, 4], BF16, name="grouped", tag="grouped", bufs=2, align_bytes=64)
@@ -126,9 +140,11 @@ def tile_drug_synergy_bilinear_s4_kernel(
                     )
             r0 = 128 * (i % 4)
             words = grouped[rc][:].rearrange("p g r t -> p g (r t)").bitcast(F32)
-            copy(
-                out=words[:, :, 2 * r0 : 2 * r0 + 256].rearrange("p g (r u) -> p g r u", u=2),
-                in_=bank[:].rearrange("p (g u r) -> p g r u", g=FG, u=2),
+            copies.append(
+                (
+                    words[:, :, 2 * r0 : 2 * r0 + 256].rearrange("p g (r u) -> p g r u", u=2),
+                    bank[:].rearrange("p (g u r) -> p g r u", g=FG, u=2),
+                )
             )
 
         def pairs_quantize(rc):
@@ -156,7 +172,7 @@ def tile_drug_synergy_bilinear_s4_kernel(
 
         def gate(bank, m, f):
             if m not in gated:
-                gated[m] = work.tile([P, F], BF16, name="gated", tag="gated", bufs=6, align_bytes=64)
+                gated[m] = work.tile([P, F], BF16, name="gated", tag="gated", bufs=4, align_bytes=64)
             half = gated[m][:].rearrange("p (u g n) -> p u g n", u=2, g=FG)[:, :, f, :]
             nc.vector.tensor_tensor(
                 out=half.rearrange("p u (b x) -> p u b x", x=16),
@@ -179,7 +195,7 @@ def tile_drug_synergy_bilinear_s4_kernel(
                         first_pass(banks[m], m, 0, g)
             return banks
 
-        def h_turn(m, copy=nc.scalar.copy):
+        def h_turn(m):
             bank = new_bank()
             words = gated[m][:].bitcast(F32)
             for g in range(FG):
@@ -189,9 +205,11 @@ def tile_drug_synergy_bilinear_s4_kernel(
                         bank[:, (2 * g + u) * P : (2 * g + u + 1) * P], words[:, start : start + P], ident[:]
                     )
             h_turned[m] = work.tile([P, 4 * FG * P], BF16, name="h_turned", tag="h_turned", bufs=4, align_bytes=64)
-            copy(
-                out=h_turned[m][:].bitcast(F32).rearrange("p (g r u) -> p g r u", g=FG, u=2),
-                in_=bank[:].rearrange("p (g u r) -> p g r u", g=FG, u=2),
+            copies.append(
+                (
+                    h_turned[m][:].bitcast(F32).rearrange("p (g r u) -> p g r u", g=FG, u=2),
+                    bank[:].rearrange("p (g u r) -> p g r u", g=FG, u=2),
+                )
             )
 
         def h_quantize(m):
@@ -200,6 +218,7 @@ def tile_drug_synergy_bilinear_s4_kernel(
             nc.vector.quantize_mx(out=h_code[m][:].bitcast(FP8X4), scales=h_plane[m][:], in_=h_turned[m][:])
 
         z = {}
+        sums = []
         waiting = []
 
         def second(m, rc, lo=0, hi=512):
@@ -216,27 +235,23 @@ def tile_drug_synergy_bilinear_s4_kernel(
                     start=(g == 0),
                     stop=(g == FG - 1),
                 )
-            col = 512 * rc
-            nc.vector.tensor_tensor(
-                out=z[m, rc // 2][:, col % 1024 + lo : col % 1024 + hi],
-                in0=bank[:, lo:hi],
-                in1=bias[:, col + lo : col + hi],
-                op=ALU.add,
-            )
-            waiting.append((m, col + lo, col + hi))
+            sums.append((bank, m, 512 * rc + lo, 512 * rc + hi))
 
-        def finish(join=True):
-            open_from = None
-            for n, (m, lo, hi) in enumerate(waiting):
-                if open_from is None:
-                    open_from = lo
-                follows = n + 1 < len(waiting) and waiting[n + 1][:2] == (m, hi) and hi % 1024 != 0
-                if not (join and follows):
-                    piece = z[m, lo // 1024][:, open_from % 1024 : open_from % 1024 + hi - open_from]
-                    nc.scalar.activation(out=piece, in_=piece, func=ACT.Sigmoid)
-                    nc.sync.dma_start(out=out[P * m : P * (m + 1), open_from:hi], in_=piece)
-                    open_from = None
-            waiting.clear()
+        def add_bias():
+            for bank, m, lo, hi in last_first(sums):
+                nc.vector.tensor_tensor(
+                    out=z[m, lo // 1024][:, lo % 1024 : lo % 1024 + hi - lo],
+                    in0=bank[:, lo % 512 : lo % 512 + hi - lo],
+                    in1=bias[:, lo:hi],
+                    op=ALU.add,
+                )
+                waiting.append((m, lo, hi))
+
+        def finish():
+            for m, lo, hi in last_first(waiting):
+                piece = z[m, lo // 1024][:, lo % 1024 : lo % 1024 + hi - lo]
+                nc.scalar.activation(out=piece, in_=piece, func=ACT.Sigmoid)
+                nc.sync.dma_start(out=out[P * m : P * (m + 1), lo:hi], in_=piece)
 
         def warm_up(passes):
             zeros = c_plane[1][:].rearrange("p g n -> p (g n)")
@@ -291,10 +306,11 @@ def tile_drug_synergy_bilinear_s4_kernel(
         four = first_four()
         gate(four[0], 0, 0)
         gate(four[1], 1, 0)
-        pairs_permute(0, on_scalar)
+        pairs_permute(0, on_vector)
         first(0, 1)
         gate(four[2], 2, 0)
         first(1, 1)
+        pairs_permute(1, on_vector)
         gate(four[3], 3, 0)
         halves = [(2, 1), (3, 1)] + [(m, f) for m in range(4, MT) for f in range(FG)]
         to_turn = [0, 1]
@@ -308,36 +324,47 @@ def tile_drug_synergy_bilinear_s4_kernel(
                 pairs_turn(2 * step + 1)
             if turned is not None:
                 h_turn(turned)
+            empty_turned(True)
+            add_bias()
             for j, copy in PERMS.get(step, ()):
                 pairs_permute(j, on_vector if copy == "V" else on_scalar)
-            finish(False)
-            for m, rc in units[:AHEAD]:
-                second(m, rc)
+            finish()
+            if turned is not None and units:
+                h_quantize(turned)
             m, f = halves.pop(0)
             first(m, f)
             if f == FG - 1:
                 to_turn.append(m)
+            if turned is not None and not units:
+                h_quantize(turned)
             if step < RT // 2 and step % 2 == 1:
                 pairs_quantize(step // 2)
                 ready_pairs.append(step // 2)
                 ready_units.extend((m, step // 2) for m in ready_cells)
-            for m, rc in units[AHEAD:AHEAD + HQ_AFTER]:
+            for n, (m, rc) in enumerate(units):
                 second(m, rc)
+                if n < SOLO[step]:
+                    add_bias()
             if turned is not None:
-                h_quantize(turned)
                 ready_cells.append(turned)
                 ready_units.extend((turned, rc) for rc in ready_pairs)
-            for m, rc in units[AHEAD + HQ_AFTER:]:
-                second(m, rc)
             step += 1
         h_turn(MT - 1)
-        finish(False)
-        for n, (m, rc) in enumerate(ready_units + [(MT - 1, rc) for rc in range(RC - 1)]):
+        empty_turned()
+        add_bias()
+        finish()
+        ready_units.extend((MT - 1, rc) for rc in range(RC - 1))
+        for n, (m, rc) in enumerate(ready_units):
             second(m, rc)
             if n == 0:
+                add_bias()
                 h_quantize(MT - 1)
-            else:
-                finish(False)
+            elif (len(ready_units) - n) % GROUP == LEFT or len(ready_units) - n <= LEFT:
+                add_bias()
+                finish()
         second(MT - 1, RC - 1, 0, 256)
+        add_bias()
+        finish()
         second(MT - 1, RC - 1, 256, 512)
-        finish(False)
+        add_bias()
+        finish()

@@ -25,11 +25,15 @@ RC = R // 512
 PERM_BUFS = 4
 Z_BUFS = 16
 PIECES = (((0, 1), (1, 2), (2, 4)), ((0, 4),))
-PERMS = {1: ((2, "V"), (3, "S")), 2: ((4, "V"),), 3: ((5, "S"),), 4: ((6, "V"),), 5: ((7, "S"),)}
-UNITS = [3,3,3,3,3,4,3,4,3,3]
-SOLO = [0,0,1,1,1,1,1,1,1,1]
-GROUP = 2
-LEFT = 1
+TURNS = [2,2,0,0,0,0]
+UNITS = [4,4,4,4,4,0]
+EARLY_PERMS = {}
+PERMS = {0: ((7, "V"),)}
+CLOSING = (2,1,2,2,1,1)
+HQ_LAST = 1
+JOIN = True
+TURN_AFTER = 3
+GROUP_S = 0
 
 
 def tile_drug_synergy_bilinear_s4_kernel(
@@ -121,8 +125,13 @@ def tile_drug_synergy_bilinear_s4_kernel(
             items.clear()
             return ordered
 
-        def empty_turned(grouped_copies=True):
-            ordered = last_first(copies) if grouped_copies else copies[:]
+        def in_order(items):
+            ordered = items[:]
+            items.clear()
+            return ordered
+
+        def empty_turned():
+            ordered = last_first(copies)
             copies.clear()
             for target, source in ordered:
                 nc.scalar.copy(out=target, in_=source)
@@ -237,8 +246,8 @@ def tile_drug_synergy_bilinear_s4_kernel(
                 )
             sums.append((bank, m, 512 * rc + lo, 512 * rc + hi))
 
-        def add_bias():
-            for bank, m, lo, hi in last_first(sums):
+        def add_bias(covered=False):
+            for bank, m, lo, hi in in_order(sums) if covered else last_first(sums):
                 nc.vector.tensor_tensor(
                     out=z[m, lo // 1024][:, lo % 1024 : lo % 1024 + hi - lo],
                     in0=bank[:, lo % 512 : lo % 512 + hi - lo],
@@ -247,8 +256,15 @@ def tile_drug_synergy_bilinear_s4_kernel(
                 )
                 waiting.append((m, lo, hi))
 
-        def finish():
-            for m, lo, hi in last_first(waiting):
+        def finish(join=True, grouped_sums=True):
+            joined = []
+            for m, lo, hi in in_order(waiting):
+                mate = [j for j in joined if j[0] == m and j[1] // 1024 == lo // 1024 and (j[2] == lo or j[1] == hi) and join]
+                if mate and hi - lo == 512:
+                    joined.remove(mate[0])
+                    lo, hi = min(lo, mate[0][1]), max(hi, mate[0][2])
+                joined.append((m, lo, hi))
+            for m, lo, hi in last_first(joined) if grouped_sums else joined:
                 piece = z[m, lo // 1024][:, lo % 1024 : lo % 1024 + hi - lo]
                 nc.scalar.activation(out=piece, in_=piece, func=ACT.Sigmoid)
                 nc.sync.dma_start(out=out[P * m : P * (m + 1), lo:hi], in_=piece)
@@ -298,70 +314,114 @@ def tile_drug_synergy_bilinear_s4_kernel(
         warm_up(2)
         load_scales(c_plane, c_scales_v, 1)
         load_codes(c_code, c_words_v, 1, 0)
+        load_pairs(4)
         load_act(2)
-        for j in range(4, 8):
-            load_pairs(j)
+        load_pairs(5)
+        load_pairs(6)
+        load_pairs(7)
         load_act(3)
+
+        def turn(cells, tiles, cells_first=True):
+            for m in cells if cells_first else ():
+                h_turn(m)
+            for i in tiles:
+                pairs_turn(i)
+            for m in () if cells_first else cells:
+                h_turn(m)
+            empty_turned()
+
+        def first_gated(m, f):
+            first(m, f)
 
         four = first_four()
         gate(four[0], 0, 0)
         gate(four[1], 1, 0)
-        pairs_permute(0, on_vector)
+        pairs_permute(0, on_scalar)
         first(0, 1)
         gate(four[2], 2, 0)
         first(1, 1)
         pairs_permute(1, on_vector)
+        turn([0], [0, 1])
         gate(four[3], 3, 0)
-        halves = [(2, 1), (3, 1)] + [(m, f) for m in range(4, MT) for f in range(FG)]
-        to_turn = [0, 1]
-        ready_cells, ready_pairs, ready_units = [], [], []
+        first(2, 1)
+        pairs_permute(2, on_vector)
+        pairs_permute(3, on_vector)
+        turn([1], [2, 3])
+        h_quantize(0)
+        pairs_quantize(0)
+        first(3, 1)
+        h_quantize(1)
+        turn([2], [4, 5, 6, 7])
+        pairs_permute(4, on_vector)
+        pairs_permute(5, on_scalar)
+        first(4, 0)
+        second(0, 0)
+        second(1, 0)
+        add_bias()
+        turn([3], [8, 9])
+        pairs_quantize(1)
+        h_quantize(2)
+        first(4, 1)
+        turn([], [10, 11])
+        finish()
+        h_quantize(3)
+        pairs_permute(6, on_vector)
+        pairs_quantize(2)
+        halves = [(m, f) for m in range(5, MT) for f in range(FG)]
+        to_turn = [4]
+        cell_from, pairs_from, multiplied = {0: 0, 1: 0, 2: 0, 3: 1, MT - 1: 99}, {0: 0, 1: 0, 2: 1}, [(0, 0), (1, 0)]
         step = 0
+        next_tile = 12
+        def ready(step):
+            units = [(max(s, t), m, rc) for m, s in cell_from.items() for rc, t in pairs_from.items()]
+            return [(m, rc) for s, m, rc in sorted(units) if s <= step and (m, rc) not in multiplied]
+
         while halves:
-            units, ready_units = ready_units[:UNITS[step]], ready_units[UNITS[step]:]
-            turned = to_turn.pop(0) if to_turn else None
-            if step < RT // 2:
-                pairs_turn(2 * step)
-                pairs_turn(2 * step + 1)
-            if turned is not None:
-                h_turn(turned)
-            empty_turned(True)
+            for m, rc in ready(step)[:UNITS[step]]:
+                second(m, rc)
+                multiplied.append((m, rc))
             add_bias()
-            for j, copy in PERMS.get(step, ()):
+            turned = to_turn.pop(0) if to_turn else None
+            for j, copy in EARLY_PERMS.get(step, ()):
                 pairs_permute(j, on_vector if copy == "V" else on_scalar)
-            finish()
-            if turned is not None and units:
-                h_quantize(turned)
             m, f = halves.pop(0)
             first(m, f)
             if f == FG - 1:
                 to_turn.append(m)
-            if turned is not None and not units:
-                h_quantize(turned)
-            if step < RT // 2 and step % 2 == 1:
-                pairs_quantize(step // 2)
-                ready_pairs.append(step // 2)
-                ready_units.extend((m, step // 2) for m in ready_cells)
-            for n, (m, rc) in enumerate(units):
-                second(m, rc)
-                if n < SOLO[step]:
-                    add_bias()
             if turned is not None:
-                ready_cells.append(turned)
-                ready_units.extend((turned, rc) for rc in ready_pairs)
-            step += 1
-        h_turn(MT - 1)
-        empty_turned()
-        add_bias()
-        finish()
-        ready_units.extend((MT - 1, rc) for rc in range(RC - 1))
-        for n, (m, rc) in enumerate(ready_units):
-            second(m, rc)
-            if n == 0:
-                add_bias()
-                h_quantize(MT - 1)
-            elif (len(ready_units) - n) % GROUP == LEFT or len(ready_units) - n <= LEFT:
-                add_bias()
+                h_turn(turned)
+            first_tile = next_tile
+            for i in range(next_tile, min(RT, next_tile + TURNS[step])):
+                pairs_turn(i)
+                next_tile = i + 1
+            empty_turned()
+            for j, copy in PERMS.get(step, ()):
+                pairs_permute(j, on_vector if copy == "V" else on_scalar)
+            if halves:
                 finish()
+            for rc in range(first_tile // 4, next_tile // 4):
+                pairs_quantize(rc)
+                pairs_from[rc] = step + 2
+            if turned is not None:
+                h_quantize(turned)
+                cell_from[turned] = step + 2
+            step += 1
+        ready_units = ready(99)[:-1]
+        finish()
+        done = 0
+        for n, size in enumerate(CLOSING):
+            for m, rc in ready_units[done : done + size]:
+                second(m, rc)
+            done += size
+            if done == TURN_AFTER:
+                h_turn(MT - 1)
+                empty_turned()
+            add_bias()
+            if done == TURN_AFTER:
+                h_quantize(MT - 1)
+            if done >= TURN_AFTER:
+                finish(False, n < GROUP_S)
+        assert done == len(ready_units)
         second(MT - 1, RC - 1, 0, 256)
         add_bias()
         finish()

@@ -63,7 +63,6 @@ def tile_drug_synergy_bilinear_s4_kernel(
         ident = fixed("ident", [P, P], F32)
         bias_words = fixed("bias_words", [P, 8], F32)
         bias = fixed("bias", [P, R], BF16)
-        warm = fixed("warm", [P, 1], F32)
 
         def clear(engine, plane):
             engine.memset(plane[:].rearrange("p g n -> p (g n)").bitcast(I32), 0)
@@ -269,26 +268,11 @@ def tile_drug_synergy_bilinear_s4_kernel(
                 nc.scalar.activation(out=piece, in_=piece, func=ACT.Sigmoid)
                 nc.sync.dma_start(out=out[P * m : P * (m + 1), lo:hi], in_=piece)
 
-        def warm_up(passes):
-            zeros = c_plane[1][:].rearrange("p g n -> p (g n)")
-            bank = new_bank()
-            for i in range(passes):
-                nc.tensor.matmul_mx(
-                    out=bank[:],
-                    lhsT=zeros[:, 0:256].bitcast(FP4X4),
-                    lhsT_scale=zeros[:, 0:P],
-                    rhs=zeros[:, 0:1024].bitcast(FP4X4),
-                    rhs_scale=zeros[:, 0:512],
-                    start=(i == 0),
-                    stop=(i == passes - 1),
-                )
-
         on_vector, on_scalar = nc.vector.tensor_copy, nc.scalar.copy
 
         clear(nc.vector, c_plane[0])
         clear(nc.vector, b_plane[0])
         clear(nc.vector, c_plane[1])
-        nc.vector.memset(warm[:], 0.0)
         clear(nc.vector, b_plane[1])
         make_identity(nc, ident[:])
         load_bias()
@@ -308,10 +292,7 @@ def tile_drug_synergy_bilinear_s4_kernel(
         load_pairs(1)
         load_pairs(2)
         load_pairs(3)
-        nc.scalar.activation(out=warm[:], in_=warm[:], func=ACT.Sigmoid)
-        warm_up(2)
         spread_bias()
-        warm_up(2)
         load_scales(c_plane, c_scales_v, 1)
         load_codes(c_code, c_words_v, 1, 0)
         load_pairs(4)

@@ -20,20 +20,13 @@ P = 128
 KG = K // 512
 FG = F // 512
 MT = M // P
-RT = R // P
+RJ = R // 256
 RC = R // 512
+ALIGN = 64
 PERM_BUFS = 4
 Z_BUFS = 16
-PIECES = (((0, 1), (1, 2), (2, 4)), ((0, 4),))
-TURNS = [2,2,0,0,0,0]
-UNITS = [4,4,4,4,4,0]
-EARLY_PERMS = {}
-PERMS = {0: ((7, "V"),)}
-CLOSING = (2,1,2,2,1,1)
-HQ_LAST = 1
-JOIN = True
-TURN_AFTER = 3
-GROUP_S = 0
+GROUPED_BUFS = 3
+PIECES = (((0, 1), (1, 4)), ((0, 4),))
 
 
 def tile_drug_synergy_bilinear_s4_kernel(
@@ -43,32 +36,39 @@ def tile_drug_synergy_bilinear_s4_kernel(
     with ExitStack() as ctx:
         keep = ctx.enter_context(tc.tile_pool(name="keep", bufs=1))
         work = ctx.enter_context(tc.tile_pool(name="work", bufs=4))
-        psum = ctx.enter_context(tc.psum_pool(name="psum", bufs=8))
+        psum = ctx.enter_context(tc.psum_pool(name="psum", bufs=1))
         ctx.enter_context(tc.manual_schedule())
 
         def fixed(name, shape, dtype):
-            return keep.tile(shape, dtype, name=name, tag=name, align_bytes=64)
+            return keep.tile(shape, dtype, name=name, tag=name, align_bytes=ALIGN)
 
-        def new_bank():
-            return psum.tile([P, 512], F32, name="bank", tag="bank")
+        free_banks = ["bank%d" % i for i in range(8)]
+        bank_tag = {}
+
+        def new_bank(key):
+            bank_tag[key] = free_banks.pop(0)
+            return psum.tile([P, 512], F32, name=bank_tag[key], tag=bank_tag[key])
+
+        def release(key):
+            free_banks.append(bank_tag[key])
 
         c_plane = [fixed("c_plane%d" % i, [P, KG, 512], U8) for i in range(2)]
         b_plane = [fixed("b_plane%d" % i, [P, KG, 512], U8) for i in range(2)]
         c_code = {(i, lo): fixed("c_code%d%d" % (i, lo), [P, hi - lo, 1024], U8) for i in range(2) for lo, hi in PIECES[i]}
         b_code = {(i, lo): fixed("b_code%d%d" % (i, lo), [P, hi - lo, 1024], U8) for i in range(2) for lo, hi in PIECES[i]}
-        act = [fixed("act%d" % j, [P, 2, F], BF16) for j in range(MT // 2)]
-        raw = [fixed("raw%d" % j, [P, 2, F], BF16) for j in range(RT // 2)]
+        act = [fixed("act%d" % m, [P, F], BF16) for m in range(MT)]
+        raw = [fixed("raw%d" % j, [P, 2 * F], BF16) for j in range(RJ)]
         d_code = [fixed("d_code%d" % rc, [P, FG, 512], U32) for rc in range(RC)]
         d_plane = [fixed("d_plane%d" % rc, [P, FG, 512], U8) for rc in range(RC)]
         ident = fixed("ident", [P, P], F32)
-        bias_words = fixed("bias_words", [P, 8], F32)
         bias = fixed("bias", [P, R], BF16)
+        bias_words = fixed("bias_words", [P, 8], F32)
 
         def clear(engine, plane):
             engine.memset(plane[:].rearrange("p g n -> p (g n)").bitcast(I32), 0)
 
-        pairs_v = pairs.rearrange("(n i p) k -> n p i k", i=2, p=P)
-        act_v = activity.rearrange("(n i p) f -> n p i f", i=2, p=P)
+        pairs_v = pairs.rearrange("(n p i) k -> n p (i k)", i=2, p=P)
+        act_v = activity.rearrange("(m p) f -> m p f", p=P)
         c_scales_v = c_scales.bitcast(I32).rearrange("g (q r) n -> r q g n", r=4)
         b_scales_v = b_scales.bitcast(I32).rearrange("g (q r) n -> r q g n", r=4)
         c_words_v = c_words.bitcast(I32).rearrange("g p n -> p g n")
@@ -77,8 +77,8 @@ def tile_drug_synergy_bilinear_s4_kernel(
         def load_pairs(j):
             nc.sync.dma_start(out=raw[j][:], in_=pairs_v[j])
 
-        def load_act(j):
-            nc.sync.dma_start(out=act[j][:], in_=act_v[j])
+        def load_act(m):
+            nc.sync.dma_start(out=act[m][:], in_=act_v[m])
 
         def load_codes(codes, source, i, piece):
             lo, hi = PIECES[i][piece]
@@ -101,59 +101,46 @@ def tile_drug_synergy_bilinear_s4_kernel(
         def spread_bias():
             spread = bias[:].bitcast(F32).rearrange("q (p h c) -> q h p c", h=2, c=4)
             for half in range(2):
-                bank = new_bank()
+                bank = new_bank(("bias", half))
                 for c in range(4):
                     column = bias_words[:, 4 * half + c : 4 * half + c + 1]
                     nc.tensor.transpose(bank[:, c * P : (c + 1) * P], column.to_broadcast([P, P]), ident[:])
                 nc.scalar.copy(out=spread[:, half], in_=bank[:].rearrange("q (c p) -> q p c", c=4))
+                release(("bias", half))
+
+        on_vector, on_scalar = nc.vector.tensor_copy, nc.scalar.copy
 
         perm = {}
         grouped = {}
+        turned = {}
 
         def pairs_permute(j, copy):
-            perm[j] = work.tile([P, F], F32, name="perm", tag="perm", bufs=PERM_BUFS, align_bytes=64)
+            perm[j] = work.tile([P, F], F32, name="perm", tag="perm", bufs=PERM_BUFS, align_bytes=ALIGN)
             copy(
                 out=perm[j][:].rearrange("p (u n x) -> p u n x", u=2, x=8),
-                in_=raw[j][:].rearrange("p i k -> p (i k)").bitcast(F32).rearrange("p (n u x) -> p u n x", u=2, x=8),
+                in_=raw[j][:].bitcast(F32).rearrange("p (n u x) -> p u n x", u=2, x=8),
             )
 
-        copies = []
-
-        def last_first(items):
-            ordered = items[-1:] + items[:-1]
-            items.clear()
-            return ordered
-
-        def in_order(items):
-            ordered = items[:]
-            items.clear()
-            return ordered
-
-        def empty_turned():
-            ordered = last_first(copies)
-            copies.clear()
-            for target, source in ordered:
-                nc.scalar.copy(out=target, in_=source)
-
-        def pairs_turn(i):
-            j, rc = i // 2, i // 4
-            if i % 4 == 0:
-                grouped[rc] = work.tile([P, FG, 512, 4], BF16, name="grouped", tag="grouped", bufs=2, align_bytes=64)
-            bank = new_bank()
-            for g in range(FG):
+        def pairs_turn(j, g):
+            bank = new_bank(("pairs", j, g))
+            for i in range(2):
                 for u in range(2):
-                    start = 512 * u + 256 * (i % 2) + 128 * g
+                    start = 512 * u + 256 * i + 128 * g
                     nc.tensor.transpose(
-                        bank[:, (2 * g + u) * P : (2 * g + u + 1) * P], perm[j][:, start : start + P], ident[:]
+                        bank[:, (2 * i + u) * P : (2 * i + u + 1) * P], perm[j][:, start : start + P], ident[:]
                     )
-            r0 = 128 * (i % 4)
+            turned[j, g] = bank
+
+        def pairs_empty(j, g, copy):
+            rc = j // 2
+            if rc not in grouped:
+                grouped[rc] = work.tile([P, FG, 512, 4], BF16, name="grouped", tag="grouped", bufs=GROUPED_BUFS, align_bytes=ALIGN)
             words = grouped[rc][:].rearrange("p g r t -> p g (r t)").bitcast(F32)
-            copies.append(
-                (
-                    words[:, :, 2 * r0 : 2 * r0 + 256].rearrange("p g (r u) -> p g r u", u=2),
-                    bank[:].rearrange("p (g u r) -> p g r u", g=FG, u=2),
-                )
+            copy(
+                out=words[:, g, 512 * (j % 2) : 512 * (j % 2 + 1)].rearrange("p (r c) -> p r c", c=4),
+                in_=turned[j, g][:].rearrange("p (c r) -> p r c", c=4),
             )
+            release(("pairs", j, g))
 
         def pairs_quantize(rc):
             nc.vector.quantize_mx(
@@ -173,38 +160,33 @@ def tile_drug_synergy_bilinear_s4_kernel(
                 stop=(g == KG - 1),
             )
 
+        product = {}
         gated = {}
         h_code = {}
         h_plane = {}
+        h_bank = {}
         h_turned = {}
 
-        def gate(bank, m, f):
+        def first(m, f, lo=0, hi=KG):
+            if lo == 0:
+                product[m, f] = new_bank(("first", m, f))
+            for g in range(lo, hi):
+                first_pass(product[m, f], m, f, g)
+
+        def gate(m, f):
             if m not in gated:
-                gated[m] = work.tile([P, F], BF16, name="gated", tag="gated", bufs=4, align_bytes=64)
+                gated[m] = work.tile([P, F], BF16, name="gated", tag="gated", bufs=4, align_bytes=ALIGN)
             half = gated[m][:].rearrange("p (u g n) -> p u g n", u=2, g=FG)[:, :, f, :]
             nc.vector.tensor_tensor(
                 out=half.rearrange("p u (b x) -> p u b x", x=16),
-                in0=bank[:].rearrange("p (b u x) -> p u b x", u=2, x=16),
-                in1=act[m // 2][:, m % 2, 512 * f : 512 * (f + 1)].rearrange("p (b u x) -> p u b x", u=2, x=16),
+                in0=product[m, f][:].rearrange("p (b u x) -> p u b x", u=2, x=16),
+                in1=act[m][:, 512 * f : 512 * (f + 1)].rearrange("p (b u x) -> p u b x", u=2, x=16),
                 op=ALU.mult,
             )
-
-        def first(m, f):
-            bank = new_bank()
-            for g in range(KG):
-                first_pass(bank, m, f, g)
-            gate(bank, m, f)
-
-        def first_four():
-            banks = [new_bank() for m in range(4)]
-            for lo, hi in PIECES[0]:
-                for m in range(4):
-                    for g in range(lo, hi):
-                        first_pass(banks[m], m, 0, g)
-            return banks
+            release(("first", m, f))
 
         def h_turn(m):
-            bank = new_bank()
+            bank = new_bank(("h", m))
             words = gated[m][:].bitcast(F32)
             for g in range(FG):
                 for u in range(2):
@@ -212,27 +194,26 @@ def tile_drug_synergy_bilinear_s4_kernel(
                     nc.tensor.transpose(
                         bank[:, (2 * g + u) * P : (2 * g + u + 1) * P], words[:, start : start + P], ident[:]
                     )
-            h_turned[m] = work.tile([P, 4 * FG * P], BF16, name="h_turned", tag="h_turned", bufs=4, align_bytes=64)
-            copies.append(
-                (
-                    h_turned[m][:].bitcast(F32).rearrange("p (g r u) -> p g r u", g=FG, u=2),
-                    bank[:].rearrange("p (g u r) -> p g r u", g=FG, u=2),
-                )
+            h_bank[m] = bank
+
+        def h_empty(m, copy):
+            h_turned[m] = work.tile([P, 4 * FG * P], BF16, name="h_turned", tag="h_turned", bufs=4, align_bytes=ALIGN)
+            copy(
+                out=h_turned[m][:].bitcast(F32).rearrange("p (g r u) -> p g r u", g=FG, u=2),
+                in_=h_bank[m][:].rearrange("p (g u r) -> p g r u", g=FG, u=2),
             )
+            release(("h", m))
 
         def h_quantize(m):
-            h_code[m] = work.tile([P, FG * P], U32, name="h_code", tag="h_code", bufs=MT, align_bytes=64)
-            h_plane[m] = work.tile([P, FG * P], U8, name="h_plane", tag="h_plane", bufs=MT, align_bytes=64)
+            h_code[m] = work.tile([P, FG * P], U32, name="h_code", tag="h_code", bufs=MT, align_bytes=ALIGN)
+            h_plane[m] = work.tile([P, FG * P], U8, name="h_plane", tag="h_plane", bufs=MT, align_bytes=ALIGN)
             nc.vector.quantize_mx(out=h_code[m][:].bitcast(FP8X4), scales=h_plane[m][:], in_=h_turned[m][:])
 
         z = {}
-        sums = []
-        waiting = []
+        sums = {}
 
         def second(m, rc, lo=0, hi=512):
-            if (m, rc // 2) not in z:
-                z[m, rc // 2] = work.tile([P, 1024], F32, name="z", tag="z", bufs=Z_BUFS, align_bytes=64)
-            bank = new_bank()
+            bank = new_bank(("second", m, rc, lo))
             for g in range(FG):
                 nc.tensor.matmul_mx(
                     out=bank[:, lo:hi],
@@ -243,169 +224,246 @@ def tile_drug_synergy_bilinear_s4_kernel(
                     start=(g == 0),
                     stop=(g == FG - 1),
                 )
-            sums.append((bank, m, 512 * rc + lo, 512 * rc + hi))
+            sums[m, rc, lo] = bank
 
-        def add_bias(covered=False):
-            for bank, m, lo, hi in in_order(sums) if covered else last_first(sums):
-                nc.vector.tensor_tensor(
-                    out=z[m, lo // 1024][:, lo % 1024 : lo % 1024 + hi - lo],
-                    in0=bank[:, lo % 512 : lo % 512 + hi - lo],
-                    in1=bias[:, lo:hi],
-                    op=ALU.add,
-                )
-                waiting.append((m, lo, hi))
+        def add_bias(m, rc, lo=0, hi=512):
+            if (m, rc // 2) not in z:
+                z[m, rc // 2] = work.tile([P, 1024], F32, name="z", tag="z", bufs=Z_BUFS, align_bytes=ALIGN)
+            c0 = 512 * (rc % 2)
+            nc.vector.tensor_tensor(
+                out=z[m, rc // 2][:, c0 + lo : c0 + hi],
+                in0=sums[m, rc, lo][:, lo:hi],
+                in1=bias[:, 512 * rc + lo : 512 * rc + hi],
+                op=ALU.add,
+            )
+            release(("second", m, rc, lo))
 
-        def finish(join=True, grouped_sums=True):
-            joined = []
-            for m, lo, hi in in_order(waiting):
-                mate = [j for j in joined if j[0] == m and j[1] // 1024 == lo // 1024 and (j[2] == lo or j[1] == hi) and join]
-                if mate and hi - lo == 512:
-                    joined.remove(mate[0])
-                    lo, hi = min(lo, mate[0][1]), max(hi, mate[0][2])
-                joined.append((m, lo, hi))
-            for m, lo, hi in last_first(joined) if grouped_sums else joined:
-                piece = z[m, lo // 1024][:, lo % 1024 : lo % 1024 + hi - lo]
-                nc.scalar.activation(out=piece, in_=piece, func=ACT.Sigmoid)
-                nc.sync.dma_start(out=out[P * m : P * (m + 1), lo:hi], in_=piece)
-
-        on_vector, on_scalar = nc.vector.tensor_copy, nc.scalar.copy
+        def finish(m, lo, hi):
+            piece = z[m, lo // 1024][:, lo % 1024 : lo % 1024 + hi - lo]
+            nc.scalar.activation(out=piece, in_=piece, func=ACT.Sigmoid)
+            nc.sync.dma_start(out=out[P * m : P * (m + 1), lo:hi], in_=piece)
 
         clear(nc.vector, c_plane[0])
         clear(nc.vector, b_plane[0])
-        clear(nc.vector, c_plane[1])
         clear(nc.vector, b_plane[1])
+        clear(nc.vector, c_plane[1])
         make_identity(nc, ident[:])
         load_bias()
+        load_pairs(0)
         load_codes(c_code, c_words_v, 0, 0)
         load_codes(b_code, b_words_v, 0, 0)
         load_scales(c_plane, c_scales_v, 0)
         load_scales(b_plane, b_scales_v, 0)
-        load_codes(c_code, c_words_v, 0, 1)
         load_codes(b_code, b_words_v, 0, 1)
-        load_codes(c_code, c_words_v, 0, 2)
-        load_codes(b_code, b_words_v, 0, 2)
-        load_act(0)
+        load_codes(c_code, c_words_v, 0, 1)
         load_scales(b_plane, b_scales_v, 1)
         load_codes(b_code, b_words_v, 1, 0)
-        load_pairs(0)
+        load_act(0)
         load_act(1)
         load_pairs(1)
+        load_act(2)
+        load_act(3)
         load_pairs(2)
         load_pairs(3)
-        spread_bias()
+        load_pairs(4)
         load_scales(c_plane, c_scales_v, 1)
         load_codes(c_code, c_words_v, 1, 0)
-        load_pairs(4)
-        load_act(2)
+        load_act(4)
         load_pairs(5)
+        load_act(5)
         load_pairs(6)
         load_pairs(7)
-        load_act(3)
-
-        def turn(cells, tiles, cells_first=True):
-            for m in cells if cells_first else ():
-                h_turn(m)
-            for i in tiles:
-                pairs_turn(i)
-            for m in () if cells_first else cells:
-                h_turn(m)
-            empty_turned()
-
-        def first_gated(m, f):
-            first(m, f)
-
-        four = first_four()
-        gate(four[0], 0, 0)
-        gate(four[1], 1, 0)
-        pairs_permute(0, on_scalar)
+        load_act(6)
+        load_act(7)
+        pairs_permute(0, on_vector)
+        spread_bias()
+        pairs_turn(0, 0)
+        pairs_empty(0, 0, on_scalar)
+        pairs_turn(0, 1)
+        pairs_empty(0, 1, on_scalar)
+        pairs_permute(1, on_scalar)
+        pairs_permute(2, on_scalar)
+        pairs_permute(3, on_scalar)
+        first(0, 0, 0, 1)
+        first(1, 0, 0, 1)
+        first(2, 0, 0, 1)
+        first(3, 0, 0, 1)
+        first(0, 0, 1)
+        gate(0, 0)
+        first(1, 0, 1)
+        gate(1, 0)
+        first(2, 0, 1)
+        gate(2, 0)
+        first(3, 0, 1)
         first(0, 1)
-        gate(four[2], 2, 0)
+        gate(0, 1)
+        gate(3, 0)
         first(1, 1)
-        pairs_permute(1, on_vector)
-        turn([0], [0, 1])
-        gate(four[3], 3, 0)
+        gate(1, 1)
         first(2, 1)
-        pairs_permute(2, on_vector)
-        pairs_permute(3, on_vector)
-        turn([1], [2, 3])
-        h_quantize(0)
-        pairs_quantize(0)
+        gate(2, 1)
         first(3, 1)
-        h_quantize(1)
-        turn([2], [4, 5, 6, 7])
+        gate(3, 1)
+        pairs_turn(1, 0)
+        pairs_empty(1, 0, on_vector)
         pairs_permute(4, on_vector)
+        pairs_turn(1, 1)
+        pairs_empty(1, 1, on_scalar)
+        pairs_quantize(0)
+        h_turn(0)
+        h_turn(1)
+        h_empty(1, on_scalar)
+        h_empty(0, on_scalar)
+        h_quantize(0)
+        h_quantize(1)
+        pairs_turn(2, 0)
+        pairs_turn(2, 1)
+        h_turn(2)
+        h_turn(3)
+        h_empty(3, on_scalar)
+        h_empty(2, on_scalar)
+        pairs_empty(2, 1, on_scalar)
+        h_quantize(2)
+        h_quantize(3)
+        pairs_empty(2, 0, on_vector)
+        pairs_turn(3, 0)
+        pairs_turn(3, 1)
+        pairs_empty(3, 1, on_scalar)
+        pairs_empty(3, 0, on_scalar)
+        pairs_turn(4, 0)
+        pairs_turn(4, 1)
+        pairs_empty(4, 1, on_scalar)
+        pairs_empty(4, 0, on_scalar)
         pairs_permute(5, on_scalar)
+        pairs_permute(6, on_scalar)
         first(4, 0)
+        gate(4, 0)
+        pairs_quantize(1)
+        pairs_permute(7, on_vector)
+        first(4, 1)
         second(0, 0)
         second(1, 0)
-        add_bias()
-        turn([3], [8, 9])
-        pairs_quantize(1)
-        h_quantize(2)
-        first(4, 1)
-        turn([], [10, 11])
-        finish()
-        h_quantize(3)
-        pairs_permute(6, on_vector)
+        add_bias(1, 0)
+        add_bias(0, 0)
+        gate(4, 1)
+        second(2, 0)
+        second(3, 0)
+        add_bias(3, 0)
+        add_bias(2, 0)
+        first(5, 0)
+        gate(5, 0)
+        pairs_turn(5, 0)
+        pairs_empty(5, 0, on_scalar)
+        pairs_turn(5, 1)
+        pairs_empty(5, 1, on_scalar)
         pairs_quantize(2)
-        halves = [(m, f) for m in range(5, MT) for f in range(FG)]
-        to_turn = [4]
-        cell_from, pairs_from, multiplied = {0: 0, 1: 0, 2: 0, 3: 1, MT - 1: 99}, {0: 0, 1: 0, 2: 1}, [(0, 0), (1, 0)]
-        step = 0
-        next_tile = 12
-        def ready(step):
-            units = [(max(s, t), m, rc) for m, s in cell_from.items() for rc, t in pairs_from.items()]
-            return [(m, rc) for s, m, rc in sorted(units) if s <= step and (m, rc) not in multiplied]
-
-        while halves:
-            for m, rc in ready(step)[:UNITS[step]]:
-                second(m, rc)
-                multiplied.append((m, rc))
-            add_bias()
-            turned = to_turn.pop(0) if to_turn else None
-            for j, copy in EARLY_PERMS.get(step, ()):
-                pairs_permute(j, on_vector if copy == "V" else on_scalar)
-            m, f = halves.pop(0)
-            first(m, f)
-            if f == FG - 1:
-                to_turn.append(m)
-            if turned is not None:
-                h_turn(turned)
-            first_tile = next_tile
-            for i in range(next_tile, min(RT, next_tile + TURNS[step])):
-                pairs_turn(i)
-                next_tile = i + 1
-            empty_turned()
-            for j, copy in PERMS.get(step, ()):
-                pairs_permute(j, on_vector if copy == "V" else on_scalar)
-            if halves:
-                finish()
-            for rc in range(first_tile // 4, next_tile // 4):
-                pairs_quantize(rc)
-                pairs_from[rc] = step + 2
-            if turned is not None:
-                h_quantize(turned)
-                cell_from[turned] = step + 2
-            step += 1
-        ready_units = ready(99)[:-1]
-        finish()
-        done = 0
-        for n, size in enumerate(CLOSING):
-            for m, rc in ready_units[done : done + size]:
-                second(m, rc)
-            done += size
-            if done == TURN_AFTER:
-                h_turn(MT - 1)
-                empty_turned()
-            add_bias()
-            if done == TURN_AFTER:
-                h_quantize(MT - 1)
-            if done >= TURN_AFTER:
-                finish(False, n < GROUP_S)
-        assert done == len(ready_units)
-        second(MT - 1, RC - 1, 0, 256)
-        add_bias()
-        finish()
-        second(MT - 1, RC - 1, 256, 512)
-        add_bias()
-        finish()
+        h_turn(4)
+        pairs_turn(6, 0)
+        pairs_empty(6, 0, on_scalar)
+        h_empty(4, on_scalar)
+        h_quantize(4)
+        pairs_turn(6, 1)
+        pairs_empty(6, 1, on_scalar)
+        pairs_turn(7, 0)
+        pairs_turn(7, 1)
+        pairs_empty(7, 1, on_scalar)
+        pairs_empty(7, 0, on_scalar)
+        second(0, 1)
+        second(1, 1)
+        add_bias(1, 1)
+        add_bias(0, 1)
+        second(2, 1)
+        finish(0, 0, 1024)
+        finish(1, 0, 1024)
+        second(3, 1)
+        add_bias(3, 1)
+        add_bias(2, 1)
+        pairs_quantize(3)
+        first(5, 1)
+        finish(2, 0, 1024)
+        gate(5, 1)
+        second(4, 0)
+        second(4, 1)
+        add_bias(4, 1)
+        add_bias(4, 0)
+        second(0, 2)
+        second(1, 2)
+        add_bias(1, 2)
+        add_bias(0, 2)
+        second(0, 3)
+        second(1, 3)
+        add_bias(1, 3)
+        add_bias(0, 3)
+        h_turn(5)
+        h_empty(5, on_scalar)
+        finish(3, 0, 1024)
+        finish(4, 0, 1024)
+        finish(0, 1024, 2048)
+        finish(1, 1024, 2048)
+        h_quantize(5)
+        second(2, 2)
+        second(2, 3)
+        add_bias(2, 3)
+        add_bias(2, 2)
+        second(3, 2)
+        finish(2, 1024, 2048)
+        first(6, 0)
+        gate(6, 0)
+        add_bias(3, 2)
+        second(3, 3)
+        first(6, 1)
+        gate(6, 1)
+        add_bias(3, 3)
+        second(4, 2)
+        second(4, 3)
+        add_bias(4, 3)
+        add_bias(4, 2)
+        second(5, 0)
+        add_bias(5, 0)
+        h_turn(6)
+        h_empty(6, on_scalar)
+        finish(3, 1024, 2048)
+        finish(4, 1024, 2048)
+        first(7, 0)
+        gate(7, 0)
+        second(5, 1)
+        add_bias(5, 1)
+        first(7, 1)
+        finish(5, 0, 1024)
+        gate(7, 1)
+        h_quantize(6)
+        second(5, 2)
+        second(5, 3)
+        add_bias(5, 3)
+        add_bias(5, 2)
+        h_turn(7)
+        h_empty(7, on_scalar)
+        finish(5, 1024, 2048)
+        second(6, 0)
+        add_bias(6, 0)
+        h_quantize(7)
+        second(6, 1)
+        finish(6, 0, 512)
+        second(6, 2)
+        add_bias(6, 2)
+        add_bias(6, 1)
+        second(6, 3)
+        finish(6, 1024, 1536)
+        finish(6, 512, 1024)
+        add_bias(6, 3)
+        second(7, 0)
+        finish(6, 1536, 2048)
+        second(7, 1)
+        add_bias(7, 1)
+        add_bias(7, 0)
+        second(7, 2)
+        finish(7, 512, 1024)
+        finish(7, 0, 512)
+        add_bias(7, 2)
+        second(7, 3, 0, 256)
+        finish(7, 1024, 1536)
+        add_bias(7, 3, 0, 256)
+        second(7, 3, 256, 512)
+        finish(7, 1536, 1792)
+        add_bias(7, 3, 256, 512)
+        finish(7, 1792, 2048)

@@ -26,7 +26,7 @@ ALIGN = 64
 PERM_BUFS = 4
 Z_BUFS = 16
 GROUPED_BUFS = 3
-PIECES = (((0, 1), (1, 4)), ((0, 4),))
+PIECES = (((0, 1), (1, 2), (2, 4)), ((0, 4),))
 
 
 def tile_drug_synergy_bilinear_s4_kernel(
@@ -62,7 +62,9 @@ def tile_drug_synergy_bilinear_s4_kernel(
         d_plane = [fixed("d_plane%d" % rc, [P, FG, 512], U8) for rc in range(RC)]
         ident = fixed("ident", [P, P], F32)
         bias = fixed("bias", [P, R], BF16)
-        bias_words = fixed("bias_words", [P, 8], F32)
+        bias_rows = fixed("bias_rows", [P, 32], F32)
+        bias_wide = fixed("bias_wide", [P, 32, 32], F32)
+        bias_turned = fixed("bias_turned", [P, 32, 32], F32)
 
         def clear(engine, plane):
             engine.memset(plane[:].rearrange("p g n -> p (g n)").bitcast(I32), 0)
@@ -96,17 +98,25 @@ def tile_drug_synergy_bilinear_s4_kernel(
                 )
 
         def load_bias():
-            nc.sync.dma_start(out=bias_words[:].bitcast(BF16), in_=pair_bias.rearrange("(p n) -> p n", p=P))
+            for q in range(4):
+                nc.sync.dma_start(
+                    out=bias_rows[32 * q : 32 * (q + 1)].bitcast(BF16).rearrange("y (c e) -> y c e", e=8),
+                    in_=pair_bias.rearrange("(c y e) -> y c e", y=32, e=8),
+                )
 
-        def spread_bias():
-            spread = bias[:].bitcast(F32).rearrange("q (p h c) -> q h p c", h=2, c=4)
-            for half in range(2):
-                bank = new_bank(("bias", half))
-                for c in range(4):
-                    column = bias_words[:, 4 * half + c : 4 * half + c + 1]
-                    nc.tensor.transpose(bank[:, c * P : (c + 1) * P], column.to_broadcast([P, P]), ident[:])
-                nc.scalar.copy(out=spread[:, half], in_=bank[:].rearrange("q (c p) -> q p c", c=4))
-                release(("bias", half))
+        def bias_widen():
+            nc.scalar.copy(out=bias_wide[:], in_=bias_rows[:].unsqueeze(2).to_broadcast([P, 32, 32]))
+
+        def bias_turn():
+            nc.vector.transpose(
+                out=bias_turned[:].rearrange("p c y -> p (c y)"), in_=bias_wide[:].rearrange("p c x -> p (c x)")
+            )
+
+        def bias_order():
+            nc.scalar.copy(
+                out=bias[:].bitcast(F32).rearrange("p (c y e) -> p c y e", y=32, e=4),
+                in_=bias_turned[:].rearrange("p (c e) y -> p c y e", e=4),
+            )
 
         on_vector, on_scalar = nc.vector.tensor_copy, nc.scalar.copy
 
@@ -243,202 +253,219 @@ def tile_drug_synergy_bilinear_s4_kernel(
             nc.scalar.activation(out=piece, in_=piece, func=ACT.Sigmoid)
             nc.sync.dma_start(out=out[P * m : P * (m + 1), lo:hi], in_=piece)
 
+        clear(nc.gpsimd, b_plane[0])
         clear(nc.vector, c_plane[0])
-        clear(nc.vector, b_plane[0])
         clear(nc.vector, b_plane[1])
         clear(nc.vector, c_plane[1])
         make_identity(nc, ident[:])
-        load_bias()
-        load_pairs(0)
         load_codes(c_code, c_words_v, 0, 0)
         load_codes(b_code, b_words_v, 0, 0)
         load_scales(c_plane, c_scales_v, 0)
         load_scales(b_plane, b_scales_v, 0)
-        load_codes(b_code, b_words_v, 0, 1)
         load_codes(c_code, c_words_v, 0, 1)
+        load_codes(b_code, b_words_v, 0, 1)
+        load_codes(c_code, c_words_v, 0, 2)
+        load_codes(b_code, b_words_v, 0, 2)
         load_scales(b_plane, b_scales_v, 1)
         load_codes(b_code, b_words_v, 1, 0)
+        load_bias()
         load_act(0)
         load_act(1)
-        load_pairs(1)
         load_act(2)
+        load_pairs(0)
         load_act(3)
+        load_pairs(1)
         load_pairs(2)
         load_pairs(3)
-        load_pairs(4)
         load_scales(c_plane, c_scales_v, 1)
         load_codes(c_code, c_words_v, 1, 0)
         load_act(4)
+        load_pairs(4)
         load_pairs(5)
         load_act(5)
         load_pairs(6)
         load_pairs(7)
         load_act(6)
         load_act(7)
-        pairs_permute(0, on_vector)
-        spread_bias()
-        pairs_turn(0, 0)
-        pairs_empty(0, 0, on_scalar)
-        pairs_turn(0, 1)
-        pairs_empty(0, 1, on_scalar)
-        pairs_permute(1, on_scalar)
-        pairs_permute(2, on_scalar)
-        pairs_permute(3, on_scalar)
+        bias_widen()
         first(0, 0, 0, 1)
         first(1, 0, 0, 1)
         first(2, 0, 0, 1)
         first(3, 0, 0, 1)
-        first(0, 0, 1)
+        first(0, 0, 1, 2)
+        first(1, 0, 1, 2)
+        first(2, 0, 1, 2)
+        first(3, 0, 1, 2)
+        first(0, 0, 2)
         gate(0, 0)
-        first(1, 0, 1)
+        bias_turn()
+        first(1, 0, 2)
+        bias_order()
+        pairs_permute(0, on_scalar)
+        pairs_permute(1, on_scalar)
         gate(1, 0)
-        first(2, 0, 1)
-        gate(2, 0)
-        first(3, 0, 1)
+        first(2, 0, 2)
+        first(3, 0, 2)
         first(0, 1)
         gate(0, 1)
-        gate(3, 0)
+        gate(2, 0)
         first(1, 1)
         gate(1, 1)
+        gate(3, 0)
         first(2, 1)
         gate(2, 1)
         first(3, 1)
         gate(3, 1)
-        pairs_turn(1, 0)
-        pairs_empty(1, 0, on_vector)
-        pairs_permute(4, on_vector)
-        pairs_turn(1, 1)
-        pairs_empty(1, 1, on_scalar)
-        pairs_quantize(0)
+        pairs_permute(2, on_vector)
+        pairs_turn(0, 0)
+        pairs_empty(0, 0, on_scalar)
+        pairs_turn(0, 1)
+        pairs_empty(0, 1, on_scalar)
         h_turn(0)
+        h_empty(0, on_vector)
+        pairs_permute(3, on_vector)
         h_turn(1)
         h_empty(1, on_scalar)
-        h_empty(0, on_scalar)
+        pairs_turn(1, 0)
+        pairs_empty(1, 0, on_scalar)
+        pairs_turn(1, 1)
+        pairs_empty(1, 1, on_vector)
         h_quantize(0)
+        pairs_quantize(0)
         h_quantize(1)
-        pairs_turn(2, 0)
-        pairs_turn(2, 1)
         h_turn(2)
         h_turn(3)
         h_empty(3, on_scalar)
         h_empty(2, on_scalar)
-        pairs_empty(2, 1, on_scalar)
         h_quantize(2)
         h_quantize(3)
-        pairs_empty(2, 0, on_vector)
+        pairs_turn(2, 0)
+        pairs_turn(2, 1)
+        pairs_empty(2, 1, on_scalar)
+        pairs_empty(2, 0, on_scalar)
         pairs_turn(3, 0)
         pairs_turn(3, 1)
         pairs_empty(3, 1, on_scalar)
         pairs_empty(3, 0, on_scalar)
-        pairs_turn(4, 0)
-        pairs_turn(4, 1)
-        pairs_empty(4, 1, on_scalar)
-        pairs_empty(4, 0, on_scalar)
+        pairs_permute(4, on_scalar)
         pairs_permute(5, on_scalar)
-        pairs_permute(6, on_scalar)
         first(4, 0)
         gate(4, 0)
         pairs_quantize(1)
-        pairs_permute(7, on_vector)
         first(4, 1)
+        gate(4, 1)
         second(0, 0)
         second(1, 0)
         add_bias(1, 0)
         add_bias(0, 0)
-        gate(4, 1)
         second(2, 0)
+        finish(0, 0, 512)
         second(3, 0)
         add_bias(3, 0)
         add_bias(2, 0)
         first(5, 0)
         gate(5, 0)
+        pairs_permute(6, on_vector)
+        pairs_turn(4, 0)
+        pairs_turn(4, 1)
+        pairs_empty(4, 1, on_scalar)
+        pairs_empty(4, 0, on_scalar)
+        h_turn(4)
+        h_empty(4, on_scalar)
         pairs_turn(5, 0)
-        pairs_empty(5, 0, on_scalar)
         pairs_turn(5, 1)
         pairs_empty(5, 1, on_scalar)
-        pairs_quantize(2)
-        h_turn(4)
-        pairs_turn(6, 0)
-        pairs_empty(6, 0, on_scalar)
-        h_empty(4, on_scalar)
-        h_quantize(4)
-        pairs_turn(6, 1)
-        pairs_empty(6, 1, on_scalar)
-        pairs_turn(7, 0)
-        pairs_turn(7, 1)
-        pairs_empty(7, 1, on_scalar)
-        pairs_empty(7, 0, on_scalar)
+        pairs_empty(5, 0, on_scalar)
+        pairs_permute(7, on_scalar)
+        finish(1, 0, 512)
         second(0, 1)
         second(1, 1)
         add_bias(1, 1)
         add_bias(0, 1)
+        h_quantize(4)
+        pairs_quantize(2)
         second(2, 1)
-        finish(0, 0, 1024)
-        finish(1, 0, 1024)
+        finish(0, 512, 1024)
+        finish(1, 512, 1024)
         second(3, 1)
+        first(5, 1)
+        gate(5, 1)
         add_bias(3, 1)
         add_bias(2, 1)
-        pairs_quantize(3)
-        first(5, 1)
-        finish(2, 0, 1024)
-        gate(5, 1)
         second(4, 0)
         second(4, 1)
         add_bias(4, 1)
         add_bias(4, 0)
+        pairs_turn(6, 0)
+        pairs_turn(6, 1)
+        pairs_empty(6, 1, on_scalar)
+        pairs_empty(6, 0, on_scalar)
+        pairs_turn(7, 0)
+        pairs_turn(7, 1)
+        pairs_empty(7, 1, on_scalar)
+        pairs_empty(7, 0, on_scalar)
+        h_turn(5)
+        h_empty(5, on_scalar)
+        finish(2, 0, 1024)
+        finish(3, 0, 1024)
+        finish(4, 0, 1024)
         second(0, 2)
         second(1, 2)
         add_bias(1, 2)
         add_bias(0, 2)
-        second(0, 3)
-        second(1, 3)
-        add_bias(1, 3)
-        add_bias(0, 3)
-        h_turn(5)
-        h_empty(5, on_scalar)
-        finish(3, 0, 1024)
-        finish(4, 0, 1024)
-        finish(0, 1024, 2048)
-        finish(1, 1024, 2048)
         h_quantize(5)
+        pairs_quantize(3)
         second(2, 2)
-        second(2, 3)
-        add_bias(2, 3)
-        add_bias(2, 2)
+        finish(1, 1024, 1536)
+        finish(0, 1024, 1536)
         second(3, 2)
-        finish(2, 1024, 2048)
         first(6, 0)
         gate(6, 0)
         add_bias(3, 2)
-        second(3, 3)
-        first(6, 1)
-        gate(6, 1)
-        add_bias(3, 3)
+        add_bias(2, 2)
         second(4, 2)
-        second(4, 3)
-        add_bias(4, 3)
-        add_bias(4, 2)
+        finish(3, 1024, 1536)
+        finish(2, 1024, 1536)
         second(5, 0)
         add_bias(5, 0)
+        add_bias(4, 2)
+        second(0, 3)
+        finish(5, 0, 512)
+        first(6, 1)
+        gate(6, 1)
+        add_bias(0, 3)
+        second(1, 3)
+        second(2, 3)
+        add_bias(2, 3)
+        add_bias(1, 3)
+        second(3, 3)
+        add_bias(3, 3)
         h_turn(6)
         h_empty(6, on_scalar)
-        finish(3, 1024, 2048)
-        finish(4, 1024, 2048)
+        finish(4, 1024, 1536)
+        finish(0, 1536, 2048)
+        finish(2, 1536, 2048)
+        finish(1, 1536, 2048)
+        finish(3, 1536, 2048)
+        h_quantize(6)
+        second(4, 3)
+        add_bias(4, 3)
         first(7, 0)
+        finish(4, 1536, 2048)
         gate(7, 0)
         second(5, 1)
         add_bias(5, 1)
         first(7, 1)
-        finish(5, 0, 1024)
+        finish(5, 512, 1024)
         gate(7, 1)
-        h_quantize(6)
         second(5, 2)
+        add_bias(5, 2)
         second(5, 3)
         add_bias(5, 3)
-        add_bias(5, 2)
         h_turn(7)
         h_empty(7, on_scalar)
-        finish(5, 1024, 2048)
+        finish(5, 1024, 1536)
+        finish(5, 1536, 2048)
         second(6, 0)
         add_bias(6, 0)
         h_quantize(7)
@@ -450,20 +477,20 @@ def tile_drug_synergy_bilinear_s4_kernel(
         second(6, 3)
         finish(6, 1024, 1536)
         finish(6, 512, 1024)
-        add_bias(6, 3)
         second(7, 0)
-        finish(6, 1536, 2048)
-        second(7, 1)
-        add_bias(7, 1)
         add_bias(7, 0)
-        second(7, 2)
-        finish(7, 512, 1024)
+        add_bias(6, 3)
+        second(7, 1)
         finish(7, 0, 512)
+        finish(6, 1536, 2048)
+        second(7, 2)
         add_bias(7, 2)
+        add_bias(7, 1)
         second(7, 3, 0, 256)
         finish(7, 1024, 1536)
-        add_bias(7, 3, 0, 256)
+        finish(7, 512, 1024)
         second(7, 3, 256, 512)
-        finish(7, 1536, 1792)
         add_bias(7, 3, 256, 512)
+        add_bias(7, 3, 0, 256)
         finish(7, 1792, 2048)
+        finish(7, 1536, 1792)

@@ -62,9 +62,7 @@ def tile_drug_synergy_bilinear_s4_kernel(
         d_plane = [fixed("d_plane%d" % rc, [P, FG, 512], U8) for rc in range(RC)]
         ident = fixed("ident", [P, P], F32)
         bias = fixed("bias", [P, R], BF16)
-        bias_rows = fixed("bias_rows", [P, 32], F32)
-        bias_wide = fixed("bias_wide", [P, 32, 32], F32)
-        bias_turned = fixed("bias_turned", [P, 32, 32], F32)
+        bias_words = fixed("bias_words", [P, 8], F32)
 
         def clear(engine, plane):
             engine.memset(plane[:].rearrange("p g n -> p (g n)").bitcast(I32), 0)
@@ -98,25 +96,17 @@ def tile_drug_synergy_bilinear_s4_kernel(
                 )
 
         def load_bias():
-            for q in range(4):
-                nc.sync.dma_start(
-                    out=bias_rows[32 * q : 32 * (q + 1)].bitcast(BF16).rearrange("y (c e) -> y c e", e=8),
-                    in_=pair_bias.rearrange("(c y e) -> y c e", y=32, e=8),
-                )
+            nc.sync.dma_start(out=bias_words[:].bitcast(BF16), in_=pair_bias.rearrange("(p n) -> p n", p=P))
 
-        def bias_widen():
-            nc.scalar.copy(out=bias_wide[:], in_=bias_rows[:].unsqueeze(2).to_broadcast([P, 32, 32]))
-
-        def bias_turn():
-            nc.vector.transpose(
-                out=bias_turned[:].rearrange("p c y -> p (c y)"), in_=bias_wide[:].rearrange("p c x -> p (c x)")
-            )
-
-        def bias_order():
-            nc.scalar.copy(
-                out=bias[:].bitcast(F32).rearrange("p (c y e) -> p c y e", y=32, e=4),
-                in_=bias_turned[:].rearrange("p (c e) y -> p c y e", e=4),
-            )
+        def spread_bias():
+            spread = bias[:].bitcast(F32).rearrange("q (p h c) -> q h p c", h=2, c=4)
+            for half in range(2):
+                bank = new_bank(("bias", half))
+                for c in range(4):
+                    column = bias_words[:, 4 * half + c : 4 * half + c + 1]
+                    nc.tensor.transpose(bank[:, c * P : (c + 1) * P], column.to_broadcast([P, P]), ident[:])
+                nc.scalar.copy(out=spread[:, half], in_=bank[:].rearrange("q (c p) -> q p c", c=4))
+                release(("bias", half))
 
         on_vector, on_scalar = nc.vector.tensor_copy, nc.scalar.copy
 
@@ -253,11 +243,12 @@ def tile_drug_synergy_bilinear_s4_kernel(
             nc.scalar.activation(out=piece, in_=piece, func=ACT.Sigmoid)
             nc.sync.dma_start(out=out[P * m : P * (m + 1), lo:hi], in_=piece)
 
-        clear(nc.gpsimd, b_plane[0])
         clear(nc.vector, c_plane[0])
+        clear(nc.vector, b_plane[0])
         clear(nc.vector, b_plane[1])
         clear(nc.vector, c_plane[1])
         make_identity(nc, ident[:])
+        load_bias()
         load_codes(c_code, c_words_v, 0, 0)
         load_codes(b_code, b_words_v, 0, 0)
         load_scales(c_plane, c_scales_v, 0)
@@ -268,7 +259,6 @@ def tile_drug_synergy_bilinear_s4_kernel(
         load_codes(b_code, b_words_v, 0, 2)
         load_scales(b_plane, b_scales_v, 1)
         load_codes(b_code, b_words_v, 1, 0)
-        load_bias()
         load_act(0)
         load_act(1)
         load_act(2)
@@ -287,7 +277,9 @@ def tile_drug_synergy_bilinear_s4_kernel(
         load_pairs(7)
         load_act(6)
         load_act(7)
-        bias_widen()
+        spread_bias()
+        pairs_permute(0, on_scalar)
+        pairs_permute(1, on_scalar)
         first(0, 0, 0, 1)
         first(1, 0, 0, 1)
         first(2, 0, 0, 1)
@@ -298,11 +290,7 @@ def tile_drug_synergy_bilinear_s4_kernel(
         first(3, 0, 1, 2)
         first(0, 0, 2)
         gate(0, 0)
-        bias_turn()
         first(1, 0, 2)
-        bias_order()
-        pairs_permute(0, on_scalar)
-        pairs_permute(1, on_scalar)
         gate(1, 0)
         first(2, 0, 2)
         first(3, 0, 2)

@@ -17,15 +17,13 @@ ACT = mybir.ActivationFunctionType
 ALU = mybir.AluOpType
 
 P = 128
-KG = K // 512
-FG = F // 512
-MT = M // P
-RJ = R // 256
-RC = R // 512
+BANK = 512
+GENE_PASSES = K // BANK
+FEATURE_PASSES = F // BANK
+CELL_TILES = M // P
+LOADS = R // (2 * P)
+QUARTERS = R // BANK
 ALIGN = 64
-PERM_BUFS = 4
-Z_BUFS = 16
-GROUPED_BUFS = 3
 PIECES = (((0, 1), (1, 2), (2, 4)), ((0, 4),))
 
 
@@ -42,32 +40,38 @@ def tile_drug_synergy_bilinear_s4_kernel(
         def fixed(name, shape, dtype):
             return keep.tile(shape, dtype, name=name, tag=name, align_bytes=ALIGN)
 
+        def rotating(name, shape, dtype, bufs):
+            return work.tile(shape, dtype, name=name, tag=name, bufs=bufs, align_bytes=ALIGN)
+
         free_banks = ["bank%d" % i for i in range(8)]
-        bank_tag = {}
+        bank_name = {}
+        bank_tile = {}
 
-        def new_bank(key):
-            bank_tag[key] = free_banks.pop(0)
-            return psum.tile([P, 512], F32, name=bank_tag[key], tag=bank_tag[key])
+        def take_bank(key):
+            bank_name[key] = free_banks.pop(0)
+            bank_tile[key] = psum.tile([P, BANK], F32, name=bank_name[key], tag=bank_name[key])
+            return bank_tile[key]
 
-        def release(key):
-            free_banks.append(bank_tag[key])
+        def release_bank(key):
+            free_banks.append(bank_name[key])
 
-        c_plane = [fixed("c_plane%d" % i, [P, KG, 512], U8) for i in range(2)]
-        b_plane = [fixed("b_plane%d" % i, [P, KG, 512], U8) for i in range(2)]
-        c_code = {(i, lo): fixed("c_code%d%d" % (i, lo), [P, hi - lo, 1024], U8) for i in range(2) for lo, hi in PIECES[i]}
-        b_code = {(i, lo): fixed("b_code%d%d" % (i, lo), [P, hi - lo, 1024], U8) for i in range(2) for lo, hi in PIECES[i]}
-        act = [fixed("act%d" % m, [P, F], BF16) for m in range(MT)]
-        raw = [fixed("raw%d" % j, [P, 2 * F], BF16) for j in range(RJ)]
-        d_code = [fixed("d_code%d" % rc, [P, FG, 512], U32) for rc in range(RC)]
-        d_plane = [fixed("d_plane%d" % rc, [P, FG, 512], U8) for rc in range(RC)]
+        c_scale = [fixed("c_scale%d" % half, [P, GENE_PASSES, BANK], U8) for half in range(2)]
+        b_scale = [fixed("b_scale%d" % half, [P, GENE_PASSES, BANK], U8) for half in range(2)]
+        c_code = {}
+        b_code = {}
+        for name, codes in (("c_code", c_code), ("b_code", b_code)):
+            for half in range(2):
+                for lo, hi in PIECES[half]:
+                    codes[half, lo] = fixed("%s%d%d" % (name, half, lo), [P, hi - lo, 2 * BANK], U8)
+        act = [fixed("act%d" % m, [P, F], BF16) for m in range(CELL_TILES)]
+        raw = [fixed("raw%d" % j, [P, 2 * F], BF16) for j in range(LOADS)]
+        d_code = [fixed("d_code%d" % q, [P, FEATURE_PASSES, BANK], U32) for q in range(QUARTERS)]
+        d_scale = [fixed("d_scale%d" % q, [P, FEATURE_PASSES, BANK], U8) for q in range(QUARTERS)]
         ident = fixed("ident", [P, P], F32)
         bias = fixed("bias", [P, R], BF16)
         bias_words = fixed("bias_words", [P, 8], F32)
 
-        def clear(engine, plane):
-            engine.memset(plane[:].rearrange("p g n -> p (g n)").bitcast(I32), 0)
-
-        pairs_v = pairs.rearrange("(n p i) k -> n p (i k)", i=2, p=P)
+        pairs_v = pairs.rearrange("(j p i) k -> j p (i k)", i=2, p=P)
         act_v = activity.rearrange("(m p) f -> m p f", p=P)
         c_scales_v = c_scales.bitcast(I32).rearrange("g (q r) n -> r q g n", r=4)
         b_scales_v = b_scales.bitcast(I32).rearrange("g (q r) n -> r q g n", r=4)
@@ -80,405 +84,345 @@ def tile_drug_synergy_bilinear_s4_kernel(
         def load_act(m):
             nc.sync.dma_start(out=act[m][:], in_=act_v[m])
 
-        def load_codes(codes, source, i, piece):
-            lo, hi = PIECES[i][piece]
-            nc.sync.dma_start(out=codes[i, lo][:].bitcast(I32), in_=source[:, lo:hi, 256 * i : 256 * (i + 1)])
+        def load_codes(codes, source, half, piece):
+            lo, hi = PIECES[half][piece]
+            nc.sync.dma_start(out=codes[half, lo][:].bitcast(I32), in_=source[:, lo:hi, 256 * half : 256 * (half + 1)])
 
-        def codes_of(codes, i, g):
-            lo = max(first_g for first_g, end_g in PIECES[i] if first_g <= g)
-            return codes[i, lo][:, g - lo]
+        def codes_of(codes, half, g):
+            lo = max(first_g for first_g, end_g in PIECES[half] if first_g <= g)
+            return codes[half, lo][:, g - lo]
 
-        def load_scales(plane, source, i):
+        def load_scales(scale, source, half):
             for r in range(4):
                 nc.sync.dma_start(
-                    out=plane[i][r:P:32].bitcast(I32),
-                    in_=source[r, :, :, 128 * i : 128 * (i + 1)],
+                    out=scale[half][r:P:32].bitcast(I32), in_=source[r, :, :, 128 * half : 128 * (half + 1)]
                 )
 
-        def load_bias():
-            nc.sync.dma_start(out=bias_words[:].bitcast(BF16), in_=pair_bias.rearrange("(p n) -> p n", p=P))
+        def spread_bias(half):
+            bank = take_bank(("bias", half))
+            for c in range(4):
+                column = bias_words[:, 4 * half + c : 4 * half + c + 1]
+                nc.tensor.transpose(bank[:, c * P : (c + 1) * P], column.to_broadcast([P, P]), ident[:])
+            spread = bias[:].bitcast(F32).rearrange("x (p h c) -> x h p c", h=2, c=4)
+            nc.scalar.copy(out=spread[:, half], in_=bank[:].rearrange("x (c p) -> x p c", c=4))
+            release_bank(("bias", half))
 
-        def spread_bias():
-            spread = bias[:].bitcast(F32).rearrange("q (p h c) -> q h p c", h=2, c=4)
-            for half in range(2):
-                bank = new_bank(("bias", half))
-                for c in range(4):
-                    column = bias_words[:, 4 * half + c : 4 * half + c + 1]
-                    nc.tensor.transpose(bank[:, c * P : (c + 1) * P], column.to_broadcast([P, P]), ident[:])
-                nc.scalar.copy(out=spread[:, half], in_=bank[:].rearrange("q (c p) -> q p c", c=4))
-                release(("bias", half))
+        def warm_up_tensor():
+            bank = take_bank("warm-up")
+            nc.tensor.matmul_mx(
+                out=bank[:],
+                lhsT=c_code[0, 0][:, 0, 0:256].bitcast(FP4X4),
+                lhsT_scale=c_scale[1][:, 0, 0:P],
+                rhs=c_code[0, 0][:, 0].bitcast(FP4X4),
+                rhs_scale=c_scale[1][:, 0, :],
+                start=True,
+                stop=True,
+            )
+            release_bank("warm-up")
 
         on_vector, on_scalar = nc.vector.tensor_copy, nc.scalar.copy
 
-        perm = {}
+        sorted_pairs = {}
         grouped = {}
-        turned = {}
 
-        def pairs_permute(j, copy):
-            perm[j] = work.tile([P, F], F32, name="perm", tag="perm", bufs=PERM_BUFS, align_bytes=ALIGN)
+        def pairs_sort(j, copy):
+            sorted_pairs[j] = rotating("sorted_pairs", [P, F], F32, 4)
             copy(
-                out=perm[j][:].rearrange("p (u n x) -> p u n x", u=2, x=8),
+                out=sorted_pairs[j][:].rearrange("p (u n x) -> p u n x", u=2, x=8),
                 in_=raw[j][:].bitcast(F32).rearrange("p (n u x) -> p u n x", u=2, x=8),
             )
 
         def pairs_turn(j, g):
-            bank = new_bank(("pairs", j, g))
+            bank = take_bank(("pairs", j, g))
             for i in range(2):
                 for u in range(2):
                     start = 512 * u + 256 * i + 128 * g
                     nc.tensor.transpose(
-                        bank[:, (2 * i + u) * P : (2 * i + u + 1) * P], perm[j][:, start : start + P], ident[:]
+                        bank[:, (2 * i + u) * P : (2 * i + u + 1) * P], sorted_pairs[j][:, start : start + P], ident[:]
                     )
-            turned[j, g] = bank
 
         def pairs_empty(j, g, copy):
-            rc = j // 2
-            if rc not in grouped:
-                grouped[rc] = work.tile([P, FG, 512, 4], BF16, name="grouped", tag="grouped", bufs=GROUPED_BUFS, align_bytes=ALIGN)
-            words = grouped[rc][:].rearrange("p g r t -> p g (r t)").bitcast(F32)
+            if j // 2 not in grouped:
+                grouped[j // 2] = rotating("grouped", [P, FEATURE_PASSES, 4 * BANK], BF16, 3)
+            words = grouped[j // 2][:].bitcast(F32)
             copy(
                 out=words[:, g, 512 * (j % 2) : 512 * (j % 2 + 1)].rearrange("p (r c) -> p r c", c=4),
-                in_=turned[j, g][:].rearrange("p (c r) -> p r c", c=4),
+                in_=bank_tile["pairs", j, g][:].rearrange("p (c r) -> p r c", c=4),
             )
-            release(("pairs", j, g))
+            release_bank(("pairs", j, g))
 
-        def pairs_quantize(rc):
+        def pairs_quantize(q):
             nc.vector.quantize_mx(
-                out=d_code[rc][:].rearrange("p g r -> p (g r)").bitcast(FP8X4),
-                scales=d_plane[rc][:].rearrange("p g r -> p (g r)"),
-                in_=grouped[rc][:].rearrange("p g r t -> p (g r t)"),
+                out=d_code[q][:].rearrange("p g r -> p (g r)").bitcast(FP8X4),
+                scales=d_scale[q][:].rearrange("p g r -> p (g r)"),
+                in_=grouped[q][:].rearrange("p g n -> p (g n)"),
             )
 
-        def first_pass(bank, m, f, g):
-            nc.tensor.matmul_mx(
-                out=bank[:],
-                lhsT=codes_of(c_code, m // 4, g)[:, 256 * (m % 4) : 256 * (m % 4 + 1)].bitcast(FP4X4),
-                lhsT_scale=c_plane[m // 4][:, g, P * (m % 4) : P * (m % 4 + 1)],
-                rhs=codes_of(b_code, f, g).bitcast(FP4X4),
-                rhs_scale=b_plane[f][:, g, :],
-                start=(g == 0),
-                stop=(g == KG - 1),
-            )
-
-        product = {}
         gated = {}
-        h_code = {}
-        h_plane = {}
-        h_bank = {}
         h_turned = {}
+        h_code = {}
+        h_scale = {}
 
-        def first(m, f, lo=0, hi=KG):
-            if lo == 0:
-                product[m, f] = new_bank(("first", m, f))
-            for g in range(lo, hi):
-                first_pass(product[m, f], m, f, g)
+        def first(m, f, g_lo=0, g_hi=GENE_PASSES):
+            if g_lo == 0:
+                take_bank(("first", m, f))
+            for g in range(g_lo, g_hi):
+                nc.tensor.matmul_mx(
+                    out=bank_tile["first", m, f][:],
+                    lhsT=codes_of(c_code, m // 4, g)[:, 256 * (m % 4) : 256 * (m % 4 + 1)].bitcast(FP4X4),
+                    lhsT_scale=c_scale[m // 4][:, g, P * (m % 4) : P * (m % 4 + 1)],
+                    rhs=codes_of(b_code, f, g).bitcast(FP4X4),
+                    rhs_scale=b_scale[f][:, g, :],
+                    start=(g == 0),
+                    stop=(g == GENE_PASSES - 1),
+                )
 
         def gate(m, f):
             if m not in gated:
-                gated[m] = work.tile([P, F], BF16, name="gated", tag="gated", bufs=4, align_bytes=ALIGN)
-            half = gated[m][:].rearrange("p (u g n) -> p u g n", u=2, g=FG)[:, :, f, :]
+                gated[m] = rotating("gated", [P, F], BF16, 4)
+            target = gated[m][:].rearrange("p (u f n) -> p u f n", u=2, f=FEATURE_PASSES)[:, :, f, :]
             nc.vector.tensor_tensor(
-                out=half.rearrange("p u (b x) -> p u b x", x=16),
-                in0=product[m, f][:].rearrange("p (b u x) -> p u b x", u=2, x=16),
-                in1=act[m][:, 512 * f : 512 * (f + 1)].rearrange("p (b u x) -> p u b x", u=2, x=16),
+                out=target.rearrange("p u (b x) -> p u b x", x=16),
+                in0=bank_tile["first", m, f][:].rearrange("p (b u x) -> p u b x", u=2, x=16),
+                in1=act[m][:, BANK * f : BANK * (f + 1)].rearrange("p (b u x) -> p u b x", u=2, x=16),
                 op=ALU.mult,
             )
-            release(("first", m, f))
+            release_bank(("first", m, f))
 
-        def h_turn(m):
-            bank = new_bank(("h", m))
+        def h_turn(m, f_lo=0, f_hi=FEATURE_PASSES):
+            bank = take_bank(("h", m, f_lo))
             words = gated[m][:].bitcast(F32)
-            for g in range(FG):
+            for f in range(f_lo, f_hi):
                 for u in range(2):
-                    start = 256 * u + 128 * g
+                    start = 256 * u + 128 * f
                     nc.tensor.transpose(
-                        bank[:, (2 * g + u) * P : (2 * g + u + 1) * P], words[:, start : start + P], ident[:]
+                        bank[:, (2 * f + u) * P : (2 * f + u + 1) * P], words[:, start : start + P], ident[:]
                     )
-            h_bank[m] = bank
 
-        def h_empty(m, copy):
-            h_turned[m] = work.tile([P, 4 * FG * P], BF16, name="h_turned", tag="h_turned", bufs=4, align_bytes=ALIGN)
-            copy(
-                out=h_turned[m][:].bitcast(F32).rearrange("p (g r u) -> p g r u", g=FG, u=2),
-                in_=h_bank[m][:].rearrange("p (g u r) -> p g r u", g=FG, u=2),
+        def h_empty(m, f_lo=0, f_hi=FEATURE_PASSES):
+            if f_lo == 0:
+                h_turned[m] = rotating("h_turned", [P, F], BF16, 4)
+            nc.scalar.copy(
+                out=h_turned[m][:].bitcast(F32).rearrange("p (f r u) -> p f r u", f=FEATURE_PASSES, u=2)[:, f_lo:f_hi],
+                in_=bank_tile["h", m, f_lo][:].rearrange("p (f u r) -> p f r u", f=FEATURE_PASSES, u=2)[:, f_lo:f_hi],
             )
-            release(("h", m))
+            release_bank(("h", m, f_lo))
 
-        def h_quantize(m):
-            h_code[m] = work.tile([P, FG * P], U32, name="h_code", tag="h_code", bufs=MT, align_bytes=ALIGN)
-            h_plane[m] = work.tile([P, FG * P], U8, name="h_plane", tag="h_plane", bufs=MT, align_bytes=ALIGN)
-            nc.vector.quantize_mx(out=h_code[m][:].bitcast(FP8X4), scales=h_plane[m][:], in_=h_turned[m][:])
+        def h_quantize(m, f_lo=0, f_hi=FEATURE_PASSES):
+            if f_lo == 0:
+                h_code[m] = rotating("h_code", [P, FEATURE_PASSES * P], U32, CELL_TILES)
+                h_scale[m] = rotating("h_scale", [P, FEATURE_PASSES * P], U8, CELL_TILES)
+            nc.vector.quantize_mx(
+                out=h_code[m][:, P * f_lo : P * f_hi].bitcast(FP8X4),
+                scales=h_scale[m][:, P * f_lo : P * f_hi],
+                in_=h_turned[m][:, BANK * f_lo : BANK * f_hi],
+            )
 
         z = {}
-        sums = {}
 
-        def second(m, rc, lo=0, hi=512):
-            bank = new_bank(("second", m, rc, lo))
-            for g in range(FG):
-                nc.tensor.matmul_mx(
-                    out=bank[:, lo:hi],
-                    lhsT=h_code[m][:, P * g : P * (g + 1)].bitcast(FP8X4),
-                    lhsT_scale=h_plane[m][:, P * g : P * (g + 1)],
-                    rhs=d_code[rc][:, g, lo:hi].bitcast(FP8X4),
-                    rhs_scale=d_plane[rc][:, g, lo:hi],
-                    start=(g == 0),
-                    stop=(g == FG - 1),
+        def unit(m, q, lo=0, hi=BANK):
+            return (m, q, lo, hi)
+
+        def second(*units):
+            for m, q, lo, hi in units:
+                bank = take_bank((m, q, lo, hi))
+                for f in range(FEATURE_PASSES):
+                    nc.tensor.matmul_mx(
+                        out=bank[:, lo:hi],
+                        lhsT=h_code[m][:, P * f : P * (f + 1)].bitcast(FP8X4),
+                        lhsT_scale=h_scale[m][:, P * f : P * (f + 1)],
+                        rhs=d_code[q][:, f, lo:hi].bitcast(FP8X4),
+                        rhs_scale=d_scale[q][:, f, lo:hi],
+                        start=(f == 0),
+                        stop=(f == FEATURE_PASSES - 1),
+                    )
+
+        def add_bias(*units):
+            tile = rotating("z", [P, 2, BANK], F32, 16)
+            for slot, (m, q, lo, hi) in reversed(list(enumerate(units))):
+                z[m, q, lo, hi] = (tile, slot)
+                nc.vector.tensor_tensor(
+                    out=tile[:, slot, lo:hi],
+                    in0=bank_tile[m, q, lo, hi][:, lo:hi],
+                    in1=bias[:, BANK * q + lo : BANK * q + hi],
+                    op=ALU.add,
                 )
-            sums[m, rc, lo] = bank
+                release_bank((m, q, lo, hi))
 
-        def add_bias(m, rc, lo=0, hi=512):
-            if (m, rc // 2) not in z:
-                z[m, rc // 2] = work.tile([P, 1024], F32, name="z", tag="z", bufs=Z_BUFS, align_bytes=ALIGN)
-            c0 = 512 * (rc % 2)
-            nc.vector.tensor_tensor(
-                out=z[m, rc // 2][:, c0 + lo : c0 + hi],
-                in0=sums[m, rc, lo][:, lo:hi],
-                in1=bias[:, 512 * rc + lo : 512 * rc + hi],
-                op=ALU.add,
-            )
-            release(("second", m, rc, lo))
-
-        def finish(m, lo, hi):
-            piece = z[m, lo // 1024][:, lo % 1024 : lo % 1024 + hi - lo]
+        def finish(*units):
+            tile, slot = z[units[0]]
+            m, q, lo, hi = units[0]
+            piece = tile[:, slot, lo:hi] if len(units) == 1 else tile[:].rearrange("p s n -> p (s n)")
             nc.scalar.activation(out=piece, in_=piece, func=ACT.Sigmoid)
-            nc.sync.dma_start(out=out[P * m : P * (m + 1), lo:hi], in_=piece)
+            if len(units) == 1 or units[1] == unit(m, q + 1):
+                start = BANK * q + lo
+                nc.sync.dma_start(out=out[P * m : P * (m + 1), start : start + piece.shape[1]], in_=piece)
+            else:
+                for slot, (m, q, lo, hi) in enumerate(units):
+                    nc.sync.dma_start(out=out[P * m : P * (m + 1), BANK * q : BANK * (q + 1)], in_=tile[:, slot])
 
-        clear(nc.vector, c_plane[0])
-        clear(nc.vector, b_plane[0])
-        clear(nc.vector, b_plane[1])
-        clear(nc.vector, c_plane[1])
+        def multiply(*units):
+            second(*units)
+            add_bias(*units)
+
+        for scale in (c_scale[0], b_scale[0], b_scale[1], c_scale[1]):
+            nc.vector.memset(scale[:].rearrange("p g n -> p (g n)").bitcast(I32), 0)
         make_identity(nc, ident[:])
-        load_bias()
-        load_codes(c_code, c_words_v, 0, 0)
-        load_codes(b_code, b_words_v, 0, 0)
-        load_scales(c_plane, c_scales_v, 0)
-        load_scales(b_plane, b_scales_v, 0)
-        load_codes(c_code, c_words_v, 0, 1)
-        load_codes(b_code, b_words_v, 0, 1)
-        load_codes(c_code, c_words_v, 0, 2)
-        load_codes(b_code, b_words_v, 0, 2)
-        load_scales(b_plane, b_scales_v, 1)
+        nc.scalar.activation(out=fixed("unread", [P, 8], F32)[:], in_=ident[:, 0:8], func=ACT.Sigmoid)
+
+        nc.sync.dma_start(out=bias_words[:].bitcast(BF16), in_=pair_bias.rearrange("(p n) -> p n", p=P))
+        for piece in range(len(PIECES[0])):
+            load_codes(c_code, c_words_v, 0, piece)
+            load_codes(b_code, b_words_v, 0, piece)
+            if piece == 0:
+                load_scales(c_scale, c_scales_v, 0)
+                load_scales(b_scale, b_scales_v, 0)
+        spread_bias(0)
+        for i in range(2):
+            warm_up_tensor()
+        spread_bias(1)
+        load_scales(b_scale, b_scales_v, 1)
         load_codes(b_code, b_words_v, 1, 0)
-        load_act(0)
-        load_act(1)
-        load_act(2)
+        for m in range(3):
+            load_act(m)
         load_pairs(0)
         load_act(3)
         load_pairs(1)
         load_pairs(2)
-        load_pairs(3)
-        load_scales(c_plane, c_scales_v, 1)
+        load_scales(c_scale, c_scales_v, 1)
         load_codes(c_code, c_words_v, 1, 0)
-        load_act(4)
-        load_pairs(4)
-        load_pairs(5)
-        load_act(5)
-        load_pairs(6)
+        for m in (4, 5):
+            load_pairs(2 * m - 5)
+            load_act(m)
+            load_pairs(2 * m - 4)
         load_pairs(7)
         load_act(6)
         load_act(7)
-        spread_bias()
-        pairs_permute(0, on_scalar)
-        pairs_permute(1, on_scalar)
-        first(0, 0, 0, 1)
-        first(1, 0, 0, 1)
-        first(2, 0, 0, 1)
-        first(3, 0, 0, 1)
-        first(0, 0, 1, 2)
-        first(1, 0, 1, 2)
-        first(2, 0, 1, 2)
-        first(3, 0, 1, 2)
-        first(0, 0, 2)
+
+        pairs_sort(0, on_scalar)
+        pairs_sort(1, on_scalar)
+        for g_lo, g_hi in PIECES[0]:
+            for m in range(4):
+                first(m, 0, g_lo, g_hi)
         gate(0, 0)
-        first(1, 0, 2)
         gate(1, 0)
-        first(2, 0, 2)
-        first(3, 0, 2)
-        first(0, 1)
-        gate(0, 1)
-        gate(2, 0)
-        first(1, 1)
-        gate(1, 1)
-        gate(3, 0)
-        first(2, 1)
-        gate(2, 1)
-        first(3, 1)
-        gate(3, 1)
-        pairs_permute(2, on_vector)
+        for m in range(4):
+            first(m, 1)
+            gate(m, 1)
+            if m < 2:
+                gate(m + 2, 0)
+        pairs_sort(2, on_vector)
+
         pairs_turn(0, 0)
-        pairs_empty(0, 0, on_scalar)
+        pairs_empty(0, 0, on_vector)
         pairs_turn(0, 1)
         pairs_empty(0, 1, on_scalar)
         h_turn(0)
-        h_empty(0, on_vector)
-        pairs_permute(3, on_vector)
+        h_empty(0)
         h_turn(1)
-        h_empty(1, on_scalar)
         pairs_turn(1, 0)
         pairs_empty(1, 0, on_scalar)
+        h_empty(1)
         pairs_turn(1, 1)
         pairs_empty(1, 1, on_vector)
         h_quantize(0)
         pairs_quantize(0)
         h_quantize(1)
-        h_turn(2)
-        h_turn(3)
-        h_empty(3, on_scalar)
-        h_empty(2, on_scalar)
+        for m in (2, 3):
+            h_turn(m)
+            h_empty(m)
         h_quantize(2)
-        h_quantize(3)
-        pairs_turn(2, 0)
-        pairs_turn(2, 1)
-        pairs_empty(2, 1, on_scalar)
-        pairs_empty(2, 0, on_scalar)
-        pairs_turn(3, 0)
-        pairs_turn(3, 1)
-        pairs_empty(3, 1, on_scalar)
-        pairs_empty(3, 0, on_scalar)
-        pairs_permute(4, on_scalar)
-        pairs_permute(5, on_scalar)
+        for g in range(FEATURE_PASSES):
+            pairs_turn(2, g)
+        for g in reversed(range(FEATURE_PASSES)):
+            pairs_empty(2, g, on_scalar)
+        pairs_sort(3, on_scalar)
+        pairs_sort(4, on_scalar)
+
         first(4, 0)
         gate(4, 0)
-        pairs_quantize(1)
+        h_quantize(3)
         first(4, 1)
         gate(4, 1)
-        second(0, 0)
-        second(1, 0)
-        add_bias(1, 0)
-        add_bias(0, 0)
-        second(2, 0)
-        finish(0, 0, 512)
-        second(3, 0)
-        add_bias(3, 0)
-        add_bias(2, 0)
-        first(5, 0)
-        gate(5, 0)
-        pairs_permute(6, on_vector)
-        pairs_turn(4, 0)
-        pairs_turn(4, 1)
-        pairs_empty(4, 1, on_scalar)
-        pairs_empty(4, 0, on_scalar)
-        h_turn(4)
-        h_empty(4, on_scalar)
-        pairs_turn(5, 0)
-        pairs_turn(5, 1)
-        pairs_empty(5, 1, on_scalar)
-        pairs_empty(5, 0, on_scalar)
-        pairs_permute(7, on_scalar)
-        finish(1, 0, 512)
-        second(0, 1)
-        second(1, 1)
-        add_bias(1, 1)
-        add_bias(0, 1)
-        h_quantize(4)
+        twos = [(unit(m, 0), unit(m + 1, 0)) for m in (0, 2)]
+        multiply(*twos[0])
+        pairs_sort(5, on_vector)
+        multiply(*twos[1])
+
+        def run(m, loads):
+            h_turn(m)
+            h_empty(m)
+            h_quantize(m)
+            for j in loads[:-1]:
+                for g in range(FEATURE_PASSES):
+                    pairs_turn(j, g)
+                for g in reversed(range(FEATURE_PASSES)):
+                    pairs_empty(j, g, on_scalar)
+            pairs_turn(loads[-1], 0)
+            pairs_empty(loads[-1], 0, on_scalar)
+            pairs_turn(loads[-1], 1)
+            pairs_empty(loads[-1], 1, on_vector)
+
+        run(4, (3, 4, 5))
+        finish(*twos[0])
+        pairs_sort(6, on_scalar)
+        pairs_sort(7, on_scalar)
+        finish(*twos[1])
+        pairs_quantize(1)
         pairs_quantize(2)
-        second(2, 1)
-        finish(0, 512, 1024)
-        finish(1, 512, 1024)
-        second(3, 1)
-        first(5, 1)
-        gate(5, 1)
-        add_bias(3, 1)
-        add_bias(2, 1)
-        second(4, 0)
-        second(4, 1)
-        add_bias(4, 1)
-        add_bias(4, 0)
-        pairs_turn(6, 0)
-        pairs_turn(6, 1)
-        pairs_empty(6, 1, on_scalar)
-        pairs_empty(6, 0, on_scalar)
-        pairs_turn(7, 0)
-        pairs_turn(7, 1)
-        pairs_empty(7, 1, on_scalar)
-        pairs_empty(7, 0, on_scalar)
-        h_turn(5)
-        h_empty(5, on_scalar)
-        finish(2, 0, 1024)
-        finish(3, 0, 1024)
-        finish(4, 0, 1024)
-        second(0, 2)
-        second(1, 2)
-        add_bias(1, 2)
-        add_bias(0, 2)
-        h_quantize(5)
-        pairs_quantize(3)
-        second(2, 2)
-        finish(1, 1024, 1536)
-        finish(0, 1024, 1536)
-        second(3, 2)
+        for f in range(FEATURE_PASSES):
+            first(5, f)
+            gate(5, f)
+        units = [unit(4, 0)] + [unit(m, 1) for m in range(5)]
+        twos = list(zip(units[0::2], units[1::2]))
+        for two in twos:
+            multiply(*two)
+
+        run(5, (6, 7))
+        for two in twos:
+            finish(*two)
+        units = [unit(m, 2) for m in range(5)] + [unit(5, q) for q in range(3)] + [unit(m, 3) for m in range(4)]
+        twos = list(zip(units[0::2], units[1::2]))
+        multiply(*twos[0])
         first(6, 0)
+        finish(*twos[0])
         gate(6, 0)
-        add_bias(3, 2)
-        add_bias(2, 2)
-        second(4, 2)
-        finish(3, 1024, 1536)
-        finish(2, 1024, 1536)
-        second(5, 0)
-        add_bias(5, 0)
-        add_bias(4, 2)
-        second(0, 3)
-        finish(5, 0, 512)
+        pairs_quantize(3)
+        for two in twos[1:3]:
+            multiply(*two)
+            finish(*two)
         first(6, 1)
         gate(6, 1)
-        add_bias(0, 3)
-        second(1, 3)
-        second(2, 3)
-        add_bias(2, 3)
-        add_bias(1, 3)
-        second(3, 3)
-        add_bias(3, 3)
-        h_turn(6)
-        h_empty(6, on_scalar)
-        finish(4, 1024, 1536)
-        finish(0, 1536, 2048)
-        finish(2, 1536, 2048)
-        finish(1, 1536, 2048)
-        finish(3, 1536, 2048)
-        h_quantize(6)
-        second(4, 3)
-        add_bias(4, 3)
+        multiply(*twos[3])
+        finish(*twos[3])
         first(7, 0)
-        finish(4, 1536, 2048)
         gate(7, 0)
-        second(5, 1)
-        add_bias(5, 1)
+        multiply(*twos[4])
+
+        h_turn(6)
+        h_empty(6)
+        h_quantize(6)
+        h_turn(7, 0, 1)
+        h_empty(7, 0, 1)
+        finish(*twos[4])
+        multiply(*twos[5])
+        finish(*twos[5])
+        multiply(unit(4, 3))
+        finish(unit(4, 3))
         first(7, 1)
-        finish(5, 512, 1024)
         gate(7, 1)
-        second(5, 2)
-        add_bias(5, 2)
-        second(5, 3)
-        add_bias(5, 3)
-        h_turn(7)
-        h_empty(7, on_scalar)
-        finish(5, 1024, 1536)
-        finish(5, 1536, 2048)
-        second(6, 0)
-        add_bias(6, 0)
-        h_quantize(7)
-        second(6, 1)
-        finish(6, 0, 512)
-        second(6, 2)
-        add_bias(6, 2)
-        add_bias(6, 1)
-        second(6, 3)
-        finish(6, 1024, 1536)
-        finish(6, 512, 1024)
-        second(7, 0)
-        add_bias(7, 0)
-        add_bias(6, 3)
-        second(7, 1)
-        finish(7, 0, 512)
-        finish(6, 1536, 2048)
-        second(7, 2)
-        add_bias(7, 2)
-        add_bias(7, 1)
-        second(7, 3, 0, 256)
-        finish(7, 1024, 1536)
-        finish(7, 512, 1024)
-        second(7, 3, 256, 512)
-        add_bias(7, 3, 256, 512)
-        add_bias(7, 3, 0, 256)
-        finish(7, 1792, 2048)
-        finish(7, 1536, 1792)
+        h_quantize(7, 0, 1)
+        units = [unit(5, 3)] + [unit(6, q) for q in range(QUARTERS)] + [unit(7, 0)]
+        twos = list(zip(units[0::2], units[1::2]))
+        multiply(*twos[0])
+        h_turn(7, 1, 2)
+        h_empty(7, 1, 2)
+        h_quantize(7, 1, 2)
+        for i, two in enumerate(twos):
+            if i > 0:
+                multiply(*two)
+            for one in reversed(two):
+                finish(one)
+        for one in (unit(7, 1), unit(7, 2), unit(7, 3, 0, BANK // 2), unit(7, 3, BANK // 2, BANK)):
+            multiply(one)
+            finish(one)

@@ -55,16 +55,18 @@ def tile_drug_synergy_bilinear_s4_kernel(
         def release_bank(key):
             free_banks.append(bank_name[key])
 
-        c_scale = [fixed("c_scale%d" % half, [P, GENE_PASSES, BANK], U8) for half in range(2)]
-        b_scale = [fixed("b_scale%d" % half, [P, GENE_PASSES, BANK], U8) for half in range(2)]
-        c_code = {}
-        b_code = {}
-        for name, codes in (("c_code", c_code), ("b_code", b_code)):
+        def operand_tiles(name):
+            scale = [fixed("%s_scale%d" % (name, half), [P, GENE_PASSES, BANK], U8) for half in range(2)]
+            code = {}
             for half in range(2):
                 for lo, hi in PIECES[half]:
-                    codes[half, lo] = fixed("%s%d%d" % (name, half, lo), [P, hi - lo, 2 * BANK], U8)
+                    code[half, lo] = fixed("%s_code%d%d" % (name, half, lo), [P, hi - lo, 2 * BANK], U8)
+            return scale, code
+
+        b_scale, b_code = operand_tiles("b")
         act = [fixed("act%d" % m, [P, F], BF16) for m in range(CELL_TILES)]
         raw = [fixed("raw%d" % j, [P, 2 * F], BF16) for j in range(LOADS)]
+        c_scale, c_code = operand_tiles("c")
         d_code = [fixed("d_code%d" % q, [P, FEATURE_PASSES, BANK], U32) for q in range(QUARTERS)]
         d_scale = [fixed("d_scale%d" % q, [P, FEATURE_PASSES, BANK], U8) for q in range(QUARTERS)]
         ident = fixed("ident", [P, P], F32)
@@ -349,7 +351,7 @@ def tile_drug_synergy_bilinear_s4_kernel(
         pairs_sort(5, on_vector)
         multiply(*twos[1])
 
-        def run(m, loads):
+        def run(m, loads, last_copy):
             h_turn(m)
             h_empty(m)
             h_quantize(m)
@@ -358,12 +360,12 @@ def tile_drug_synergy_bilinear_s4_kernel(
                     pairs_turn(j, g)
                 for g in reversed(range(FEATURE_PASSES)):
                     pairs_empty(j, g, on_scalar)
-            pairs_turn(loads[-1], 0)
+            for g in range(FEATURE_PASSES):
+                pairs_turn(loads[-1], g)
+            pairs_empty(loads[-1], 1, last_copy)
             pairs_empty(loads[-1], 0, on_scalar)
-            pairs_turn(loads[-1], 1)
-            pairs_empty(loads[-1], 1, on_vector)
 
-        run(4, (3, 4, 5))
+        run(4, (3, 4, 5), on_vector)
         finish(*twos[0])
         pairs_sort(6, on_scalar)
         pairs_sort(7, on_scalar)
@@ -378,7 +380,7 @@ def tile_drug_synergy_bilinear_s4_kernel(
         for two in twos:
             multiply(*two)
 
-        run(5, (6, 7))
+        run(5, (6, 7), on_scalar)
         for two in twos:
             finish(*two)
         units = [unit(m, 2) for m in range(5)] + [unit(5, q) for q in range(3)] + [unit(m, 3) for m in range(4)]
@@ -411,13 +413,12 @@ def tile_drug_synergy_bilinear_s4_kernel(
         finish(unit(4, 3))
         first(7, 1)
         gate(7, 1)
-        h_quantize(7, 0, 1)
         units = [unit(5, 3)] + [unit(6, q) for q in range(QUARTERS)] + [unit(7, 0)]
         twos = list(zip(units[0::2], units[1::2]))
         multiply(*twos[0])
         h_turn(7, 1, 2)
         h_empty(7, 1, 2)
-        h_quantize(7, 1, 2)
+        h_quantize(7)
         for i, two in enumerate(twos):
             if i > 0:
                 multiply(*two)

@@ -55,18 +55,16 @@ def tile_drug_synergy_bilinear_s4_kernel(
         def release_bank(key):
             free_banks.append(bank_name[key])
 
-        def operand_tiles(name):
-            scale = [fixed("%s_scale%d" % (name, half), [P, GENE_PASSES, BANK], U8) for half in range(2)]
-            code = {}
+        c_scale = [fixed("c_scale%d" % half, [P, GENE_PASSES, BANK], U8) for half in range(2)]
+        b_scale = [fixed("b_scale%d" % half, [P, GENE_PASSES, BANK], U8) for half in range(2)]
+        c_code = {}
+        b_code = {}
+        for name, codes in (("c_code", c_code), ("b_code", b_code)):
             for half in range(2):
                 for lo, hi in PIECES[half]:
-                    code[half, lo] = fixed("%s_code%d%d" % (name, half, lo), [P, hi - lo, 2 * BANK], U8)
-            return scale, code
-
-        b_scale, b_code = operand_tiles("b")
+                    codes[half, lo] = fixed("%s%d%d" % (name, half, lo), [P, hi - lo, 2 * BANK], U8)
         act = [fixed("act%d" % m, [P, F], BF16) for m in range(CELL_TILES)]
         raw = [fixed("raw%d" % j, [P, 2 * F], BF16) for j in range(LOADS)]
-        c_scale, c_code = operand_tiles("c")
         d_code = [fixed("d_code%d" % q, [P, FEATURE_PASSES, BANK], U32) for q in range(QUARTERS)]
         d_scale = [fixed("d_scale%d" % q, [P, FEATURE_PASSES, BANK], U8) for q in range(QUARTERS)]
         ident = fixed("ident", [P, P], F32)
@@ -191,34 +189,28 @@ def tile_drug_synergy_bilinear_s4_kernel(
             )
             release_bank(("first", m, f))
 
-        def h_turn(m, f_lo=0, f_hi=FEATURE_PASSES):
-            bank = take_bank(("h", m, f_lo))
+        def h_turn(m):
+            bank = take_bank(("h", m))
             words = gated[m][:].bitcast(F32)
-            for f in range(f_lo, f_hi):
+            for f in range(FEATURE_PASSES):
                 for u in range(2):
                     start = 256 * u + 128 * f
                     nc.tensor.transpose(
                         bank[:, (2 * f + u) * P : (2 * f + u + 1) * P], words[:, start : start + P], ident[:]
                     )
 
-        def h_empty(m, f_lo=0, f_hi=FEATURE_PASSES):
-            if f_lo == 0:
-                h_turned[m] = rotating("h_turned", [P, F], BF16, 4)
+        def h_empty(m):
+            h_turned[m] = rotating("h_turned", [P, F], BF16, 4)
             nc.scalar.copy(
-                out=h_turned[m][:].bitcast(F32).rearrange("p (f r u) -> p f r u", f=FEATURE_PASSES, u=2)[:, f_lo:f_hi],
-                in_=bank_tile["h", m, f_lo][:].rearrange("p (f u r) -> p f r u", f=FEATURE_PASSES, u=2)[:, f_lo:f_hi],
+                out=h_turned[m][:].bitcast(F32).rearrange("p (f r u) -> p f r u", f=FEATURE_PASSES, u=2),
+                in_=bank_tile["h", m][:].rearrange("p (f u r) -> p f r u", f=FEATURE_PASSES, u=2),
             )
-            release_bank(("h", m, f_lo))
+            release_bank(("h", m))
 
-        def h_quantize(m, f_lo=0, f_hi=FEATURE_PASSES):
-            if f_lo == 0:
-                h_code[m] = rotating("h_code", [P, FEATURE_PASSES * P], U32, CELL_TILES)
-                h_scale[m] = rotating("h_scale", [P, FEATURE_PASSES * P], U8, CELL_TILES)
-            nc.vector.quantize_mx(
-                out=h_code[m][:, P * f_lo : P * f_hi].bitcast(FP8X4),
-                scales=h_scale[m][:, P * f_lo : P * f_hi],
-                in_=h_turned[m][:, BANK * f_lo : BANK * f_hi],
-            )
+        def h_quantize(m):
+            h_code[m] = fixed("h_code%d" % m, [P, FEATURE_PASSES * P], U32)
+            h_scale[m] = fixed("h_scale%d" % m, [P, FEATURE_PASSES * P], U8)
+            nc.vector.quantize_mx(out=h_code[m][:].bitcast(FP8X4), scales=h_scale[m][:], in_=h_turned[m][:])
 
         z = {}
 
@@ -383,7 +375,7 @@ def tile_drug_synergy_bilinear_s4_kernel(
         run(5, (6, 7), on_scalar)
         for two in twos:
             finish(*two)
-        units = [unit(m, 2) for m in range(5)] + [unit(5, q) for q in range(3)] + [unit(m, 3) for m in range(4)]
+        units = [unit(m, 2) for m in range(5)] + [unit(5, q) for q in range(3)] + [unit(m, 3) for m in range(6)]
         twos = list(zip(units[0::2], units[1::2]))
         multiply(*twos[0])
         first(6, 0)
@@ -395,35 +387,30 @@ def tile_drug_synergy_bilinear_s4_kernel(
             finish(*two)
         first(6, 1)
         gate(6, 1)
-        multiply(*twos[3])
-        finish(*twos[3])
-        first(7, 0)
-        gate(7, 0)
-        multiply(*twos[4])
-
+        for two in twos[3:5]:
+            multiply(*two)
         h_turn(6)
         h_empty(6)
         h_quantize(6)
-        h_turn(7, 0, 1)
-        h_empty(7, 0, 1)
-        finish(*twos[4])
-        multiply(*twos[5])
-        finish(*twos[5])
-        multiply(unit(4, 3))
-        finish(unit(4, 3))
-        first(7, 1)
-        gate(7, 1)
-        units = [unit(5, 3)] + [unit(6, q) for q in range(QUARTERS)] + [unit(7, 0)]
-        twos = list(zip(units[0::2], units[1::2]))
+        for two in twos[3:5]:
+            finish(*two)
+        for two in twos[5:]:
+            multiply(*two)
+            finish(*two)
+
+        for f in range(FEATURE_PASSES):
+            first(7, f)
+            gate(7, f)
+        twos = [(unit(6, q), unit(6, q + 1)) for q in (0, 2)]
         multiply(*twos[0])
-        h_turn(7, 1, 2)
-        h_empty(7, 1, 2)
+        h_turn(7)
+        h_empty(7)
         h_quantize(7)
-        for i, two in enumerate(twos):
-            if i > 0:
-                multiply(*two)
-            for one in reversed(two):
-                finish(one)
-        for one in (unit(7, 1), unit(7, 2), unit(7, 3, 0, BANK // 2), unit(7, 3, BANK // 2, BANK)):
+        for one in reversed(twos[0]):
+            finish(one)
+        multiply(*twos[1])
+        for one in reversed(twos[1]):
+            finish(one)
+        for one in [unit(7, q) for q in range(3)] + [unit(7, 3, 0, BANK // 2), unit(7, 3, BANK // 2, BANK)]:
             multiply(one)
             finish(one)

@@ -23,6 +23,7 @@ FEATURE_PASSES = F // BANK
 CELL_TILES = M // P
 LOADS = R // (2 * P)
 QUARTERS = R // BANK
+UNIT_SCALES = 0x7F7F7F7F
 ALIGN = 64
 PIECES = (((0, 1), (1, 2), (2, 4)), ((0, 4),))
 
@@ -260,7 +261,7 @@ def tile_drug_synergy_bilinear_s4_kernel(
             add_bias(*units)
 
         for scale in (c_scale[0], b_scale[0], b_scale[1], c_scale[1]):
-            nc.vector.memset(scale[:].rearrange("p g n -> p (g n)").bitcast(I32), 0)
+            nc.vector.memset(scale[:].rearrange("p g n -> p (g n)").bitcast(I32), UNIT_SCALES)
         make_identity(nc, ident[:])
         nc.scalar.activation(out=fixed("unread", [P, 8], F32)[:], in_=ident[:, 0:8], func=ACT.Sigmoid)
 

@@ -272,10 +272,10 @@ def tile_drug_synergy_bilinear_s4_kernel(
             if piece == 0:
                 load_scales(c_scale, c_scales_v, 0)
                 load_scales(b_scale, b_scales_v, 0)
-        spread_bias(0)
+        for half in range(2):
+            spread_bias(half)
         for i in range(2):
             warm_up_tensor()
-        spread_bias(1)
         load_scales(b_scale, b_scales_v, 1)
         load_codes(b_code, b_words_v, 1, 0)
         for m in range(3):

@@ -24,8 +24,10 @@ CELL_TILES = M // P
 LOADS = R // (2 * P)
 QUARTERS = R // BANK
 UNIT_SCALES = 0x7F7F7F7F
+SORT_BUFS = 6
+UNIT_CODES = 0x22222222
 ALIGN = 64
-PIECES = (((0, 1), (1, 2), (2, 4)), ((0, 4),))
+CELL_GROUPS = ((0, 4), (4, 6), (6, 8))
 
 
 def tile_drug_synergy_bilinear_s4_kernel(
@@ -56,14 +58,16 @@ def tile_drug_synergy_bilinear_s4_kernel(
         def release_bank(key):
             free_banks.append(bank_name[key])
 
-        c_scale = [fixed("c_scale%d" % half, [P, GENE_PASSES, BANK], U8) for half in range(2)]
+        c_scale = [fixed("c_scale%d" % k, [P, GENE_PASSES, P * (hi - lo)], U8) for k, (lo, hi) in enumerate(CELL_GROUPS)]
         b_scale = [fixed("b_scale%d" % half, [P, GENE_PASSES, BANK], U8) for half in range(2)]
         c_code = {}
-        b_code = {}
-        for name, codes in (("c_code", c_code), ("b_code", b_code)):
-            for half in range(2):
-                for lo, hi in PIECES[half]:
-                    codes[half, lo] = fixed("%s%d%d" % (name, half, lo), [P, hi - lo, 2 * BANK], U8)
+        for g in range(GENE_PASSES):
+            c_code[0, g] = fixed("c_code0%d" % g, [P, 1, 2 * BANK], U8)
+        b_first = [fixed("b_first%d" % f, [P, 1, 2 * BANK], U8) for f in range(FEATURE_PASSES)]
+        b_code = {g: fixed("b_code%d" % g, [P, 1, 2 * F], U8) for g in range(1, GENE_PASSES)}
+        for k, (lo, hi) in list(enumerate(CELL_GROUPS))[1:]:
+            c_code[k, 0] = fixed("c_code%d" % k, [P, GENE_PASSES, 2 * P * (hi - lo)], U8)
+        c_first = fixed("c_first", [P, 2 * P], U8)
         act = [fixed("act%d" % m, [P, F], BF16) for m in range(CELL_TILES)]
         raw = [fixed("raw%d" % j, [P, 2 * F], BF16) for j in range(LOADS)]
         d_code = [fixed("d_code%d" % q, [P, FEATURE_PASSES, BANK], U32) for q in range(QUARTERS)]
@@ -85,19 +89,42 @@ def tile_drug_synergy_bilinear_s4_kernel(
         def load_act(m):
             nc.sync.dma_start(out=act[m][:], in_=act_v[m])
 
-        def load_codes(codes, source, half, piece):
-            lo, hi = PIECES[half][piece]
-            nc.sync.dma_start(out=codes[half, lo][:].bitcast(I32), in_=source[:, lo:hi, 256 * half : 256 * (half + 1)])
+        def load_codes(tile, source, g_lo, g_hi, lo, hi):
+            nc.sync.dma_start(out=tile.bitcast(I32), in_=source[:, g_lo:g_hi, lo // 2 : hi // 2])
 
-        def codes_of(codes, half, g):
-            lo = max(first_g for first_g, end_g in PIECES[half] if first_g <= g)
-            return codes[half, lo][:, g - lo]
+        def codes_of(codes, part, g):
+            first_g = max(g_lo for k, g_lo in codes if k == part and g_lo <= g)
+            return codes[part, first_g][:, g - first_g]
 
-        def load_scales(scale, source, half):
+        def feature_codes(f, g):
+            if g == 0:
+                return b_first[f][:, 0]
+            return b_code[g][:, 0, 2 * BANK * f : 2 * BANK * (f + 1)]
+
+        def group_of(m):
+            k = max(k for k, (lo, hi) in enumerate(CELL_GROUPS) if lo <= m)
+            return k, m - CELL_GROUPS[k][0]
+
+        def load_first_codes():
+            nc.sync.dma_start(out=c_first[:].bitcast(I32), in_=c_words_v[:, 0, 0:64])
+
+        def load_other_first_codes():
+            nc.sync.dma_start(out=c_code[0, 0][:, 0, 2 * P :].bitcast(I32), in_=c_words_v[:, 0, 64:256])
+
+        def cell_codes(m, g):
+            if m == 0 and g == 0:
+                return c_first[:]
+            k, place = group_of(m)
+            return codes_of(c_code, k, g)[:, 2 * P * place : 2 * P * (place + 1)]
+
+        def load_scales(scale, source, lo, hi):
             for r in range(4):
-                nc.sync.dma_start(
-                    out=scale[half][r:P:32].bitcast(I32), in_=source[r, :, :, 128 * half : 128 * (half + 1)]
-                )
+                nc.sync.dma_start(out=scale[r:P:32].bitcast(I32), in_=source[r, :, :, lo // 4 : hi // 4])
+
+        def load_cell_group(k):
+            lo, hi = P * CELL_GROUPS[k][0], P * CELL_GROUPS[k][1]
+            load_scales(c_scale[k], c_scales_v, lo, hi)
+            load_codes(c_code[k, 0][:], c_words_v, 0, GENE_PASSES, lo, hi)
 
         def spread_bias(half):
             bank = take_bank(("bias", half))
@@ -112,10 +139,10 @@ def tile_drug_synergy_bilinear_s4_kernel(
             bank = take_bank("warm-up")
             nc.tensor.matmul_mx(
                 out=bank[:],
-                lhsT=c_code[0, 0][:, 0, 0:256].bitcast(FP4X4),
-                lhsT_scale=c_scale[1][:, 0, 0:P],
-                rhs=c_code[0, 0][:, 0].bitcast(FP4X4),
-                rhs_scale=c_scale[1][:, 0, :],
+                lhsT=filler_codes[:, 0 : 2 * P].bitcast(FP4X4),
+                lhsT_scale=filler_scales[:, 0:P],
+                rhs=filler_codes.bitcast(FP4X4),
+                rhs_scale=filler_scales,
                 start=True,
                 stop=True,
             )
@@ -127,11 +154,14 @@ def tile_drug_synergy_bilinear_s4_kernel(
         grouped = {}
 
         def pairs_sort(j, copy):
-            sorted_pairs[j] = rotating("sorted_pairs", [P, F], F32, 4)
+            sorted_pairs[j] = rotating("sorted_pairs", [P, F], F32, SORT_BUFS)
             copy(
                 out=sorted_pairs[j][:].rearrange("p (u n x) -> p u n x", u=2, x=8),
                 in_=raw[j][:].bitcast(F32).rearrange("p (n u x) -> p u n x", u=2, x=8),
             )
+
+        def on_gpsimd(out, in_):
+            nc.gpsimd.tensor_copy(out=out.bitcast(U32), in_=in_.bitcast(U32))
 
         def pairs_turn(j, g):
             bank = take_bank(("pairs", j, g))
@@ -164,54 +194,58 @@ def tile_drug_synergy_bilinear_s4_kernel(
         h_code = {}
         h_scale = {}
 
-        def first(m, f, g_lo=0, g_hi=GENE_PASSES):
+        def first(m, f, g_lo=0, g_hi=GENE_PASSES, lo=0, hi=BANK):
+            k, place = group_of(m)
             if g_lo == 0:
-                take_bank(("first", m, f))
+                take_bank(("first", m, f, lo))
             for g in range(g_lo, g_hi):
                 nc.tensor.matmul_mx(
-                    out=bank_tile["first", m, f][:],
-                    lhsT=codes_of(c_code, m // 4, g)[:, 256 * (m % 4) : 256 * (m % 4 + 1)].bitcast(FP4X4),
-                    lhsT_scale=c_scale[m // 4][:, g, P * (m % 4) : P * (m % 4 + 1)],
-                    rhs=codes_of(b_code, f, g).bitcast(FP4X4),
-                    rhs_scale=b_scale[f][:, g, :],
+                    out=bank_tile["first", m, f, lo][:, lo:hi],
+                    lhsT=cell_codes(m, g).bitcast(FP4X4),
+                    lhsT_scale=c_scale[k][:, g, P * place : P * (place + 1)],
+                    rhs=feature_codes(f, g)[:, 2 * lo : 2 * hi].bitcast(FP4X4),
+                    rhs_scale=b_scale[f][:, g, lo:hi],
                     start=(g == 0),
                     stop=(g == GENE_PASSES - 1),
                 )
 
-        def gate(m, f):
-            if m not in gated:
-                gated[m] = rotating("gated", [P, F], BF16, 4)
-            target = gated[m][:].rearrange("p (u f n) -> p u f n", u=2, f=FEATURE_PASSES)[:, :, f, :]
+        def gate(m, f, lo=0, hi=BANK):
+            if lo == 0:
+                gated[m, f] = rotating("gated", [P, BANK], BF16, 8)
             nc.vector.tensor_tensor(
-                out=target.rearrange("p u (b x) -> p u b x", x=16),
-                in0=bank_tile["first", m, f][:].rearrange("p (b u x) -> p u b x", u=2, x=16),
-                in1=act[m][:, BANK * f : BANK * (f + 1)].rearrange("p (b u x) -> p u b x", u=2, x=16),
+                out=gated[m, f][:].rearrange("p (u b x) -> p u b x", u=2, x=16)[:, :, lo // 32 : hi // 32],
+                in0=bank_tile["first", m, f, lo][:, lo:hi].rearrange("p (b u x) -> p u b x", u=2, x=16),
+                in1=act[m][:, BANK * f + lo : BANK * f + hi].rearrange("p (b u x) -> p u b x", u=2, x=16),
                 op=ALU.mult,
             )
-            release_bank(("first", m, f))
+            release_bank(("first", m, f, lo))
 
-        def h_turn(m):
-            bank = take_bank(("h", m))
-            words = gated[m][:].bitcast(F32)
-            for f in range(FEATURE_PASSES):
+        def h_turn(m, f_lo=0, f_hi=FEATURE_PASSES):
+            bank = take_bank(("h", m, f_lo))
+            for f in range(f_lo, f_hi):
+                words = gated[m, f][:].bitcast(F32)
                 for u in range(2):
-                    start = 256 * u + 128 * f
                     nc.tensor.transpose(
-                        bank[:, (2 * f + u) * P : (2 * f + u + 1) * P], words[:, start : start + P], ident[:]
+                        bank[:, (2 * f + u) * P : (2 * f + u + 1) * P], words[:, P * u : P * (u + 1)], ident[:]
                     )
 
-        def h_empty(m):
-            h_turned[m] = rotating("h_turned", [P, F], BF16, 4)
-            nc.scalar.copy(
-                out=h_turned[m][:].bitcast(F32).rearrange("p (f r u) -> p f r u", f=FEATURE_PASSES, u=2),
-                in_=bank_tile["h", m][:].rearrange("p (f u r) -> p f r u", f=FEATURE_PASSES, u=2),
-            )
-            release_bank(("h", m))
+        def h_empty(m, f_lo=0, f_hi=FEATURE_PASSES, copy=on_scalar):
+            if f_lo == 0:
+                h_turned[m] = rotating("h_turned", [P, F], BF16, 4)
+            words = h_turned[m][:].bitcast(F32).rearrange("p (f r u) -> p f r u", f=FEATURE_PASSES, u=2)
+            turned = bank_tile["h", m, f_lo][:].rearrange("p (f u r) -> p f r u", f=FEATURE_PASSES, u=2)
+            copy(out=words[:, f_lo:f_hi], in_=turned[:, f_lo:f_hi])
+            release_bank(("h", m, f_lo))
 
-        def h_quantize(m):
-            h_code[m] = fixed("h_code%d" % m, [P, FEATURE_PASSES * P], U32)
-            h_scale[m] = fixed("h_scale%d" % m, [P, FEATURE_PASSES * P], U8)
-            nc.vector.quantize_mx(out=h_code[m][:].bitcast(FP8X4), scales=h_scale[m][:], in_=h_turned[m][:])
+        def h_quantize(m, f_lo=0, f_hi=FEATURE_PASSES):
+            if f_lo == 0:
+                h_code[m] = fixed("h_code%d" % m, [P, FEATURE_PASSES * P], U32)
+                h_scale[m] = fixed("h_scale%d" % m, [P, FEATURE_PASSES * P], U8)
+            nc.vector.quantize_mx(
+                out=h_code[m][:, P * f_lo : P * f_hi].bitcast(FP8X4),
+                scales=h_scale[m][:, P * f_lo : P * f_hi],
+                in_=h_turned[m][:, BANK * f_lo : BANK * f_hi],
+            )
 
         z = {}
 
@@ -232,84 +266,113 @@ def tile_drug_synergy_bilinear_s4_kernel(
                         stop=(f == FEATURE_PASSES - 1),
                     )
 
+        def reserve(*units):
+            tile = fixed("z%d%d_%d" % units[0][:3], [P, sum(hi - lo for m, q, lo, hi in units)], F32)
+            start = 0
+            for one in units:
+                z[one] = (tile, start)
+                start = start + one[3] - one[2]
+
         def add_bias(*units):
-            tile = rotating("z", [P, 2, BANK], F32, 16)
-            for slot, (m, q, lo, hi) in reversed(list(enumerate(units))):
-                z[m, q, lo, hi] = (tile, slot)
+            if units[0] not in z:
+                reserve(*units)
+            for m, q, lo, hi in reversed(units):
+                tile, start = z[m, q, lo, hi]
                 nc.vector.tensor_tensor(
-                    out=tile[:, slot, lo:hi],
+                    out=tile[:, start : start + hi - lo],
                     in0=bank_tile[m, q, lo, hi][:, lo:hi],
                     in1=bias[:, BANK * q + lo : BANK * q + hi],
                     op=ALU.add,
                 )
                 release_bank((m, q, lo, hi))
 
-        def finish(*units):
-            tile, slot = z[units[0]]
-            m, q, lo, hi = units[0]
-            piece = tile[:, slot, lo:hi] if len(units) == 1 else tile[:].rearrange("p s n -> p (s n)")
+        def sigmoid(*units):
+            tile, start = z[units[0]]
+            piece = tile[:, start : start + sum(hi - lo for m, q, lo, hi in units)]
             nc.scalar.activation(out=piece, in_=piece, func=ACT.Sigmoid)
-            if len(units) == 1 or units[1] == unit(m, q + 1):
-                start = BANK * q + lo
-                nc.sync.dma_start(out=out[P * m : P * (m + 1), start : start + piece.shape[1]], in_=piece)
-            else:
-                for slot, (m, q, lo, hi) in enumerate(units):
-                    nc.sync.dma_start(out=out[P * m : P * (m + 1), BANK * q : BANK * (q + 1)], in_=tile[:, slot])
+
+        def store(*units):
+            for m in sorted(set(one[0] for one in units)):
+                row = [one for one in units if one[0] == m]
+                tile, start = z[row[0]]
+                column = BANK * row[0][1] + row[0][2]
+                width = sum(hi - lo for m, q, lo, hi in row)
+                nc.sync.dma_start(out=out[P * m : P * (m + 1), column : column + width], in_=tile[:, start : start + width])
+
+        def finish(*units):
+            sigmoid(*units)
+            store(*units)
 
         def multiply(*units):
             second(*units)
             add_bias(*units)
 
-        for scale in (c_scale[0], b_scale[0], b_scale[1], c_scale[1]):
-            nc.vector.memset(scale[:].rearrange("p g n -> p (g n)").bitcast(I32), UNIT_SCALES)
+        def fill(tile, value):
+            nc.vector.memset(tile[:].rearrange("p g n -> p (g n)").bitcast(I32), value)
+
+        filler_codes = c_code[2, 0][:].rearrange("p g n -> p (g n)")[:, 0 : 2 * BANK]
+        filler_scales = c_scale[2][:].rearrange("p g n -> p (g n)")[:, 0:BANK]
+        for scale in (c_scale[0], b_scale[0], c_scale[2]):
+            fill(scale, UNIT_SCALES)
+        nc.vector.memset(filler_codes.bitcast(I32), UNIT_CODES)
+        for scale in (b_scale[1], c_scale[1]):
+            fill(scale, UNIT_SCALES)
         make_identity(nc, ident[:])
         nc.scalar.activation(out=fixed("unread", [P, 8], F32)[:], in_=ident[:, 0:8], func=ACT.Sigmoid)
 
         nc.sync.dma_start(out=bias_words[:].bitcast(BF16), in_=pair_bias.rearrange("(p n) -> p n", p=P))
-        for piece in range(len(PIECES[0])):
-            load_codes(c_code, c_words_v, 0, piece)
-            load_codes(b_code, b_words_v, 0, piece)
-            if piece == 0:
-                load_scales(c_scale, c_scales_v, 0)
-                load_scales(b_scale, b_scales_v, 0)
+        load_codes(b_first[0][:], b_words_v, 0, 1, 0, BANK)
+        load_first_codes()
+        load_scales(c_scale[0], c_scales_v, 0, BANK)
+        load_scales(b_scale[0], b_scales_v, 0, BANK)
+        load_other_first_codes()
+        for g in range(1, GENE_PASSES):
+            load_codes(c_code[0, g][:], c_words_v, g, g + 1, 0, BANK)
+            load_codes(b_code[g][:], b_words_v, g, g + 1, 0, F)
+        for i in range(3):
+            warm_up_tensor()
         for half in range(2):
             spread_bias(half)
-        for i in range(2):
+        for i in range(1):
             warm_up_tensor()
-        load_scales(b_scale, b_scales_v, 1)
-        load_codes(b_code, b_words_v, 1, 0)
-        for m in range(3):
-            load_act(m)
+        load_scales(b_scale[1], b_scales_v, BANK, F)
+        load_codes(b_first[1][:], b_words_v, 0, 1, BANK, F)
+        load_act(0)
+        load_act(1)
         load_pairs(0)
-        load_act(3)
+        load_act(2)
         load_pairs(1)
+        load_act(3)
+        load_cell_group(1)
         load_pairs(2)
-        load_scales(c_scale, c_scales_v, 1)
-        load_codes(c_code, c_words_v, 1, 0)
-        for m in (4, 5):
-            load_pairs(2 * m - 5)
-            load_act(m)
-            load_pairs(2 * m - 4)
+        load_act(4)
+        load_pairs(3)
+        load_pairs(4)
+        load_act(5)
+        load_pairs(5)
+        load_pairs(6)
         load_pairs(7)
+        load_cell_group(2)
         load_act(6)
         load_act(7)
 
         pairs_sort(0, on_scalar)
         pairs_sort(1, on_scalar)
-        for g_lo, g_hi in PIECES[0]:
+        for g in range(GENE_PASSES):
             for m in range(4):
-                first(m, 0, g_lo, g_hi)
+                first(m, 0, g, g + 1)
         gate(0, 0)
         gate(1, 0)
         for m in range(4):
             first(m, 1)
             gate(m, 1)
-            if m < 2:
-                gate(m + 2, 0)
-        pairs_sort(2, on_vector)
+            if m == 3:
+                gate(3, 0)
+            if m == 0:
+                gate(2, 0)
 
         pairs_turn(0, 0)
-        pairs_empty(0, 0, on_vector)
+        pairs_empty(0, 0, on_scalar)
         pairs_turn(0, 1)
         pairs_empty(0, 1, on_scalar)
         h_turn(0)
@@ -322,96 +385,101 @@ def tile_drug_synergy_bilinear_s4_kernel(
         pairs_empty(1, 1, on_vector)
         h_quantize(0)
         pairs_quantize(0)
-        h_quantize(1)
         for m in (2, 3):
             h_turn(m)
             h_empty(m)
         h_quantize(2)
-        for g in range(FEATURE_PASSES):
-            pairs_turn(2, g)
-        for g in reversed(range(FEATURE_PASSES)):
-            pairs_empty(2, g, on_scalar)
-        pairs_sort(3, on_scalar)
-        pairs_sort(4, on_scalar)
+        h_quantize(1)
+        for j in (2, 3, 4):
+            pairs_sort(j, on_scalar)
+        pairs_sort(5, on_gpsimd)
 
         first(4, 0)
-        gate(4, 0)
         h_quantize(3)
         first(4, 1)
         gate(4, 1)
-        twos = [(unit(m, 0), unit(m + 1, 0)) for m in (0, 2)]
-        multiply(*twos[0])
-        pairs_sort(5, on_vector)
-        multiply(*twos[1])
+        gate(4, 0)
 
-        def run(m, loads, last_copy):
+        def turn_load(j, copies=(on_scalar, on_scalar)):
+            for g in range(FEATURE_PASSES):
+                pairs_turn(j, g)
+            for g in reversed(range(FEATURE_PASSES)):
+                pairs_empty(j, g, copies[g])
+
+        def turn_cells(m):
             h_turn(m)
             h_empty(m)
-            h_quantize(m)
-            for j in loads[:-1]:
-                for g in range(FEATURE_PASSES):
-                    pairs_turn(j, g)
-                for g in reversed(range(FEATURE_PASSES)):
-                    pairs_empty(j, g, on_scalar)
-            for g in range(FEATURE_PASSES):
-                pairs_turn(loads[-1], g)
-            pairs_empty(loads[-1], 1, last_copy)
-            pairs_empty(loads[-1], 0, on_scalar)
 
-        run(4, (3, 4, 5), on_vector)
-        finish(*twos[0])
-        pairs_sort(6, on_scalar)
-        pairs_sort(7, on_scalar)
-        finish(*twos[1])
-        pairs_quantize(1)
-        pairs_quantize(2)
-        for f in range(FEATURE_PASSES):
-            first(5, f)
-            gate(5, f)
-        units = [unit(4, 0)] + [unit(m, 1) for m in range(5)]
-        twos = list(zip(units[0::2], units[1::2]))
-        for two in twos:
-            multiply(*two)
+        def in_twos(units):
+            return list(zip(units[0::2], units[1::2]))
 
-        run(5, (6, 7), on_scalar)
-        for two in twos:
-            finish(*two)
-        units = [unit(m, 2) for m in range(5)] + [unit(5, q) for q in range(3)] + [unit(m, 3) for m in range(6)]
-        twos = list(zip(units[0::2], units[1::2]))
+        twos = in_twos([unit(m, 0) for m in range(4)])
         multiply(*twos[0])
-        first(6, 0)
+        first(5, 0)
+        gate(5, 0)
+        first(5, 1)
+        gate(5, 1)
         finish(*twos[0])
-        gate(6, 0)
+        second(*twos[1])
+        for g in range(FEATURE_PASSES):
+            pairs_turn(2, g)
+            pairs_empty(2, g, on_scalar)
+        add_bias(*twos[1])
+        pairs_sort(6, on_gpsimd)
+        turn_load(3, (on_scalar, on_vector))
+        pairs_sort(7, on_gpsimd)
+        pairs_quantize(1)
+        turn_cells(4)
+        turn_cells(5)
+        h_quantize(4)
+        h_quantize(5)
+        turn_load(4)
+        turn_load(5, (on_scalar, on_vector))
+        pairs_quantize(2)
+        turn_load(6)
+        turn_load(7)
+        finish(*twos[1])
+        units = [unit(m, 1) for m in range(4)] + [unit(m, q) for m in (4, 5) for q in (0, 1)] + [unit(m, 2) for m in range(6)] + [unit(m, 3) for m in range(6)]
+        twos = in_twos(units)
+        multiply(*twos[0])
+        multiply(*twos[1])
         pairs_quantize(3)
-        for two in twos[1:3]:
-            multiply(*two)
+        reserve(*twos[2])
+        reserve(*twos[3])
+        multiply(*twos[2], *twos[3])
+        finish(*twos[0])
+        finish(*twos[1])
+        multiply(*twos[4])
+        finish(*twos[2])
+        finish(*twos[3])
+        for two, f in zip(twos[5:7], range(FEATURE_PASSES)):
+            second(*two)
+            first(6, f)
+            gate(6, f)
+            add_bias(*two)
+        for two in twos[4:6]:
             finish(*two)
-        first(6, 1)
-        gate(6, 1)
-        for two in twos[3:5]:
-            multiply(*two)
-        h_turn(6)
-        h_empty(6)
+        multiply(*twos[7])
+        finish(*twos[6])
+        multiply(*twos[8])
+        turn_cells(6)
         h_quantize(6)
-        for two in twos[3:5]:
-            finish(*two)
-        for two in twos[5:]:
-            multiply(*two)
-            finish(*two)
-
+        finish(*twos[7])
+        finish(*twos[8])
         for f in range(FEATURE_PASSES):
             first(7, f)
             gate(7, f)
-        twos = [(unit(6, q), unit(6, q + 1)) for q in (0, 2)]
-        multiply(*twos[0])
+        twos[6] = twos[9]
+        ahead = list(twos[6]) + [unit(6, 0)]
+        for one in ahead:
+            multiply(one)
+        finish(ahead[0])
         h_turn(7)
         h_empty(7)
+        multiply(unit(6, 1))
         h_quantize(7)
-        for one in reversed(twos[0]):
+        for one in ahead[1:] + [unit(6, 1)]:
             finish(one)
-        multiply(*twos[1])
-        for one in reversed(twos[1]):
-            finish(one)
-        for one in [unit(7, q) for q in range(3)] + [unit(7, 3, 0, BANK // 2), unit(7, 3, BANK // 2, BANK)]:
+        for one in [unit(6, 2), unit(6, 3)] + [unit(7, q) for q in range(3)] + [unit(7, 3, 0, BANK // 2), unit(7, 3, BANK // 2, BANK)]:
             multiply(one)
             finish(one)

@@ -347,10 +347,10 @@ def tile_drug_synergy_bilinear_s4_kernel(
         load_pairs(2)
         load_act(4)
         load_pairs(3)
-        load_pairs(4)
-        load_act(5)
         load_pairs(5)
+        load_pairs(4)
         load_pairs(6)
+        load_act(5)
         load_pairs(7)
         load_cell_group(2)
         load_act(6)

@@ -63,8 +63,9 @@ def tile_drug_synergy_bilinear_s4_kernel(
         c_code = {}
         for g in range(GENE_PASSES):
             c_code[0, g] = fixed("c_code0%d" % g, [P, 1, 2 * BANK], U8)
-        b_first = [fixed("b_first%d" % f, [P, 1, 2 * BANK], U8) for f in range(FEATURE_PASSES)]
-        b_code = {g: fixed("b_code%d" % g, [P, 1, 2 * F], U8) for g in range(1, GENE_PASSES)}
+        b_first = [fixed("b_first%d" % g, [P, 1, 2 * BANK], U8) for g in range(2)]
+        b_other = fixed("b_other", [P, 2, 2 * BANK], U8)
+        b_code = {g: fixed("b_code%d" % g, [P, 1, 2 * F], U8) for g in range(2, GENE_PASSES)}
         for k, (lo, hi) in list(enumerate(CELL_GROUPS))[1:]:
             c_code[k, 0] = fixed("c_code%d" % k, [P, GENE_PASSES, 2 * P * (hi - lo)], U8)
         c_first = fixed("c_first", [P, 2 * P], U8)
@@ -97,8 +98,8 @@ def tile_drug_synergy_bilinear_s4_kernel(
             return codes[part, first_g][:, g - first_g]
 
         def feature_codes(f, g):
-            if g == 0:
-                return b_first[f][:, 0]
+            if g < 2:
+                return b_other[:, g] if f else b_first[g][:, 0]
             return b_code[g][:, 0, 2 * BANK * f : 2 * BANK * (f + 1)]
 
         def group_of(m):
@@ -328,15 +329,18 @@ def tile_drug_synergy_bilinear_s4_kernel(
         load_other_first_codes()
         for g in range(1, GENE_PASSES):
             load_codes(c_code[0, g][:], c_words_v, g, g + 1, 0, BANK)
-            load_codes(b_code[g][:], b_words_v, g, g + 1, 0, F)
-        for i in range(3):
+            if g < 2:
+                load_codes(b_first[g][:], b_words_v, g, g + 1, 0, BANK)
+            else:
+                load_codes(b_code[g][:], b_words_v, g, g + 1, 0, F)
+        for i in range(4):
             warm_up_tensor()
         for half in range(2):
             spread_bias(half)
-        for i in range(1):
+        for i in range(0):
             warm_up_tensor()
         load_scales(b_scale[1], b_scales_v, BANK, F)
-        load_codes(b_first[1][:], b_words_v, 0, 1, BANK, F)
+        load_codes(b_other[:], b_words_v, 0, 2, BANK, F)
         load_act(0)
         load_act(1)
         load_pairs(0)

from contextlib import ExitStack

import concourse.mybir as mybir
from concourse.masks import make_identity

M, K, F, R = 1024, 2048, 1024, 2048
FLOPS = 2 * M * K * F + 2 * M * F * R

F32 = mybir.dt.float32
BF16 = mybir.dt.bfloat16
I32 = mybir.dt.int32
U32 = mybir.dt.uint32
U8 = mybir.dt.uint8
FP4X4 = mybir.dt.float4_e2m1fn_x4
FP8X4 = mybir.dt.float8_e4m3fn_x4
ACT = mybir.ActivationFunctionType
ALU = mybir.AluOpType

P = 128
BANK = 512
GENE_PASSES = K // BANK
FEATURE_PASSES = F // BANK
CELL_TILES = M // P
LOADS = R // (2 * P)
QUARTERS = R // BANK
UNIT_SCALES = 0x7F7F7F7F
SORT_BUFS = 6
UNIT_CODES = 0x22222222
ALIGN = 64
CELL_GROUPS = ((0, 4), (4, 6), (6, 8))


def tile_drug_synergy_bilinear_s4_kernel(
    tc, c_words, c_scales, b_words, b_scales, activity, pairs, pair_bias, out
):
    nc = tc.nc
    with ExitStack() as ctx:
        keep = ctx.enter_context(tc.tile_pool(name="keep", bufs=1))
        work = ctx.enter_context(tc.tile_pool(name="work", bufs=4))
        psum = ctx.enter_context(tc.psum_pool(name="psum", bufs=1))
        ctx.enter_context(tc.manual_schedule())

        def fixed(name, shape, dtype):
            return keep.tile(shape, dtype, name=name, tag=name, align_bytes=ALIGN)

        def rotating(name, shape, dtype, bufs):
            return work.tile(shape, dtype, name=name, tag=name, bufs=bufs, align_bytes=ALIGN)

        free_banks = ["bank%d" % i for i in range(8)]
        bank_name = {}
        bank_tile = {}

        def take_bank(key):
            bank_name[key] = free_banks.pop(0)
            bank_tile[key] = psum.tile([P, BANK], F32, name=bank_name[key], tag=bank_name[key])
            return bank_tile[key]

        def release_bank(key):
            free_banks.append(bank_name[key])

        c_scale = [fixed("c_scale%d" % k, [P, GENE_PASSES, P * (hi - lo)], U8) for k, (lo, hi) in enumerate(CELL_GROUPS)]
        b_scale = [fixed("b_scale%d" % half, [P, GENE_PASSES, BANK], U8) for half in range(2)]
        c_code = {}
        for g in range(GENE_PASSES):
            c_code[0, g] = fixed("c_code0%d" % g, [P, 1, 2 * BANK], U8)
        b_first = [fixed("b_first%d" % g, [P, 1, 2 * BANK], U8) for g in range(2)]
        b_other = fixed("b_other", [P, 2, 2 * BANK], U8)
        b_code = {g: fixed("b_code%d" % g, [P, 1, 2 * F], U8) for g in range(2, GENE_PASSES)}
        for k, (lo, hi) in list(enumerate(CELL_GROUPS))[1:]:
            c_code[k, 0] = fixed("c_code%d" % k, [P, GENE_PASSES, 2 * P * (hi - lo)], U8)
        c_first = fixed("c_first", [P, 2 * P], U8)
        act = [fixed("act%d" % m, [P, F], BF16) for m in range(CELL_TILES)]
        raw = [fixed("raw%d" % j, [P, 2 * F], BF16) for j in range(LOADS)]
        d_code = [fixed("d_code%d" % q, [P, FEATURE_PASSES, BANK], U32) for q in range(QUARTERS)]
        d_scale = [fixed("d_scale%d" % q, [P, FEATURE_PASSES, BANK], U8) for q in range(QUARTERS)]
        ident = fixed("ident", [P, P], F32)
        bias = fixed("bias", [P, R], BF16)
        bias_words = fixed("bias_words", [P, 8], F32)

        pairs_v = pairs.rearrange("(j p i) k -> j p (i k)", i=2, p=P)
        act_v = activity.rearrange("(m p) f -> m p f", p=P)
        c_scales_v = c_scales.bitcast(I32).rearrange("g (q r) n -> r q g n", r=4)
        b_scales_v = b_scales.bitcast(I32).rearrange("g (q r) n -> r q g n", r=4)
        c_words_v = c_words.bitcast(I32).rearrange("g p n -> p g n")
        b_words_v = b_words.bitcast(I32).rearrange("g p n -> p g n")

        def load_pairs(j):
            nc.sync.dma_start(out=raw[j][:], in_=pairs_v[j])

        def load_act(m):
            nc.sync.dma_start(out=act[m][:], in_=act_v[m])

        def load_codes(tile, source, g_lo, g_hi, lo, hi):
            nc.sync.dma_start(out=tile.bitcast(I32), in_=source[:, g_lo:g_hi, lo // 2 : hi // 2])

        def codes_of(codes, part, g):
            first_g = max(g_lo for k, g_lo in codes if k == part and g_lo <= g)
            return codes[part, first_g][:, g - first_g]

        def feature_codes(f, g):
            if g < 2:
                return b_other[:, g] if f else b_first[g][:, 0]
            return b_code[g][:, 0, 2 * BANK * f : 2 * BANK * (f + 1)]

        def group_of(m):
            k = max(k for k, (lo, hi) in enumerate(CELL_GROUPS) if lo <= m)
            return k, m - CELL_GROUPS[k][0]

        def load_first_codes():
            nc.sync.dma_start(out=c_first[:].bitcast(I32), in_=c_words_v[:, 0, 0:64])

        def load_other_first_codes():
            nc.sync.dma_start(out=c_code[0, 0][:, 0, 2 * P :].bitcast(I32), in_=c_words_v[:, 0, 64:256])

        def cell_codes(m, g):
            if m == 0 and g == 0:
                return c_first[:]
            k, place = group_of(m)
            return codes_of(c_code, k, g)[:, 2 * P * place : 2 * P * (place + 1)]

        def load_scales(scale, source, lo, hi):
            for r in range(4):
                nc.sync.dma_start(out=scale[r:P:32].bitcast(I32), in_=source[r, :, :, lo // 4 : hi // 4])

        def load_cell_group(k):
            lo, hi = P * CELL_GROUPS[k][0], P * CELL_GROUPS[k][1]
            load_scales(c_scale[k], c_scales_v, lo, hi)
            load_codes(c_code[k, 0][:], c_words_v, 0, GENE_PASSES, lo, hi)

        def spread_bias(half):
            bank = take_bank(("bias", half))
            for c in range(4):
                column = bias_words[:, 4 * half + c : 4 * half + c + 1]
                nc.tensor.transpose(bank[:, c * P : (c + 1) * P], column.to_broadcast([P, P]), ident[:])
            spread = bias[:].bitcast(F32).rearrange("x (p h c) -> x h p c", h=2, c=4)
            nc.scalar.copy(out=spread[:, half], in_=bank[:].rearrange("x (c p) -> x p c", c=4))
            release_bank(("bias", half))

        def warm_up_tensor():
            bank = take_bank("warm-up")
            nc.tensor.matmul_mx(
                out=bank[:],
                lhsT=filler_codes[:, 0 : 2 * P].bitcast(FP4X4),
                lhsT_scale=filler_scales[:, 0:P],
                rhs=filler_codes.bitcast(FP4X4),
                rhs_scale=filler_scales,
                start=True,
                stop=True,
            )
            release_bank("warm-up")

        on_vector, on_scalar = nc.vector.tensor_copy, nc.scalar.copy

        sorted_pairs = {}
        grouped = {}

        def pairs_sort(j, copy):
            sorted_pairs[j] = rotating("sorted_pairs", [P, F], F32, SORT_BUFS)
            copy(
                out=sorted_pairs[j][:].rearrange("p (u n x) -> p u n x", u=2, x=8),
                in_=raw[j][:].bitcast(F32).rearrange("p (n u x) -> p u n x", u=2, x=8),
            )

        def on_gpsimd(out, in_):
            nc.gpsimd.tensor_copy(out=out.bitcast(U32), in_=in_.bitcast(U32))

        def pairs_turn(j, g):
            bank = take_bank(("pairs", j, g))
            for i in range(2):
                for u in range(2):
                    start = 512 * u + 256 * i + 128 * g
                    nc.tensor.transpose(
                        bank[:, (2 * i + u) * P : (2 * i + u + 1) * P], sorted_pairs[j][:, start : start + P], ident[:]
                    )

        def pairs_empty(j, g, copy):
            if j // 2 not in grouped:
                grouped[j // 2] = rotating("grouped", [P, FEATURE_PASSES, 4 * BANK], BF16, 3)
            words = grouped[j // 2][:].bitcast(F32)
            copy(
                out=words[:, g, 512 * (j % 2) : 512 * (j % 2 + 1)].rearrange("p (r c) -> p r c", c=4),
                in_=bank_tile["pairs", j, g][:].rearrange("p (c r) -> p r c", c=4),
            )
            release_bank(("pairs", j, g))

        def pairs_quantize(q):
            nc.vector.quantize_mx(
                out=d_code[q][:].rearrange("p g r -> p (g r)").bitcast(FP8X4),
                scales=d_scale[q][:].rearrange("p g r -> p (g r)"),
                in_=grouped[q][:].rearrange("p g n -> p (g n)"),
            )

        gated = {}
        h_turned = {}
        h_code = {}
        h_scale = {}

        def first(m, f, g_lo=0, g_hi=GENE_PASSES, lo=0, hi=BANK):
            k, place = group_of(m)
            if g_lo == 0:
                take_bank(("first", m, f, lo))
            for g in range(g_lo, g_hi):
                nc.tensor.matmul_mx(
                    out=bank_tile["first", m, f, lo][:, lo:hi],
                    lhsT=cell_codes(m, g).bitcast(FP4X4),
                    lhsT_scale=c_scale[k][:, g, P * place : P * (place + 1)],
                    rhs=feature_codes(f, g)[:, 2 * lo : 2 * hi].bitcast(FP4X4),
                    rhs_scale=b_scale[f][:, g, lo:hi],
                    start=(g == 0),
                    stop=(g == GENE_PASSES - 1),
                )

        def gate(m, f, lo=0, hi=BANK):
            if lo == 0:
                gated[m, f] = rotating("gated", [P, BANK], BF16, 8)
            nc.vector.tensor_tensor(
                out=gated[m, f][:].rearrange("p (u b x) -> p u b x", u=2, x=16)[:, :, lo // 32 : hi // 32],
                in0=bank_tile["first", m, f, lo][:, lo:hi].rearrange("p (b u x) -> p u b x", u=2, x=16),
                in1=act[m][:, BANK * f + lo : BANK * f + hi].rearrange("p (b u x) -> p u b x", u=2, x=16),
                op=ALU.mult,
            )
            release_bank(("first", m, f, lo))

        def h_turn(m, f_lo=0, f_hi=FEATURE_PASSES):
            bank = take_bank(("h", m, f_lo))
            for f in range(f_lo, f_hi):
                words = gated[m, f][:].bitcast(F32)
                for u in range(2):
                    nc.tensor.transpose(
                        bank[:, (2 * f + u) * P : (2 * f + u + 1) * P], words[:, P * u : P * (u + 1)], ident[:]
                    )

        def h_empty(m, f_lo=0, f_hi=FEATURE_PASSES, copy=on_scalar):
            if f_lo == 0:
                h_turned[m] = rotating("h_turned", [P, F], BF16, 4)
            words = h_turned[m][:].bitcast(F32).rearrange("p (f r u) -> p f r u", f=FEATURE_PASSES, u=2)
            turned = bank_tile["h", m, f_lo][:].rearrange("p (f u r) -> p f r u", f=FEATURE_PASSES, u=2)
            copy(out=words[:, f_lo:f_hi], in_=turned[:, f_lo:f_hi])
            release_bank(("h", m, f_lo))

        def h_quantize(m, f_lo=0, f_hi=FEATURE_PASSES):
            if f_lo == 0:
                h_code[m] = fixed("h_code%d" % m, [P, FEATURE_PASSES * P], U32)
                h_scale[m] = fixed("h_scale%d" % m, [P, FEATURE_PASSES * P], U8)
            nc.vector.quantize_mx(
                out=h_code[m][:, P * f_lo : P * f_hi].bitcast(FP8X4),
                scales=h_scale[m][:, P * f_lo : P * f_hi],
                in_=h_turned[m][:, BANK * f_lo : BANK * f_hi],
            )

        z = {}

        def unit(m, q, lo=0, hi=BANK):
            return (m, q, lo, hi)

        def second(*units):
            for m, q, lo, hi in units:
                bank = take_bank((m, q, lo, hi))
                for f in range(FEATURE_PASSES):
                    nc.tensor.matmul_mx(
                        out=bank[:, lo:hi],
                        lhsT=h_code[m][:, P * f : P * (f + 1)].bitcast(FP8X4),
                        lhsT_scale=h_scale[m][:, P * f : P * (f + 1)],
                        rhs=d_code[q][:, f, lo:hi].bitcast(FP8X4),
                        rhs_scale=d_scale[q][:, f, lo:hi],
                        start=(f == 0),
                        stop=(f == FEATURE_PASSES - 1),
                    )

        def reserve(*units):
            tile = fixed("z%d%d_%d" % units[0][:3], [P, sum(hi - lo for m, q, lo, hi in units)], F32)
            start = 0
            for one in units:
                z[one] = (tile, start)
                start = start + one[3] - one[2]

        def add_bias(*units):
            if units[0] not in z:
                reserve(*units)
            for m, q, lo, hi in reversed(units):
                tile, start = z[m, q, lo, hi]
                nc.vector.tensor_tensor(
                    out=tile[:, start : start + hi - lo],
                    in0=bank_tile[m, q, lo, hi][:, lo:hi],
                    in1=bias[:, BANK * q + lo : BANK * q + hi],
                    op=ALU.add,
                )
                release_bank((m, q, lo, hi))

        def sigmoid(*units):
            tile, start = z[units[0]]
            piece = tile[:, start : start + sum(hi - lo for m, q, lo, hi in units)]
            nc.scalar.activation(out=piece, in_=piece, func=ACT.Sigmoid)

        def store(*units):
            for m in sorted(set(one[0] for one in units)):
                row = [one for one in units if one[0] == m]
                tile, start = z[row[0]]
                column = BANK * row[0][1] + row[0][2]
                width = sum(hi - lo for m, q, lo, hi in row)
                nc.sync.dma_start(out=out[P * m : P * (m + 1), column : column + width], in_=tile[:, start : start + width])

        def finish(*units):
            sigmoid(*units)
            store(*units)

        def multiply(*units):
            second(*units)
            add_bias(*units)

        def fill(tile, value):
            nc.vector.memset(tile[:].rearrange("p g n -> p (g n)").bitcast(I32), value)

        filler_codes = c_code[2, 0][:].rearrange("p g n -> p (g n)")[:, 0 : 2 * BANK]
        filler_scales = c_scale[2][:].rearrange("p g n -> p (g n)")[:, 0:BANK]
        for scale in (c_scale[0], b_scale[0], c_scale[2]):
            fill(scale, UNIT_SCALES)
        nc.vector.memset(filler_codes.bitcast(I32), UNIT_CODES)
        for scale in (b_scale[1], c_scale[1]):
            fill(scale, UNIT_SCALES)
        make_identity(nc, ident[:])
        nc.scalar.activation(out=fixed("unread", [P, 8], F32)[:], in_=ident[:, 0:8], func=ACT.Sigmoid)

        nc.sync.dma_start(out=bias_words[:].bitcast(BF16), in_=pair_bias.rearrange("(p n) -> p n", p=P))
        load_codes(b_first[0][:], b_words_v, 0, 1, 0, BANK)
        load_first_codes()
        load_scales(c_scale[0], c_scales_v, 0, BANK)
        load_scales(b_scale[0], b_scales_v, 0, BANK)
        load_other_first_codes()
        for g in range(1, GENE_PASSES):
            load_codes(c_code[0, g][:], c_words_v, g, g + 1, 0, BANK)
            if g < 2:
                load_codes(b_first[g][:], b_words_v, g, g + 1, 0, BANK)
            else:
                load_codes(b_code[g][:], b_words_v, g, g + 1, 0, F)
        for i in range(4):
            warm_up_tensor()
        for half in range(2):
            spread_bias(half)
        for i in range(0):
            warm_up_tensor()
        load_scales(b_scale[1], b_scales_v, BANK, F)
        load_codes(b_other[:], b_words_v, 0, 2, BANK, F)
        load_act(0)
        load_act(1)
        load_pairs(0)
        load_act(2)
        load_pairs(1)
        load_act(3)
        load_cell_group(1)
        load_pairs(2)
        load_act(4)
        load_pairs(3)
        load_pairs(5)
        load_pairs(4)
        load_pairs(6)
        load_act(5)
        load_pairs(7)
        load_cell_group(2)
        load_act(6)
        load_act(7)

        pairs_sort(0, on_scalar)
        pairs_sort(1, on_scalar)
        for g in range(GENE_PASSES):
            for m in range(4):
                first(m, 0, g, g + 1)
        gate(0, 0)
        gate(1, 0)
        for m in range(4):
            first(m, 1)
            gate(m, 1)
            if m == 3:
                gate(3, 0)
            if m == 0:
                gate(2, 0)

        pairs_turn(0, 0)
        pairs_empty(0, 0, on_scalar)
        pairs_turn(0, 1)
        pairs_empty(0, 1, on_scalar)
        h_turn(0)
        h_empty(0)
        h_turn(1)
        pairs_turn(1, 0)
        pairs_empty(1, 0, on_scalar)
        h_empty(1)
        pairs_turn(1, 1)
        pairs_empty(1, 1, on_vector)
        h_quantize(0)
        pairs_quantize(0)
        for m in (2, 3):
            h_turn(m)
            h_empty(m)
        h_quantize(2)
        h_quantize(1)
        for j in (2, 3, 4):
            pairs_sort(j, on_scalar)
        pairs_sort(5, on_gpsimd)

        first(4, 0)
        h_quantize(3)
        first(4, 1)
        gate(4, 1)
        gate(4, 0)

        def turn_load(j, copies=(on_scalar, on_scalar)):
            for g in range(FEATURE_PASSES):
                pairs_turn(j, g)
            for g in reversed(range(FEATURE_PASSES)):
                pairs_empty(j, g, copies[g])

        def turn_cells(m):
            h_turn(m)
            h_empty(m)

        def in_twos(units):
            return list(zip(units[0::2], units[1::2]))

        twos = in_twos([unit(m, 0) for m in range(4)])
        multiply(*twos[0])
        first(5, 0)
        gate(5, 0)
        first(5, 1)
        gate(5, 1)
        finish(*twos[0])
        second(*twos[1])
        for g in range(FEATURE_PASSES):
            pairs_turn(2, g)
            pairs_empty(2, g, on_scalar)
        add_bias(*twos[1])
        pairs_sort(6, on_gpsimd)
        turn_load(3, (on_scalar, on_vector))
        pairs_sort(7, on_gpsimd)
        pairs_quantize(1)
        turn_cells(4)
        turn_cells(5)
        h_quantize(4)
        h_quantize(5)
        turn_load(4)
        turn_load(5, (on_scalar, on_vector))
        pairs_quantize(2)
        turn_load(6)
        turn_load(7)
        finish(*twos[1])
        units = [unit(m, 1) for m in range(4)] + [unit(m, q) for m in (4, 5) for q in (0, 1)] + [unit(m, 2) for m in range(6)] + [unit(m, 3) for m in range(6)]
        twos = in_twos(units)
        multiply(*twos[0])
        multiply(*twos[1])
        pairs_quantize(3)
        reserve(*twos[2])
        reserve(*twos[3])
        multiply(*twos[2], *twos[3])
        finish(*twos[0])
        finish(*twos[1])
        multiply(*twos[4])
        finish(*twos[2])
        finish(*twos[3])
        for two, f in zip(twos[5:7], range(FEATURE_PASSES)):
            second(*two)
            first(6, f)
            gate(6, f)
            add_bias(*two)
        for two in twos[4:6]:
            finish(*two)
        multiply(*twos[7])
        finish(*twos[6])
        multiply(*twos[8])
        turn_cells(6)
        h_quantize(6)
        finish(*twos[7])
        finish(*twos[8])
        for f in range(FEATURE_PASSES):
            first(7, f)
            gate(7, f)
        twos[6] = twos[9]
        ahead = list(twos[6]) + [unit(6, 0)]
        for one in ahead:
            multiply(one)
        finish(ahead[0])
        h_turn(7)
        h_empty(7)
        multiply(unit(6, 1))
        h_quantize(7)
        for one in ahead[1:] + [unit(6, 1)]:
            finish(one)
        for one in [unit(6, 2), unit(6, 3)] + [unit(7, q) for q in range(3)] + [unit(7, 3, 0, BANK // 2), unit(7, 3, BANK // 2, BANK)]:
            multiply(one)
            finish(one)
